import numpy as np
import ml_dtypes


def mxq(x, axis, fmt="e4m3"):
    dtype, down = {"e4m3": (ml_dtypes.float8_e4m3fn, 7), "e5m2": (ml_dtypes.float8_e5m2, 14)}[fmt]
    v = np.moveaxis(np.asarray(x, np.float32).astype(ml_dtypes.bfloat16).astype(np.float64), axis, -1)
    blocks = v.reshape(v.shape[:-1] + (-1, 32))
    amax = np.abs(blocks).max(-1, keepdims=True)
    byte = np.maximum(np.where(amax > 0, np.frexp(amax)[1] - 1 + 127, 0) - down, 1)
    scale = np.exp2(byte - 127.0)
    codes = (blocks / scale).astype(np.float32).astype(dtype).astype(np.float64)
    return np.moveaxis((codes * scale).reshape(v.shape), -1, axis)


WIDE = False


def mx_kscale(k):
    if not WIDE:
        return np.ones(k)
    levels = np.array([10, -10, 5, -5, 0])
    if k % 512:
        return np.exp2(np.random.permutation(np.resize(levels, k // 32))).repeat(32)
    a = np.empty((k // 512, 16))
    for p in range(k // 512):
        a[p, :8] = np.random.permutation(np.resize(levels, 8))
        for g in range(8):
            far = levels[np.abs(levels - a[p, g]) >= 10]
            a[p, g + 8] = far[np.random.randint(len(far))]
    return np.exp2(a.ravel()).repeat(32)


def f64(x):
    return np.asarray(x).astype(np.float64)


def striped(idx):
    return np.tile(idx.reshape(-1, 16).T, (8, 1)).astype(np.uint16)


def unstriped(offs):
    return offs[:16].T.reshape(-1).astype(np.int64)


E2M1 = np.array([0.0, 0.5, 1.0, 1.5, 2.0, 3.0, 4.0, 6.0, -0.0, -0.5, -1.0, -1.5, -2.0, -3.0, -4.0, -6.0])


def pack_weight(w, fmt):
    k, n = w.shape
    w = f64(np.asarray(w, np.float32).astype(ml_dtypes.bfloat16)).reshape(k // 32, 32, n)
    amax = np.abs(w).max(1)
    if fmt == "e4m3":
        byte = np.frexp(amax)[1] - 1 + 127 - 7
    else:
        mant, ex = np.frexp(amax / 6.0)
        byte = np.where(mant > 0.5, ex, ex - 1) + 127
    byte = np.clip(np.where(amax > 0, byte, 1), 1, 254)
    scaled = (w * np.exp2(127.0 - byte)[:, None, :]).reshape(k, n).astype(np.float32)
    by_word = np.ascontiguousarray(scaled.reshape(k // 512, 128, 4, n).transpose(0, 1, 3, 2))
    if fmt == "e4m3":
        words = by_word.astype(ml_dtypes.float8_e4m3fn).view(np.uint8)
    else:
        c = by_word.astype(ml_dtypes.float4_e2m1fn).view(np.uint8) & 0xF
        words = (c[..., 0::2] | (c[..., 1::2] << 4)).reshape(k // 512, 128, 2 * n)
    return np.ascontiguousarray(words), np.ascontiguousarray(byte.astype(np.uint8).reshape(k // 512, 16, n))


def unpack_weight(words, scales, fmt):
    g, _, n = scales.shape
    words = np.ascontiguousarray(words).reshape(g, 128, n, -1)
    if fmt == "e4m3":
        vals = words.view(ml_dtypes.float8_e4m3fn).astype(np.float64)
    else:
        nib = np.empty((g, 128, n, 4), np.uint8)
        nib[..., 0::2] = words & 0xF
        nib[..., 1::2] = words >> 4
        vals = E2M1[nib]
    vals = vals * np.repeat(np.exp2(scales.astype(np.float64) - 127.0), 8, axis=1)[..., None]
    return vals.transpose(0, 1, 3, 2).reshape(g * 512, n)


def gelu(v):
    return 0.5 * v * (1.0 + np.tanh(np.sqrt(2.0 / np.pi) * (v + 0.044715 * v**3)))


def bf(x):
    return np.asarray(x, np.float32).astype(ml_dtypes.bfloat16)


def planes(Y):
    n, m = Y.shape
    b = f64(bf(Y)).reshape(n // 32, 32, m)
    amax = np.abs(b).max(1)
    byte = np.clip(np.where(amax > 0, np.frexp(amax)[1] - 1 + 127 - 7, 1), 1, 254)
    codes = (b * np.exp2(127.0 - byte)[:, None, :]).reshape(n, m).astype(np.float32).astype(ml_dtypes.float8_e4m3fn).view(np.uint8)
    words = codes.reshape(n // 512, 128, 4, m).transpose(0, 1, 3, 2)
    return np.ascontiguousarray(words), np.ascontiguousarray(byte.astype(np.uint8).reshape(n // 512, 16, m))


K, T, S, H, N = 1024, 2048, 1024, 1024, 512

def setup_inputs():
    n = np.random.standard_normal
    s = mx_kscale(K)[:, None]
    s2 = mx_kscale(N)[:, None]
    u = mx_kscale(H)[:, None]
    d = {}
    d["tab_words"], d["tab_scales"] = pack_weight(n((K, T)) * s, "e4m3")
    d["offs"] = striped(np.random.permutation(T)[:S])
    d["gT"] = np.exp(0.8 * n((N, 1)) + 0.4 * n((N, T))).astype(np.float32)
    d["lv"] = (np.exp(0.2 * n(N)) * s2[:, 0]).astype(np.float32)
    d["w1_words"], d["w1_scales"] = pack_weight(n((K, H)) / np.sqrt(K) / s * u.T, "e2m1")
    d["w2"] = (n((N, H)) / np.sqrt(N) / s2 * u.T).astype(np.float32)
    d["b"] = (0.5 * n(H) * u[:, 0]).astype(np.float32)
    d["w3_words"], d["w3_scales"] = pack_weight(0.35 * n((H, N)) / np.sqrt(H) / u, "e4m3")
    return d

def reference(tab_words, tab_scales, offs, gT, lv, w1_words, w1_scales, w2, b, w3_words, w3_scales):
    v = unpack_weight(tab_words, tab_scales, "e4m3")[:, unstriped(offs)]
    w1 = unpack_weight(w1_words, w1_scales, "e2m1")
    w3 = unpack_weight(w3_words, w3_scales, "e4m3")
    g = f64(gT)[:, unstriped(offs)]
    lg = np.log(g) * f64(lv)[:, None]
    a = w1.T @ v + mxq(f64(w2), 0, "e4m3").T @ mxq(lg, 0, "e4m3")
    h = np.maximum(a - f64(b)[:, None], 0.0)
    e = w3.T @ mxq(h, 0, "e4m3")
    new = g * np.exp(e)
    y = f64(gT).copy()
    y[:, unstriped(offs)] = new
    words, scales = planes(y)
    return y, words, scales

@@ -1,0 +1,308 @@
+from contextlib import ExitStack
+
+import concourse.mybir as mybir
+
+K, T, S, H, N = 1024, 2048, 1024, 1024, 512
+FLOPS = 2 * S * (K * H + N * H + H * N)
+
+F32 = mybir.dt.float32
+BF16 = mybir.dt.bfloat16
+I32 = mybir.dt.int32
+U32 = mybir.dt.uint32
+U16 = mybir.dt.uint16
+U8 = mybir.dt.uint8
+FP8X4 = mybir.dt.float8_e4m3fn_x4
+FP4X4 = mybir.dt.float4_e2m1fn_x4
+ACT = mybir.ActivationFunctionType
+ALU = mybir.AluOpType
+
+P = 128
+PACK = 4
+GROUP = P * PACK
+HALF = 512
+HALVES = S // HALF
+LIST_COLS = HALF // 16
+K_PASSES = K // GROUP
+H_GROUPS = H // GROUP
+CHUNK = 256
+CHUNKS = S // CHUNK
+SUM_BANKS = 4
+Y_SPLIT = 1152
+Y_CHUNK = 512
+Y_CHUNKS = T // Y_CHUNK
+
+
+def weave(copy, woven, rows):
+    copy(
+        woven.rearrange("p (c i t) -> p c t i", i=4, t=PACK),
+        rows.rearrange("p t (c i) -> p c t i", i=4),
+    )
+
+
+def tile_list_gain_drift_rewrite_kernel(
+    tc, tab_words, tab_scales, offs, gT, lv, w1_words, w1_scales, w2, b, w3_words, w3_scales, out_0, out_1, out_2
+):
+    nc = tc.nc
+    with ExitStack() as ctx:
+        keep = ctx.enter_context(tc.tile_pool(name="keep", bufs=1))
+        ring = ctx.enter_context(tc.tile_pool(name="ring", bufs=4))
+        psum = ctx.enter_context(tc.psum_pool(name="psum", bufs=1))
+
+        def held(shape, dtype, name):
+            return keep.tile(shape, dtype, name=name, align_bytes=64)
+
+        def bank(index):
+            return psum.tile([P, HALF], F32, name="bank%d" % index)
+
+        tab_sc = held([P, T], U8, "tab_sc")
+        w_sc_raw = held([P, H], U8, "w_sc_raw")
+        v_sc_down = held([P, S], U8, "v_sc_down")
+        w_sc_down = held([P, H], U8, "w_sc_down")
+        nc.gpsimd.memset(tab_sc[:].bitcast(I32), 0)
+        for plane in (w_sc_raw, w_sc_down, v_sc_down):
+            nc.vector.memset(plane[:].bitcast(I32), 0)
+
+        offsets = keep.tile([P, S // 16], U16, name="offsets")
+        nc.sync.dma_start(offsets[:], offs)
+        lv_sb = held([P, PACK], F32, "lv_sb")
+        nc.sync.dma_start(lv_sb[:], lv.rearrange("(p t) -> p t", t=PACK))
+        b_sb = held([P, H_GROUPS, PACK], F32, "b_sb")
+        nc.sync.dma_start(b_sb[:], b.rearrange("(g p t) -> p g t", p=P, t=PACK))
+        pages = [held([P, T], F32, "page%d" % t) for t in range(PACK)]
+        gT_dealt = gT.rearrange("(p t) c -> t p c", t=PACK)
+        w2_raw = [held([P, PACK, GROUP], F32, "w2_raw%d" % g) for g in range(H_GROUPS)]
+        w2_dealt = w2.rearrange("(p j) c -> p j c", j=PACK)
+        w1_raw = held([P, K_PASSES, 2 * H], U8, "w1_raw")
+        tab = [held([P, T], I32, "tab%d" % a) for a in range(K_PASSES)]
+        for q in range(4):
+            nc.sync.dma_start(
+                tab_sc[32 * q : 32 * q + 8, :].bitcast(I32), tab_scales[:, 4 * q : 4 * q + 4, :].bitcast(I32)
+            )
+        nc.sync.dma_start(pages[0][:], gT_dealt[0])
+        nc.sync.dma_start(pages[1][:], gT_dealt[1])
+        nc.sync.dma_start(pages[2][:], gT_dealt[2])
+        nc.sync.dma_start(pages[3][:], gT_dealt[3])
+        for q in range(4):
+            nc.sync.dma_start(
+                w_sc_raw[32 * q + 8 : 32 * q + 12, :].rearrange("p (a c) -> p a c", a=H_GROUPS).bitcast(I32),
+                w3_scales[:, 4 * q : 4 * q + 4, :].rearrange("a r c -> r a c").bitcast(I32),
+            )
+        nc.sync.dma_start(w2_raw[0][:], w2_dealt[:, :, 0:GROUP])
+        nc.sync.dma_start(w1_raw[:].bitcast(I32), w1_words.rearrange("a p c -> p a c").bitcast(I32))
+        nc.sync.dma_start(w2_raw[1][:], w2_dealt[:, :, GROUP:H])
+        nc.sync.dma_start(tab[0][:], tab_words[0].rearrange("p c i -> p (c i)").bitcast(I32))
+        nc.sync.dma_start(tab[1][:], tab_words[1].rearrange("p c i -> p (c i)").bitcast(I32))
+        w3_raw = held([P, H_GROUPS, N], I32, "w3_raw")
+        nc.sync.dma_start(w3_raw[:], w3_words.rearrange("a p c i -> p a (c i)").bitcast(I32))
+
+        for q in range(4):
+            nc.gpsimd.dma_start(
+                w_sc_raw[32 * q : 32 * q + 8, :].bitcast(I32), w1_scales[:, 4 * q : 4 * q + 4, :].bitcast(I32)
+            )
+        neg_b = held([P, H_GROUPS, PACK], F32, "neg_b")
+        nc.gpsimd.tensor_scalar(neg_b[:], b_sb[:], -1.0, 0.0, ALU.mult, ALU.add)
+
+        def picks(first, count):
+            return offsets[:, first // 16 : (first + count) // 16]
+
+        v_sc = held([P, S], U8, "v_sc")
+        nc.vector.tensor_copy(v_sc[:], tab_sc[:].indirect(offsets[:]))
+        nc.gpsimd.dma_start(v_sc_down[0 : P - 4, :].bitcast(I32), v_sc[4:P, :].bitcast(I32))
+        v_planes = [v_sc, v_sc_down]
+
+        gains = [held([P, S], F32, "gains%d" % t) for t in range(PACK)]
+        lg_rows = held([P, PACK, HALF], BF16, "lg_rows")
+        late_logs = [held([P, HALF], F32, "late_logs%d" % t) for t in range(PACK)]
+        for t in range(PACK):
+            for half in range(HALVES):
+                picked = gains[t][:, half * HALF : (half + 1) * HALF]
+                nc.vector.tensor_copy(picked, pages[t][:].indirect(picks(half * HALF, HALF)))
+            logs = ring.tile([P, HALF], F32, name="logs")
+            nc.scalar.activation(logs[:], gains[t][:, 0:HALF], ACT.Ln)
+            nc.scalar.activation(lg_rows[:, t, :], logs[:], ACT.Copy, scale=lv_sb[:, t : t + 1])
+            nc.scalar.activation(late_logs[t][:], gains[t][:, HALF:S], ACT.Ln)
+
+        def quantize(woven, name):
+            codes = held([P, woven.shape[1] // PACK], U32, name + "_codes")
+            scales = held([P, woven.shape[1] // PACK], U8, name + "_scales")
+            nc.vector.quantize_mx(codes[:].bitcast(FP8X4), scales[:], woven[:])
+            return codes, scales
+
+        def quantize_w2(g):
+            woven = held([P, PACK * GROUP], BF16, "w2_woven%d" % g)
+            copy = nc.vector.tensor_copy if g == 0 else nc.scalar.copy
+            copy(
+                woven[:].rearrange("p (t m j) -> p m t j", t=PACK, j=PACK),
+                w2_raw[g][:].rearrange("p j (m t) -> p m t j", t=PACK),
+            )
+            return woven, quantize(woven, "w2_%d" % g)
+
+        def quantize_lg(rows, lo, hi, woven_name, name, copy=nc.vector.tensor_copy):
+            woven = held([P, PACK * (hi - lo)], BF16, woven_name)
+            weave(copy, woven[:], rows[:, :, lo:hi])
+            return quantize(woven, name)
+
+        w_sc = held([P, H], U8, "w_sc")
+        nc.vector.tensor_copy(
+            w_sc[:].rearrange("p (g t m) -> p g t m", t=PACK, m=P),
+            w_sc_raw[:].rearrange("p (g m t) -> p g t m", t=PACK, m=P),
+        )
+        nc.gpsimd.dma_start(w_sc_down[0 : P - 4, :].bitcast(I32), w_sc[4:P, :].bitcast(I32))
+        w1_planes = [w_sc, w_sc_down]
+
+        early_mx = quantize_lg(lg_rows, 0, HALF, "lg_woven", "lg0")
+        lg_mx = [early_mx + (0,), early_mx + (CHUNK,)]
+        w2_woven, w2_mx = zip(*[quantize_w2(g) for g in range(H_GROUPS)])
+        exp_warm = held([P, 1], F32, "exp_warm")
+        nc.scalar.activation(exp_warm[:], w2_woven[1][:, 0:1], ACT.Exp, scale=0.0)
+
+        w1_sb = held([P, K_PASSES * 2 * H], U8, "w1_sb")
+        nc.vector.tensor_copy(
+            w1_sb[:].bitcast(U16).rearrange("p (g t m) -> p g t m", t=PACK, m=P),
+            w1_raw[:].rearrange("p a c -> p (a c)").bitcast(U16).rearrange("p (g m t) -> p g t m", t=PACK, m=P),
+        )
+
+        v_words = []
+
+        def first_product(c):
+            first = c * CHUNK
+            within = first % HALF
+            if within == 0:
+                names = ("v0", "v1") if c == 0 else ("w3_raw", "tab0")
+                v_words[:] = [held([P, HALF], U32, name) for name in names]
+            count = CHUNK if first < HALF else HALF
+            if first % count == 0:
+                for a in range(K_PASSES):
+                    window = tab[a][:].bitcast(U32).indirect(picks(first, count))
+                    nc.vector.tensor_copy(v_words[a][:, within : within + count], window)
+            lg_codes, lg_scales, lg_first = lg_mx[c]
+            lg_cols = slice(lg_first, lg_first + CHUNK)
+            sums = [bank((PACK * c + t) % SUM_BANKS) for t in range(PACK)]
+            for step in range(2):
+                for t in range(PACK):
+                    w_cols = slice(t * P, (t + 1) * P)
+                    nc.tensor.matmul_mx(
+                        sums[t][:, step * CHUNK : (step + 1) * CHUNK],
+                        lhsT=w2_mx[step][0][:, w_cols].bitcast(FP8X4),
+                        lhsT_scale=w2_mx[step][1][:, w_cols],
+                        rhs=lg_codes[:, lg_cols].bitcast(FP8X4),
+                        rhs_scale=lg_scales[:, lg_cols],
+                        start=(step == 0),
+                        stop=False,
+                    )
+                for t in range(PACK):
+                    for g in range(H_GROUPS):
+                        c0 = g * GROUP + t * P
+                        for n0 in range(0, CHUNK, P):
+                            nc.tensor.matmul_mx(
+                                sums[t][:, g * CHUNK + n0 : g * CHUNK + n0 + P],
+                                lhsT=w1_sb[:, 2 * (step * H + c0) : 2 * (step * H + c0 + P)].bitcast(FP4X4),
+                                lhsT_scale=w1_planes[step][:, c0 : c0 + P],
+                                rhs=v_words[step][:, within + n0 : within + n0 + P].bitcast(FP8X4),
+                                rhs_scale=v_planes[step][:, first + n0 : first + n0 + P],
+                                start=False,
+                                stop=(step == 1 and g == H_GROUPS - 1 and n0 == CHUNK - P),
+                            )
+            return sums
+
+        def hidden(c, copy):
+            sums = first_product(c)
+            rows = held([P, PACK, H_GROUPS * CHUNK], BF16, "h_rows%d" % c)
+            for t in range(PACK):
+                for g in range(H_GROUPS):
+                    span = slice(g * CHUNK, (g + 1) * CHUNK)
+                    nc.scalar.activation(rows[:, t, span], sums[t][:, span], ACT.Relu, bias=neg_b[:, g, t : t + 1])
+            woven = held([P, PACK * HALF], BF16, "h_woven%d" % (c % 2))
+            weave(copy, woven[:], rows[:])
+            return quantize(woven, "h%d" % (c % 2))
+
+        def drift(t, h_mx):
+            acc = bank(SUM_BANKS + t)[:, 0:CHUNK]
+            for a in range(H_GROUPS):
+                c0 = a * N + t * P
+                nc.tensor.matmul_mx(
+                    acc,
+                    lhsT=w3_sb[:, c0 : c0 + P].bitcast(FP8X4),
+                    lhsT_scale=w_sc[8:P, c0 : c0 + P],
+                    rhs=h_mx[0][:, a * CHUNK : (a + 1) * CHUNK].bitcast(FP8X4),
+                    rhs_scale=h_mx[1][:, a * CHUNK : (a + 1) * CHUNK],
+                    start=(a == 0),
+                    stop=(a == H_GROUPS - 1),
+                )
+            return acc
+
+        def exp_into(factors, sums):
+            for u in range(2):
+                nc.scalar.activation(factors[:, u, :], sums[u], ACT.Exp)
+
+        def rewrite(t, first, count, factor):
+            nc.vector.tensor_tensor(
+                pages[t][:].indirect(picks(first, count)), gains[t][:, first : first + count], factor, ALU.mult
+            )
+
+        h_mx = hidden(0, nc.vector.tensor_copy)
+        late_rows = held([P, PACK, HALF], BF16, "w2_raw1")
+        for t in range(PACK):
+            nc.scalar.activation(late_rows[:, t, :], late_logs[t][:], ACT.Copy, scale=lv_sb[:, t : t + 1])
+        late_mx = quantize_lg(late_rows, 0, HALF, "lg_woven", "lg2", nc.scalar.copy)
+        lg_mx.extend([late_mx + (0,), late_mx + (CHUNK,)])
+        w3_sb = held([P, H_GROUPS * N], I32, "w3_sb")
+        nc.vector.tensor_copy(
+            w3_sb[:].rearrange("p (a t m) -> p a m t", t=PACK, m=P),
+            w3_raw[:].rearrange("p a (m t) -> p a m t", t=PACK),
+        )
+        out_dealt = out_0.rearrange("(p t) c -> t p c", t=PACK)
+        last = PACK - 1
+
+        def finish(t):
+            nc.sync.dma_start(out_dealt[t], pages[t][:])
+            if t < last:
+                nc.scalar.copy(y_rows[:, t, :], pages[t][:])
+
+        for c in range(CHUNKS - 1):
+            first = c * CHUNK
+            sums = [drift(t, h_mx) for t in range(PACK)]
+            early = keep.tile([P, 2, CHUNK], F32, name="early", bufs=2)
+            exp_into(early[:], sums[0:2])
+            for t in range(2):
+                rewrite(t, first, CHUNK, early[:, t, :])
+            h_mx = hidden(c + 1, nc.scalar.copy)
+            late = held([P, 2, 2 * CHUNK], F32, "h_rows%d" % (c + 1))
+            exp_into(late[:, :, 0:CHUNK], sums[2:4])
+            rewrite(2, first, CHUNK, late[:, 0, 0:CHUNK])
+            if c < CHUNKS - 2:
+                rewrite(last, first, CHUNK, late[:, 1, 0:CHUNK])
+
+        first = S - CHUNK
+        sums = [drift(t, h_mx) for t in range(PACK)]
+        y_rows = held([P, PACK, T], BF16, "h1_codes")
+        early = keep.tile([P, 2, CHUNK], F32, name="early", bufs=2)
+        exp_into(early[:], sums[0:2])
+        exp_into(late[:, :, CHUNK : 2 * CHUNK], sums[2:4])
+        for t in range(2):
+            rewrite(t, first, CHUNK, early[:, t, :])
+            finish(t)
+        rewrite(2, first, CHUNK, late[:, 0, CHUNK : 2 * CHUNK])
+        finish(2)
+        rewrite(last, first - CHUNK, 2 * CHUNK, late[:, 1, :])
+        finish(last)
+        y_woven = held([P, PACK * T], BF16, "y_woven")
+        y_scales = held([P, T], U8, "y_scales")
+        words_out = out_1[0].rearrange("p m t -> p (m t)").bitcast(I32)
+        nc.vector.tensor_copy(y_rows[:, last, 0:Y_SPLIT], pages[last][:, 0:Y_SPLIT])
+        nc.scalar.copy(y_rows[:, last, Y_SPLIT:T], pages[last][:, Y_SPLIT:T])
+        for copy, lo, hi in (
+            (nc.vector.tensor_copy, 0, Y_CHUNK),
+            (nc.vector.tensor_copy, Y_CHUNK, Y_SPLIT),
+            (nc.scalar.copy, Y_SPLIT, T - Y_CHUNK),
+            (nc.scalar.copy, T - Y_CHUNK, T),
+        ):
+            weave(copy, y_woven[:, PACK * lo : PACK * hi], y_rows[:, :, lo:hi])
+        for lo in range(0, T, Y_CHUNK):
+            hi = lo + Y_CHUNK
+            y_codes = held([P, hi - lo], I32, "y_codes%d" % lo)
+            nc.vector.quantize_mx(y_codes[:].bitcast(FP8X4), y_scales[:, lo:hi], y_woven[:, PACK * lo : PACK * hi])
+            nc.sync.dma_start(words_out[:, lo:hi], y_codes[:])
+        for q in range(4):
+            queue = nc.sync if q % 2 == 0 else nc.scalar
+            queue.dma_start(out_2[0, 4 * q : 4 * q + 4, :].bitcast(I32), y_scales[32 * q : 32 * q + 4, :].bitcast(I32))

@@ -28,6 +28,7 @@ CHUNK = 256
 CHUNKS = S // CHUNK
 SUM_BANKS = 4
 Y_SPLIT = 1152
+MOVED = 112
 Y_CHUNK = 512
 Y_CHUNKS = T // Y_CHUNK
 
@@ -56,29 +57,25 @@ def tile_list_gain_drift_rewrite_kernel(
 
         tab_sc = held([P, T], U8, "tab_sc")
         w_sc_raw = held([P, H], U8, "w_sc_raw")
-        v_sc_down = held([P, S], U8, "v_sc_down")
         w_sc_down = held([P, H], U8, "w_sc_down")
-        nc.gpsimd.memset(tab_sc[:].bitcast(I32), 0)
-        for plane in (w_sc_raw, w_sc_down, v_sc_down):
-            nc.vector.memset(plane[:].bitcast(I32), 0)
+        v_planes = [held([P, S], U8, "v_plane%d" % a) for a in range(K_PASSES)]
+        for plane in [tab_sc[32:64, :], tab_sc[64:P, :], w_sc_raw[:], w_sc_down[:]] + [plane[:] for plane in v_planes]:
+            nc.vector.memset(plane.bitcast(I32), 0)
+        nc.sync.dma_start(tab_sc[0:32, :].bitcast(I32), tab_scales.rearrange("a q c -> (a q) c").bitcast(I32))
 
         offsets = keep.tile([P, S // 16], U16, name="offsets")
         nc.sync.dma_start(offsets[:], offs)
+        pages = [held([P, T], F32, "page%d" % t) for t in range(PACK)]
+        gT_dealt = gT.rearrange("(p t) c -> t p c", t=PACK)
+        nc.sync.dma_start(pages[0][:], gT_dealt[0])
         lv_sb = held([P, PACK], F32, "lv_sb")
         nc.sync.dma_start(lv_sb[:], lv.rearrange("(p t) -> p t", t=PACK))
         b_sb = held([P, H_GROUPS, PACK], F32, "b_sb")
         nc.sync.dma_start(b_sb[:], b.rearrange("(g p t) -> p g t", p=P, t=PACK))
-        pages = [held([P, T], F32, "page%d" % t) for t in range(PACK)]
-        gT_dealt = gT.rearrange("(p t) c -> t p c", t=PACK)
         w2_raw = [held([P, PACK, GROUP], F32, "w2_raw%d" % g) for g in range(H_GROUPS)]
         w2_dealt = w2.rearrange("(p j) c -> p j c", j=PACK)
         w1_raw = held([P, K_PASSES, 2 * H], U8, "w1_raw")
         tab = [held([P, T], I32, "tab%d" % a) for a in range(K_PASSES)]
-        for q in range(4):
-            nc.sync.dma_start(
-                tab_sc[32 * q : 32 * q + 8, :].bitcast(I32), tab_scales[:, 4 * q : 4 * q + 4, :].bitcast(I32)
-            )
-        nc.sync.dma_start(pages[0][:], gT_dealt[0])
         nc.sync.dma_start(pages[1][:], gT_dealt[1])
         nc.sync.dma_start(pages[2][:], gT_dealt[2])
         nc.sync.dma_start(pages[3][:], gT_dealt[3])
@@ -107,8 +104,10 @@ def tile_list_gain_drift_rewrite_kernel(
 
         v_sc = held([P, S], U8, "v_sc")
         nc.vector.tensor_copy(v_sc[:], tab_sc[:].indirect(offsets[:]))
-        nc.gpsimd.dma_start(v_sc_down[0 : P - 4, :].bitcast(I32), v_sc[4:P, :].bitcast(I32))
-        v_planes = [v_sc, v_sc_down]
+        for a in range(K_PASSES):
+            for q in range(4):
+                row = 16 * a + 4 * q
+                nc.gpsimd.dma_start(v_planes[a][32 * q : 32 * q + 4, :].bitcast(I32), v_sc[row : row + 4, :].bitcast(I32))
 
         gains = [held([P, S], F32, "gains%d" % t) for t in range(PACK)]
         lg_rows = held([P, PACK, HALF], BF16, "lg_rows")
@@ -147,7 +146,7 @@ def tile_list_gain_drift_rewrite_kernel(
             w_sc[:].rearrange("p (g t m) -> p g t m", t=PACK, m=P),
             w_sc_raw[:].rearrange("p (g m t) -> p g t m", t=PACK, m=P),
         )
-        nc.gpsimd.dma_start(w_sc_down[0 : P - 4, :].bitcast(I32), w_sc[4:P, :].bitcast(I32))
+        nc.scalar.dma_start(w_sc_down[0:MOVED, :].bitcast(I32), w_sc[4 : 4 + MOVED, :].bitcast(I32))
         w1_planes = [w_sc, w_sc_down]
 
         early_mx = quantize_lg(lg_rows, 0, HALF, "lg_woven", "lg0")
@@ -177,12 +176,15 @@ def tile_list_gain_drift_rewrite_kernel(
                     nc.vector.tensor_copy(v_words[a][:, within : within + count], window)
             lg_codes, lg_scales, lg_first = lg_mx[c]
             lg_cols = slice(lg_first, lg_first + CHUNK)
-            sums = [bank((PACK * c + t) % SUM_BANKS) for t in range(PACK)]
+            banks = [bank(t) for t in range(PACK)]
+            sums = [[banks[t][:, g * CHUNK : (g + 1) * CHUNK] for g in range(H_GROUPS)] for t in range(PACK)]
+            sums[PACK - 1][H_GROUPS - 1] = bank(PACK + c % 2)[:, 0:CHUNK]
+            alone = [(PACK - 1, g) for g in range(H_GROUPS)]
             for step in range(2):
                 for t in range(PACK):
                     w_cols = slice(t * P, (t + 1) * P)
                     nc.tensor.matmul_mx(
-                        sums[t][:, step * CHUNK : (step + 1) * CHUNK],
+                        sums[t][step],
                         lhsT=w2_mx[step][0][:, w_cols].bitcast(FP8X4),
                         lhsT_scale=w2_mx[step][1][:, w_cols],
                         rhs=lg_codes[:, lg_cols].bitcast(FP8X4),
@@ -195,13 +197,13 @@ def tile_list_gain_drift_rewrite_kernel(
                         c0 = g * GROUP + t * P
                         for n0 in range(0, CHUNK, P):
                             nc.tensor.matmul_mx(
-                                sums[t][:, g * CHUNK + n0 : g * CHUNK + n0 + P],
+                                sums[t][g][:, n0 : n0 + P],
                                 lhsT=w1_sb[:, 2 * (step * H + c0) : 2 * (step * H + c0 + P)].bitcast(FP4X4),
                                 lhsT_scale=w1_planes[step][:, c0 : c0 + P],
                                 rhs=v_words[step][:, within + n0 : within + n0 + P].bitcast(FP8X4),
                                 rhs_scale=v_planes[step][:, first + n0 : first + n0 + P],
-                                start=False,
-                                stop=(step == 1 and g == H_GROUPS - 1 and n0 == CHUNK - P),
+                                start=(step == 0 and n0 == 0 and (t, g) == alone[1]),
+                                stop=(step == 1 and n0 == CHUNK - P and (g == H_GROUPS - 1 or (t, g) in alone)),
                             )
             return sums
 
@@ -211,13 +213,16 @@ def tile_list_gain_drift_rewrite_kernel(
             for t in range(PACK):
                 for g in range(H_GROUPS):
                     span = slice(g * CHUNK, (g + 1) * CHUNK)
-                    nc.scalar.activation(rows[:, t, span], sums[t][:, span], ACT.Relu, bias=neg_b[:, g, t : t + 1])
+                    nc.scalar.activation(rows[:, t, span], sums[t][g], ACT.Relu, bias=neg_b[:, g, t : t + 1])
             woven = held([P, PACK * HALF], BF16, "h_woven%d" % (c % 2))
             weave(copy, woven[:], rows[:])
             return quantize(woven, "h%d" % (c % 2))
 
-        def drift(t, h_mx):
-            acc = bank(SUM_BANKS + t)[:, 0:CHUNK]
+        def drift_banks(c):
+            pair = bank(7)
+            return [bank(PACK + (c + 1) % 2)[:, 0:CHUNK], bank(6)[:, 0:CHUNK], pair[:, 0:CHUNK], pair[:, CHUNK:HALF]]
+
+        def drift(t, h_mx, acc):
             for a in range(H_GROUPS):
                 c0 = a * N + t * P
                 nc.tensor.matmul_mx(
@@ -261,7 +266,7 @@ def tile_list_gain_drift_rewrite_kernel(
 
         for c in range(CHUNKS - 1):
             first = c * CHUNK
-            sums = [drift(t, h_mx) for t in range(PACK)]
+            sums = [drift(t, h_mx, acc) for t, acc in enumerate(drift_banks(c))]
             early = keep.tile([P, 2, CHUNK], F32, name="early", bufs=2)
             exp_into(early[:], sums[0:2])
             for t in range(2):
@@ -274,7 +279,7 @@ def tile_list_gain_drift_rewrite_kernel(
                 rewrite(last, first, CHUNK, late[:, 1, 0:CHUNK])
 
         first = S - CHUNK
-        sums = [drift(t, h_mx) for t in range(PACK)]
+        sums = [drift(t, h_mx, acc) for t, acc in enumerate(drift_banks(CHUNKS - 1))]
         y_rows = held([P, PACK, T], BF16, "h1_codes")
         early = keep.tile([P, 2, CHUNK], F32, name="early", bufs=2)
         exp_into(early[:], sums[0:2])

@@ -19,18 +19,15 @@ ALU = mybir.AluOpType
 P = 128
 PACK = 4
 GROUP = P * PACK
-HALF = 512
-HALVES = S // HALF
-LIST_COLS = HALF // 16
 K_PASSES = K // GROUP
 H_GROUPS = H // GROUP
 CHUNK = 256
 CHUNKS = S // CHUNK
-SUM_BANKS = 4
+SUM_BANKS = 6
+DRIFT_BANKS = 2
 Y_SPLIT = 1152
-MOVED = 112
 Y_CHUNK = 512
-Y_CHUNKS = T // Y_CHUNK
+W3_ROW = 4
 
 
 def weave(copy, woven, rows):
@@ -46,218 +43,245 @@ def tile_list_gain_drift_rewrite_kernel(
     nc = tc.nc
     with ExitStack() as ctx:
         keep = ctx.enter_context(tc.tile_pool(name="keep", bufs=1))
-        ring = ctx.enter_context(tc.tile_pool(name="ring", bufs=4))
         psum = ctx.enter_context(tc.psum_pool(name="psum", bufs=1))
 
-        def held(shape, dtype, name):
-            return keep.tile(shape, dtype, name=name, align_bytes=64)
-
-        def bank(index):
-            return psum.tile([P, HALF], F32, name="bank%d" % index)
+        def held(shape, dtype, name, bufs=1):
+            return keep.tile(shape, dtype, name=name, align_bytes=64, bufs=bufs)
 
         tab_sc = held([P, T], U8, "tab_sc")
-        w_sc_raw = held([P, H], U8, "w_sc_raw")
-        w_sc_down = held([P, H], U8, "w_sc_down")
-        v_planes = [held([P, S], U8, "v_plane%d" % a) for a in range(K_PASSES)]
-        for plane in [tab_sc[32:64, :], tab_sc[64:P, :], w_sc_raw[:], w_sc_down[:]] + [plane[:] for plane in v_planes]:
+        w_sc_raw = held([P, K_PASSES * H], U8, "w_sc_raw")
+        v_planes = held([P, K_PASSES * S], U8, "v_planes")
+        for plane in [tab_sc[32:64, :], tab_sc[64:P, :], w_sc_raw[:], v_planes[:]]:
             nc.vector.memset(plane.bitcast(I32), 0)
-        nc.sync.dma_start(tab_sc[0:32, :].bitcast(I32), tab_scales.rearrange("a q c -> (a q) c").bitcast(I32))
+        nc.sync.dma_start(tab_sc[0:32, :].bitcast(I32), tab_scales.rearrange("a q c -> q a c").bitcast(I32))
 
         offsets = keep.tile([P, S // 16], U16, name="offsets")
         nc.sync.dma_start(offsets[:], offs)
         pages = [held([P, T], F32, "page%d" % t) for t in range(PACK)]
         gT_dealt = gT.rearrange("(p t) c -> t p c", t=PACK)
-        nc.sync.dma_start(pages[0][:], gT_dealt[0])
         lv_sb = held([P, PACK], F32, "lv_sb")
-        nc.sync.dma_start(lv_sb[:], lv.rearrange("(p t) -> p t", t=PACK))
         b_sb = held([P, H_GROUPS, PACK], F32, "b_sb")
-        nc.sync.dma_start(b_sb[:], b.rearrange("(g p t) -> p g t", p=P, t=PACK))
         w2_raw = [held([P, PACK, GROUP], F32, "w2_raw%d" % g) for g in range(H_GROUPS)]
         w2_dealt = w2.rearrange("(p j) c -> p j c", j=PACK)
         w1_raw = held([P, K_PASSES, 2 * H], U8, "w1_raw")
         tab = [held([P, T], I32, "tab%d" % a) for a in range(K_PASSES)]
-        nc.sync.dma_start(pages[1][:], gT_dealt[1])
-        nc.sync.dma_start(pages[2][:], gT_dealt[2])
-        nc.sync.dma_start(pages[3][:], gT_dealt[3])
-        for q in range(4):
-            nc.sync.dma_start(
-                w_sc_raw[32 * q + 8 : 32 * q + 12, :].rearrange("p (a c) -> p a c", a=H_GROUPS).bitcast(I32),
-                w3_scales[:, 4 * q : 4 * q + 4, :].rearrange("a r c -> r a c").bitcast(I32),
-            )
-        nc.sync.dma_start(w2_raw[0][:], w2_dealt[:, :, 0:GROUP])
-        nc.sync.dma_start(w1_raw[:].bitcast(I32), w1_words.rearrange("a p c -> p a c").bitcast(I32))
-        nc.sync.dma_start(w2_raw[1][:], w2_dealt[:, :, GROUP:H])
-        nc.sync.dma_start(tab[0][:], tab_words[0].rearrange("p c i -> p (c i)").bitcast(I32))
-        nc.sync.dma_start(tab[1][:], tab_words[1].rearrange("p c i -> p (c i)").bitcast(I32))
         w3_raw = held([P, H_GROUPS, N], I32, "w3_raw")
-        nc.sync.dma_start(w3_raw[:], w3_words.rearrange("a p c i -> p a (c i)").bitcast(I32))
 
-        for q in range(4):
-            nc.gpsimd.dma_start(
-                w_sc_raw[32 * q : 32 * q + 8, :].bitcast(I32), w1_scales[:, 4 * q : 4 * q + 4, :].bitcast(I32)
-            )
-        neg_b = held([P, H_GROUPS, PACK], F32, "neg_b")
-        nc.gpsimd.tensor_scalar(neg_b[:], b_sb[:], -1.0, 0.0, ALU.mult, ALU.add)
+        def load_page(t):
+            nc.sync.dma_start(pages[t][:], gT_dealt[t])
+
+        def load_scale_rows(scales, row, quadrants):
+            width = scales.shape[0] * scales.shape[2]
+            for q in quadrants:
+                nc.sync.dma_start(
+                    w_sc_raw[32 * q + row : 32 * q + row + 4, 0:width].bitcast(I32),
+                    scales[:, 4 * q : 4 * q + 4, :].rearrange("a r c -> r a c").bitcast(I32),
+                )
+
+        def load_w2(g):
+            nc.sync.dma_start(w2_raw[g][:], w2_dealt[:, :, g * GROUP : (g + 1) * GROUP])
+
+        def load_tab(a):
+            nc.sync.dma_start(tab[a][:], tab_words[a].rearrange("p c i -> p (c i)").bitcast(I32))
+
+        load_page(0)
+        nc.sync.dma_start(lv_sb[:], lv.rearrange("(p t) -> p t", t=PACK))
+        nc.sync.dma_start(b_sb[:], b.rearrange("(g p t) -> p g t", p=P, t=PACK))
+        load_page(1)
+        load_scale_rows(w1_scales, 0, (0, 1))
+        load_page(2)
+        load_scale_rows(w1_scales, 0, (2, 3))
+        load_page(3)
+        load_scale_rows(w3_scales, W3_ROW, (0, 1))
+        nc.sync.dma_start(w1_raw[:].bitcast(I32), w1_words.rearrange("a p c -> p a c").bitcast(I32))
+        load_scale_rows(w3_scales, W3_ROW, (2, 3))
+        load_tab(0)
+        load_w2(0)
+        load_w2(1)
+        load_tab(1)
+        nc.sync.dma_start(w3_raw[:], w3_words.rearrange("a p c i -> p a (c i)").bitcast(I32))
 
         def picks(first, count):
             return offsets[:, first // 16 : (first + count) // 16]
 
         v_sc = held([P, S], U8, "v_sc")
         nc.vector.tensor_copy(v_sc[:], tab_sc[:].indirect(offsets[:]))
-        for a in range(K_PASSES):
-            for q in range(4):
-                row = 16 * a + 4 * q
-                nc.gpsimd.dma_start(v_planes[a][32 * q : 32 * q + 4, :].bitcast(I32), v_sc[row : row + 4, :].bitcast(I32))
+        for q in range(4):
+            nc.gpsimd.dma_start(v_planes[32 * q : 32 * q + 4, :].bitcast(I32), v_sc[8 * q : 8 * q + 8, :].bitcast(I32))
 
-        gains = [held([P, S], F32, "gains%d" % t) for t in range(PACK)]
-        lg_rows = held([P, PACK, HALF], BF16, "lg_rows")
-        late_logs = [held([P, HALF], F32, "late_logs%d" % t) for t in range(PACK)]
-        for t in range(PACK):
-            for half in range(HALVES):
-                picked = gains[t][:, half * HALF : (half + 1) * HALF]
-                nc.vector.tensor_copy(picked, pages[t][:].indirect(picks(half * HALF, HALF)))
-            logs = ring.tile([P, HALF], F32, name="logs")
-            nc.scalar.activation(logs[:], gains[t][:, 0:HALF], ACT.Ln)
-            nc.scalar.activation(lg_rows[:, t, :], logs[:], ACT.Copy, scale=lv_sb[:, t : t + 1])
-            nc.scalar.activation(late_logs[t][:], gains[t][:, HALF:S], ACT.Ln)
-
-        def quantize(woven, name):
-            codes = held([P, woven.shape[1] // PACK], U32, name + "_codes")
-            scales = held([P, woven.shape[1] // PACK], U8, name + "_scales")
+        def quantize(woven, codes_name, scales_name):
+            codes = held([P, woven.shape[1] // PACK], U32, codes_name)
+            scales = held([P, woven.shape[1] // PACK], U8, scales_name)
             nc.vector.quantize_mx(codes[:].bitcast(FP8X4), scales[:], woven[:])
             return codes, scales
 
-        def quantize_w2(g):
-            woven = held([P, PACK * GROUP], BF16, "w2_woven%d" % g)
-            copy = nc.vector.tensor_copy if g == 0 else nc.scalar.copy
-            copy(
+        def weave_w2(g):
+            woven = held([P, PACK * GROUP], BF16, "logs%d" % g)
+            nc.scalar.copy(
                 woven[:].rearrange("p (t m j) -> p m t j", t=PACK, j=PACK),
                 w2_raw[g][:].rearrange("p j (m t) -> p m t j", t=PACK),
             )
-            return woven, quantize(woven, "w2_%d" % g)
+            return woven
 
-        def quantize_lg(rows, lo, hi, woven_name, name, copy=nc.vector.tensor_copy):
-            woven = held([P, PACK * (hi - lo)], BF16, woven_name)
-            weave(copy, woven[:], rows[:, :, lo:hi])
-            return quantize(woven, name)
+        def gather_words(a, first, count, name):
+            words = held([P, count], U32, name)
+            nc.vector.tensor_copy(words[:], tab[a][:].bitcast(U32).indirect(picks(first, count)))
+            return [(words, c * CHUNK) for c in range(count // CHUNK)]
 
-        w_sc = held([P, H], U8, "w_sc")
+        gains = [held([P, S], F32, "gains%d" % t) for t in range(PACK)]
+        lg_rows = held([P, PACK, S], BF16, "lg_rows")
+        for t in range(PACK):
+            nc.vector.tensor_copy(gains[t][:], pages[t][:].indirect(offsets[:]))
+            logs = held([P, S], F32, "logs%d" % (t % 2))
+            nc.scalar.activation(logs[:], gains[t][:], ACT.Ln)
+            nc.gpsimd.tensor_scalar(lg_rows[:, t, :], logs[:], lv_sb[:, t : t + 1], 0.0, ALU.mult, ALU.add)
+        exp_warm = held([P, 1], F32, "exp_warm")
+        nc.scalar.activation(exp_warm[:], logs[:, 0:1], ACT.Exp, scale=0.0)
+        neg_b = held([P, H_GROUPS, PACK], F32, "neg_b")
+        nc.gpsimd.tensor_scalar(neg_b[:], b_sb[:], -1.0, 0.0, ALU.mult, ALU.add)
+        w_sc = held([P, K_PASSES * H], U8, "w_sc")
         nc.vector.tensor_copy(
             w_sc[:].rearrange("p (g t m) -> p g t m", t=PACK, m=P),
             w_sc_raw[:].rearrange("p (g m t) -> p g t m", t=PACK, m=P),
         )
-        nc.scalar.dma_start(w_sc_down[0:MOVED, :].bitcast(I32), w_sc[4 : 4 + MOVED, :].bitcast(I32))
-        w1_planes = [w_sc, w_sc_down]
-
-        early_mx = quantize_lg(lg_rows, 0, HALF, "lg_woven", "lg0")
-        lg_mx = [early_mx + (0,), early_mx + (CHUNK,)]
-        w2_woven, w2_mx = zip(*[quantize_w2(g) for g in range(H_GROUPS)])
-        exp_warm = held([P, 1], F32, "exp_warm")
-        nc.scalar.activation(exp_warm[:], w2_woven[1][:, 0:1], ACT.Exp, scale=0.0)
-
         w1_sb = held([P, K_PASSES * 2 * H], U8, "w1_sb")
         nc.vector.tensor_copy(
             w1_sb[:].bitcast(U16).rearrange("p (g t m) -> p g t m", t=PACK, m=P),
             w1_raw[:].rearrange("p a c -> p (a c)").bitcast(U16).rearrange("p (g m t) -> p g t m", t=PACK, m=P),
         )
+        v_words = [gather_words(0, 0, S, "v0"), []]
 
-        v_words = []
+        def weave_lg_on_gpsimd(first, count, name):
+            woven = held([P, PACK * count], BF16, name)
+            for lo in range(0, count, P):
+                nc.gpsimd.tensor_scalar(
+                    woven[:, PACK * lo : PACK * (lo + P)].rearrange("p (c t) -> p c t", t=PACK),
+                    lg_rows[:, :, first + lo : first + lo + P].rearrange("p t c -> p c t"),
+                    1.0,
+                    0.0,
+                    ALU.mult,
+                    ALU.add,
+                )
+            return woven
 
-        def first_product(c):
-            first = c * CHUNK
-            within = first % HALF
-            if within == 0:
-                names = ("v0", "v1") if c == 0 else ("w3_raw", "tab0")
-                v_words[:] = [held([P, HALF], U32, name) for name in names]
-            count = CHUNK if first < HALF else HALF
-            if first % count == 0:
-                for a in range(K_PASSES):
-                    window = tab[a][:].bitcast(U32).indirect(picks(first, count))
-                    nc.vector.tensor_copy(v_words[a][:, within : within + count], window)
-            lg_codes, lg_scales, lg_first = lg_mx[c]
-            lg_cols = slice(lg_first, lg_first + CHUNK)
-            banks = [bank(t) for t in range(PACK)]
-            sums = [[banks[t][:, g * CHUNK : (g + 1) * CHUNK] for g in range(H_GROUPS)] for t in range(PACK)]
-            sums[PACK - 1][H_GROUPS - 1] = bank(PACK + c % 2)[:, 0:CHUNK]
-            alone = [(PACK - 1, g) for g in range(H_GROUPS)]
-            for step in range(2):
-                for t in range(PACK):
-                    w_cols = slice(t * P, (t + 1) * P)
-                    nc.tensor.matmul_mx(
-                        sums[t][step],
-                        lhsT=w2_mx[step][0][:, w_cols].bitcast(FP8X4),
-                        lhsT_scale=w2_mx[step][1][:, w_cols],
-                        rhs=lg_codes[:, lg_cols].bitcast(FP8X4),
-                        rhs_scale=lg_scales[:, lg_cols],
-                        start=(step == 0),
-                        stop=False,
-                    )
-                for t in range(PACK):
-                    for g in range(H_GROUPS):
-                        c0 = g * GROUP + t * P
-                        for n0 in range(0, CHUNK, P):
-                            nc.tensor.matmul_mx(
-                                sums[t][g][:, n0 : n0 + P],
-                                lhsT=w1_sb[:, 2 * (step * H + c0) : 2 * (step * H + c0 + P)].bitcast(FP4X4),
-                                lhsT_scale=w1_planes[step][:, c0 : c0 + P],
-                                rhs=v_words[step][:, within + n0 : within + n0 + P].bitcast(FP8X4),
-                                rhs_scale=v_planes[step][:, first + n0 : first + n0 + P],
-                                start=(step == 0 and n0 == 0 and (t, g) == alone[1]),
-                                stop=(step == 1 and n0 == CHUNK - P and (g == H_GROUPS - 1 or (t, g) in alone)),
+        lg_second = quantize(weave_lg_on_gpsimd(CHUNK, CHUNK, "lg_woven1"), "tab0", "lg_scales1")
+        late_woven = weave_lg_on_gpsimd(2 * CHUNK, 2 * CHUNK, "lg_woven2")
+        w2_mx = [quantize(weave_w2(0), "w2_codes0", "w2_scales0")]
+        first_woven = held([P, PACK * CHUNK], BF16, "w2_raw0")
+        weave(nc.scalar.copy, first_woven[:], lg_rows[:, :, 0:CHUNK])
+        lg_first = quantize(first_woven, "lg_codes0", "lg_scales0")
+        lg_late = quantize(late_woven, "w2_raw0", "lg_scales2")
+        lg_mx = [lg_first + (0,), lg_second + (0,), lg_late + (0,), lg_late + (CHUNK,)]
+        for c in range(2):
+            v_words[1].extend(gather_words(1, c * CHUNK, CHUNK, "v1_%d" % c))
+        w2_mx.append(quantize(weave_w2(1), "w2_codes1", "w2_scales1"))
+
+        def first_sums(c, g, pair, w2_at):
+            bank = psum.tile([P, 2 * CHUNK], F32, name="sums", bufs=SUM_BANKS)
+            passes = []
+            for step in range(K_PASSES + 1):
+                for u in range(2):
+                    t = 2 * pair + u
+                    acc = bank[:, u * CHUNK : (u + 1) * CHUNK]
+                    if step == w2_at:
+                        codes, scales, at = lg_mx[c]
+                        w_cols = slice(t * P, (t + 1) * P)
+                        passes.append(
+                            (
+                                acc,
+                                w2_mx[g][0][:, w_cols].bitcast(FP8X4),
+                                w2_mx[g][1][:, w_cols],
+                                codes[:, at : at + CHUNK].bitcast(FP8X4),
+                                scales[:, at : at + CHUNK],
                             )
-            return sums
-
-        def hidden(c, copy):
-            sums = first_product(c)
-            rows = held([P, PACK, H_GROUPS * CHUNK], BF16, "h_rows%d" % c)
-            for t in range(PACK):
-                for g in range(H_GROUPS):
-                    span = slice(g * CHUNK, (g + 1) * CHUNK)
-                    nc.scalar.activation(rows[:, t, span], sums[t][g], ACT.Relu, bias=neg_b[:, g, t : t + 1])
-            woven = held([P, PACK * HALF], BF16, "h_woven%d" % (c % 2))
-            weave(copy, woven[:], rows[:])
-            return quantize(woven, "h%d" % (c % 2))
-
-        def drift_banks(c):
-            pair = bank(7)
-            return [bank(PACK + (c + 1) % 2)[:, 0:CHUNK], bank(6)[:, 0:CHUNK], pair[:, 0:CHUNK], pair[:, CHUNK:HALF]]
-
-        def drift(t, h_mx, acc):
-            for a in range(H_GROUPS):
-                c0 = a * N + t * P
+                        )
+                        continue
+                    a = step if step < w2_at else step - 1
+                    words, at = v_words[a][c]
+                    w_col = a * H + g * GROUP + t * P
+                    for n0 in range(0, CHUNK, P):
+                        v_col = a * S + c * CHUNK + n0
+                        passes.append(
+                            (
+                                acc[:, n0 : n0 + P],
+                                w1_sb[:, 2 * w_col : 2 * (w_col + P)].bitcast(FP4X4),
+                                w_sc[:, w_col : w_col + P],
+                                words[:, at + n0 : at + n0 + P].bitcast(FP8X4),
+                                v_planes[:, v_col : v_col + P],
+                            )
+                        )
+            for i, (acc, lhsT, lhsT_scale, rhs, rhs_scale) in enumerate(passes):
                 nc.tensor.matmul_mx(
                     acc,
-                    lhsT=w3_sb[:, c0 : c0 + P].bitcast(FP8X4),
-                    lhsT_scale=w_sc[8:P, c0 : c0 + P],
-                    rhs=h_mx[0][:, a * CHUNK : (a + 1) * CHUNK].bitcast(FP8X4),
-                    rhs_scale=h_mx[1][:, a * CHUNK : (a + 1) * CHUNK],
-                    start=(a == 0),
-                    stop=(a == H_GROUPS - 1),
+                    lhsT=lhsT,
+                    lhsT_scale=lhsT_scale,
+                    rhs=rhs,
+                    rhs_scale=rhs_scale,
+                    start=(i == 0),
+                    stop=(i == len(passes) - 1),
                 )
-            return acc
+            return bank
 
-        def exp_into(factors, sums):
+        def relu_rows(c, g, rows, w2_at):
+            for pair in range(2):
+                bank = first_sums(c, g, pair, w2_at)
+                for u in range(2):
+                    t = 2 * pair + u
+                    acc = bank[:, u * CHUNK : (u + 1) * CHUNK]
+                    nc.scalar.activation(rows[:, t, :], acc, ACT.Relu, bias=neg_b[:, g, t : t + 1])
+
+        def hidden(c):
+            rows = held([P, PACK, H_GROUPS * CHUNK], BF16, "h_rows%d" % c)
+            for g in range(H_GROUPS):
+                relu_rows(c, g, rows[:, :, g * CHUNK : (g + 1) * CHUNK], 0)
+            woven = held([P, PACK * H_GROUPS * CHUNK], BF16, "h_woven%d" % (c % 2))
+            weave(nc.scalar.copy, woven[:], rows[:])
+            codes, scales = quantize(woven, "h_codes%d" % (c % 2), "h_scales%d" % (c % 2))
+            return [(codes, scales, g * CHUNK) for g in range(H_GROUPS)]
+
+        def drift(pair, h_mx):
+            bank = psum.tile([P, 2, CHUNK], F32, name="drift", bufs=DRIFT_BANKS)
+            for a in range(H_GROUPS):
+                codes, scales, at = h_mx[a]
+                for u in range(2):
+                    c0 = a * N + (2 * pair + u) * P
+                    nc.tensor.matmul_mx(
+                        bank[:, u, :],
+                        lhsT=w3_sb[:, c0 : c0 + P].bitcast(FP8X4),
+                        lhsT_scale=w_sc[W3_ROW:P, c0 : c0 + P],
+                        rhs=codes[:, at : at + CHUNK].bitcast(FP8X4),
+                        rhs_scale=scales[:, at : at + CHUNK],
+                        start=(a == 0 and u == 0),
+                        stop=(a == H_GROUPS - 1 and u == 1),
+                    )
+            return bank
+
+        def exp_into(factors, bank):
             for u in range(2):
-                nc.scalar.activation(factors[:, u, :], sums[u], ACT.Exp)
+                nc.scalar.activation(factors[:, u, :], bank[:, u, :], ACT.Exp)
 
         def rewrite(t, first, count, factor):
             nc.vector.tensor_tensor(
                 pages[t][:].indirect(picks(first, count)), gains[t][:, first : first + count], factor, ALU.mult
             )
 
-        h_mx = hidden(0, nc.vector.tensor_copy)
-        late_rows = held([P, PACK, HALF], BF16, "w2_raw1")
-        for t in range(PACK):
-            nc.scalar.activation(late_rows[:, t, :], late_logs[t][:], ACT.Copy, scale=lv_sb[:, t : t + 1])
-        late_mx = quantize_lg(late_rows, 0, HALF, "lg_woven", "lg2", nc.scalar.copy)
-        lg_mx.extend([late_mx + (0,), late_mx + (CHUNK,)])
         w3_sb = held([P, H_GROUPS * N], I32, "w3_sb")
         nc.vector.tensor_copy(
             w3_sb[:].rearrange("p (a t m) -> p a m t", t=PACK, m=P),
             w3_raw[:].rearrange("p a (m t) -> p a m t", t=PACK),
         )
+        v_words[1].extend(gather_words(1, 2 * CHUNK, 2 * CHUNK, "w3_raw"))
+        h_mx = []
+        for g in range(H_GROUPS):
+            rows = held([P, PACK, CHUNK], BF16, "h_first_rows%d" % g)
+            relu_rows(0, g, rows[:], 1 + g)
+            woven = held([P, PACK * CHUNK], BF16, "h_first_woven%d" % g)
+            weave(nc.vector.tensor_copy, woven[:], rows[:])
+            h_mx.append(quantize(woven, "h_first_codes%d" % g, "h_first_scales%d" % g) + (0,))
+
         out_dealt = out_0.rearrange("(p t) c -> t p c", t=PACK)
         last = PACK - 1
+        y_rows = held([P, PACK, T], BF16, "w2_raw1")
 
         def finish(t):
             nc.sync.dma_start(out_dealt[t], pages[t][:])
@@ -266,24 +290,23 @@ def tile_list_gain_drift_rewrite_kernel(
 
         for c in range(CHUNKS - 1):
             first = c * CHUNK
-            sums = [drift(t, h_mx, acc) for t, acc in enumerate(drift_banks(c))]
-            early = keep.tile([P, 2, CHUNK], F32, name="early", bufs=2)
-            exp_into(early[:], sums[0:2])
+            banks = [drift(pair, h_mx) for pair in range(2)]
+            early = held([P, 2, CHUNK], F32, "early", bufs=2)
+            exp_into(early[:], banks[0])
             for t in range(2):
                 rewrite(t, first, CHUNK, early[:, t, :])
-            h_mx = hidden(c + 1, nc.scalar.copy)
+            h_mx = hidden(c + 1)
             late = held([P, 2, 2 * CHUNK], F32, "h_rows%d" % (c + 1))
-            exp_into(late[:, :, 0:CHUNK], sums[2:4])
+            exp_into(late[:, :, 0:CHUNK], banks[1])
             rewrite(2, first, CHUNK, late[:, 0, 0:CHUNK])
             if c < CHUNKS - 2:
                 rewrite(last, first, CHUNK, late[:, 1, 0:CHUNK])
 
         first = S - CHUNK
-        sums = [drift(t, h_mx, acc) for t, acc in enumerate(drift_banks(CHUNKS - 1))]
-        y_rows = held([P, PACK, T], BF16, "h1_codes")
-        early = keep.tile([P, 2, CHUNK], F32, name="early", bufs=2)
-        exp_into(early[:], sums[0:2])
-        exp_into(late[:, :, CHUNK : 2 * CHUNK], sums[2:4])
+        banks = [drift(pair, h_mx) for pair in range(2)]
+        early = held([P, 2, CHUNK], F32, "early", bufs=2)
+        exp_into(early[:], banks[0])
+        exp_into(late[:, :, CHUNK : 2 * CHUNK], banks[1])
         for t in range(2):
             rewrite(t, first, CHUNK, early[:, t, :])
             finish(t)
@@ -291,7 +314,7 @@ def tile_list_gain_drift_rewrite_kernel(
         finish(2)
         rewrite(last, first - CHUNK, 2 * CHUNK, late[:, 1, :])
         finish(last)
-        y_woven = held([P, PACK * T], BF16, "y_woven")
+        y_woven = held([P, PACK * T], BF16, "tab1")
         y_scales = held([P, T], U8, "y_scales")
         words_out = out_1[0].rearrange("p m t -> p (m t)").bitcast(I32)
         nc.vector.tensor_copy(y_rows[:, last, 0:Y_SPLIT], pages[last][:, 0:Y_SPLIT])

@@ -51,7 +51,8 @@ def tile_list_gain_drift_rewrite_kernel(
         tab_sc = held([P, T], U8, "tab_sc")
         w_sc_raw = held([P, K_PASSES * H], U8, "w_sc_raw")
         v_planes = held([P, K_PASSES * S], U8, "v_planes")
-        for plane in [tab_sc[32:64, :], tab_sc[64:P, :], w_sc_raw[:], v_planes[:]]:
+        nc.gpsimd.memset(w_sc_raw[:].bitcast(I32), 0)
+        for plane in [tab_sc[32:64, :], tab_sc[64:P, :], v_planes[:]]:
             nc.vector.memset(plane.bitcast(I32), 0)
         nc.sync.dma_start(tab_sc[0:32, :].bitcast(I32), tab_scales.rearrange("a q c -> q a c").bitcast(I32))
 
@@ -63,7 +64,7 @@ def tile_list_gain_drift_rewrite_kernel(
         b_sb = held([P, H_GROUPS, PACK], F32, "b_sb")
         w2_raw = [held([P, PACK, GROUP], F32, "w2_raw%d" % g) for g in range(H_GROUPS)]
         w2_dealt = w2.rearrange("(p j) c -> p j c", j=PACK)
-        w1_raw = held([P, K_PASSES, 2 * H], U8, "w1_raw")
+        w1_raw = [held([P, 2 * H], U8, "w1_raw%d" % a) for a in range(K_PASSES)]
         tab = [held([P, T], I32, "tab%d" % a) for a in range(K_PASSES)]
         w3_raw = held([P, H_GROUPS, N], I32, "w3_raw")
 
@@ -88,14 +89,15 @@ def tile_list_gain_drift_rewrite_kernel(
         nc.sync.dma_start(lv_sb[:], lv.rearrange("(p t) -> p t", t=PACK))
         nc.sync.dma_start(b_sb[:], b.rearrange("(g p t) -> p g t", p=P, t=PACK))
         load_page(1)
-        load_scale_rows(w1_scales, 0, (0, 1))
+        load_scale_rows(w1_scales, 0, range(0, 3))
         load_page(2)
-        load_scale_rows(w1_scales, 0, (2, 3))
+        load_scale_rows(w1_scales, 0, range(3, 4))
+        load_scale_rows(w3_scales, W3_ROW, range(0, 2))
         load_page(3)
-        load_scale_rows(w3_scales, W3_ROW, (0, 1))
-        nc.sync.dma_start(w1_raw[:].bitcast(I32), w1_words.rearrange("a p c -> p a c").bitcast(I32))
-        load_scale_rows(w3_scales, W3_ROW, (2, 3))
+        load_scale_rows(w3_scales, W3_ROW, range(2, 4))
         load_tab(0)
+        for a in range(K_PASSES):
+            nc.sync.dma_start(w1_raw[a][:].bitcast(I32), w1_words[a].bitcast(I32))
         load_w2(0)
         load_w2(1)
         load_tab(1)
@@ -144,12 +146,14 @@ def tile_list_gain_drift_rewrite_kernel(
             w_sc[:].rearrange("p (g t m) -> p g t m", t=PACK, m=P),
             w_sc_raw[:].rearrange("p (g m t) -> p g t m", t=PACK, m=P),
         )
-        w1_sb = held([P, K_PASSES * 2 * H], U8, "w1_sb")
-        nc.vector.tensor_copy(
-            w1_sb[:].bitcast(U16).rearrange("p (g t m) -> p g t m", t=PACK, m=P),
-            w1_raw[:].rearrange("p a c -> p (a c)").bitcast(U16).rearrange("p (g m t) -> p g t m", t=PACK, m=P),
-        )
-        v_words = [gather_words(0, 0, S, "v0"), []]
+        v_words = [gather_words(0, 0, 2 * CHUNK, "v0"), []]
+        w1_sb = held([P, K_PASSES, 2 * H], U8, "w1_sb")
+        for a in range(K_PASSES):
+            nc.vector.tensor_copy(
+                w1_sb[:, a, :].bitcast(U16).rearrange("p (g t m) -> p g t m", t=PACK, m=P),
+                w1_raw[a][:].bitcast(U16).rearrange("p (g m t) -> p g t m", t=PACK, m=P),
+            )
+        v_words[0].extend(gather_words(0, 2 * CHUNK, 2 * CHUNK, "w1_raw0"))
 
         def weave_lg_on_gpsimd(first, count, name):
             woven = held([P, PACK * count], BF16, name)
@@ -164,16 +168,15 @@ def tile_list_gain_drift_rewrite_kernel(
                 )
             return woven
 
-        lg_second = quantize(weave_lg_on_gpsimd(CHUNK, CHUNK, "lg_woven1"), "tab0", "lg_scales1")
-        late_woven = weave_lg_on_gpsimd(2 * CHUNK, 2 * CHUNK, "lg_woven2")
+        second_woven = weave_lg_on_gpsimd(CHUNK, CHUNK, "w1_raw1")
         w2_mx = [quantize(weave_w2(0), "w2_codes0", "w2_scales0")]
+        lg_second = quantize(second_woven, "tab0", "lg_scales1")
         first_woven = held([P, PACK * CHUNK], BF16, "w2_raw0")
         weave(nc.scalar.copy, first_woven[:], lg_rows[:, :, 0:CHUNK])
-        lg_first = quantize(first_woven, "lg_codes0", "lg_scales0")
-        lg_late = quantize(late_woven, "w2_raw0", "lg_scales2")
-        lg_mx = [lg_first + (0,), lg_second + (0,), lg_late + (0,), lg_late + (CHUNK,)]
-        for c in range(2):
-            v_words[1].extend(gather_words(1, c * CHUNK, CHUNK, "v1_%d" % c))
+        lg_mx = [quantize(first_woven, "lg_codes0", "lg_scales0") + (0,), lg_second + (0,)]
+        late_woven = weave_lg_on_gpsimd(2 * CHUNK, 2 * CHUNK, "w2_raw0")
+        v_words[1].extend(gather_words(1, 0, CHUNK, "v1_first"))
+        v_words[1].extend(gather_words(1, CHUNK, S - CHUNK, "v1_rest"))
         w2_mx.append(quantize(weave_w2(1), "w2_codes1", "w2_scales1"))
 
         def first_sums(c, g, pair, w2_at):
@@ -198,14 +201,14 @@ def tile_list_gain_drift_rewrite_kernel(
                         continue
                     a = step if step < w2_at else step - 1
                     words, at = v_words[a][c]
-                    w_col = a * H + g * GROUP + t * P
+                    w_col = g * GROUP + t * P
                     for n0 in range(0, CHUNK, P):
                         v_col = a * S + c * CHUNK + n0
                         passes.append(
                             (
                                 acc[:, n0 : n0 + P],
-                                w1_sb[:, 2 * w_col : 2 * (w_col + P)].bitcast(FP4X4),
-                                w_sc[:, w_col : w_col + P],
+                                w1_sb[:, a, 2 * w_col : 2 * (w_col + P)].bitcast(FP4X4),
+                                w_sc[:, a * H + w_col : a * H + w_col + P],
                                 words[:, at + n0 : at + n0 + P].bitcast(FP8X4),
                                 v_planes[:, v_col : v_col + P],
                             )
@@ -265,19 +268,21 @@ def tile_list_gain_drift_rewrite_kernel(
                 pages[t][:].indirect(picks(first, count)), gains[t][:, first : first + count], factor, ALU.mult
             )
 
-        w3_sb = held([P, H_GROUPS * N], I32, "w3_sb")
-        nc.vector.tensor_copy(
-            w3_sb[:].rearrange("p (a t m) -> p a m t", t=PACK, m=P),
-            w3_raw[:].rearrange("p a (m t) -> p a m t", t=PACK),
-        )
-        v_words[1].extend(gather_words(1, 2 * CHUNK, 2 * CHUNK, "w3_raw"))
-        h_mx = []
+        woven = held([P, H_GROUPS, PACK * CHUNK], BF16, "h_first_woven")
         for g in range(H_GROUPS):
             rows = held([P, PACK, CHUNK], BF16, "h_first_rows%d" % g)
             relu_rows(0, g, rows[:], 1 + g)
-            woven = held([P, PACK * CHUNK], BF16, "h_first_woven%d" % g)
-            weave(nc.vector.tensor_copy, woven[:], rows[:])
-            h_mx.append(quantize(woven, "h_first_codes%d" % g, "h_first_scales%d" % g) + (0,))
+            weave(nc.vector.tensor_copy, woven[:, g, :], rows[:])
+            if g == 0:
+                w3_sb = held([P, H_GROUPS * N], I32, "h_first_rows0")
+                nc.vector.tensor_copy(
+                    w3_sb[:].rearrange("p (a t m) -> p a m t", t=PACK, m=P),
+                    w3_raw[:].rearrange("p a (m t) -> p a m t", t=PACK),
+                )
+        codes, scales = quantize(woven[:].rearrange("p g c -> p (g c)"), "h_first_codes", "h_first_scales")
+        h_mx = [(codes, scales, g * CHUNK) for g in range(H_GROUPS)]
+        lg_late = quantize(late_woven, "h_first_woven", "lg_scales2")
+        lg_mx.extend([lg_late + (0,), lg_late + (CHUNK,)])
 
         out_dealt = out_0.rearrange("(p t) c -> t p c", t=PACK)
         last = PACK - 1

@@ -27,6 +27,7 @@ SUM_BANKS = 6
 DRIFT_BANKS = 2
 Y_SPLIT = 1152
 Y_CHUNK = 512
+Y_LAST = 256
 W3_ROW = 4
 
 
@@ -242,26 +243,21 @@ def tile_list_gain_drift_rewrite_kernel(
             codes, scales = quantize(woven, "h_codes%d" % (c % 2), "h_scales%d" % (c % 2))
             return [(codes, scales, g * CHUNK) for g in range(H_GROUPS)]
 
-        def drift(pair, h_mx):
-            bank = psum.tile([P, 2, CHUNK], F32, name="drift", bufs=DRIFT_BANKS)
+        def drift_factor(t, h_mx):
+            bank = psum.tile([P, CHUNK], F32, name="drift", bufs=DRIFT_BANKS)
             for a in range(H_GROUPS):
                 codes, scales, at = h_mx[a]
-                for u in range(2):
-                    c0 = a * N + (2 * pair + u) * P
-                    nc.tensor.matmul_mx(
-                        bank[:, u, :],
-                        lhsT=w3_sb[:, c0 : c0 + P].bitcast(FP8X4),
-                        lhsT_scale=w_sc[W3_ROW:P, c0 : c0 + P],
-                        rhs=codes[:, at : at + CHUNK].bitcast(FP8X4),
-                        rhs_scale=scales[:, at : at + CHUNK],
-                        start=(a == 0 and u == 0),
-                        stop=(a == H_GROUPS - 1 and u == 1),
-                    )
+                c0 = a * N + t * P
+                nc.tensor.matmul_mx(
+                    bank[:],
+                    lhsT=w3_sb[:, c0 : c0 + P].bitcast(FP8X4),
+                    lhsT_scale=w_sc[W3_ROW:P, c0 : c0 + P],
+                    rhs=codes[:, at : at + CHUNK].bitcast(FP8X4),
+                    rhs_scale=scales[:, at : at + CHUNK],
+                    start=(a == 0),
+                    stop=(a == H_GROUPS - 1),
+                )
             return bank
-
-        def exp_into(factors, bank):
-            for u in range(2):
-                nc.scalar.activation(factors[:, u, :], bank[:, u, :], ACT.Exp)
 
         def rewrite(t, first, count, factor):
             nc.vector.tensor_tensor(
@@ -286,7 +282,6 @@ def tile_list_gain_drift_rewrite_kernel(
 
         out_dealt = out_0.rearrange("(p t) c -> t p c", t=PACK)
         last = PACK - 1
-        y_rows = held([P, PACK, T], BF16, "w2_raw1")
 
         def finish(t):
             nc.sync.dma_start(out_dealt[t], pages[t][:])
@@ -295,23 +290,26 @@ def tile_list_gain_drift_rewrite_kernel(
 
         for c in range(CHUNKS - 1):
             first = c * CHUNK
-            banks = [drift(pair, h_mx) for pair in range(2)]
             early = held([P, 2, CHUNK], F32, "early", bufs=2)
-            exp_into(early[:], banks[0])
             for t in range(2):
+                nc.scalar.activation(early[:, t, :], drift_factor(t, h_mx)[:], ACT.Exp)
                 rewrite(t, first, CHUNK, early[:, t, :])
+            banks = [drift_factor(t, h_mx) for t in range(2, PACK)]
             h_mx = hidden(c + 1)
             late = held([P, 2, 2 * CHUNK], F32, "h_rows%d" % (c + 1))
-            exp_into(late[:, :, 0:CHUNK], banks[1])
+            for u in range(2):
+                nc.scalar.activation(late[:, u, 0:CHUNK], banks[u][:], ACT.Exp)
             rewrite(2, first, CHUNK, late[:, 0, 0:CHUNK])
             if c < CHUNKS - 2:
                 rewrite(last, first, CHUNK, late[:, 1, 0:CHUNK])
 
         first = S - CHUNK
-        banks = [drift(pair, h_mx) for pair in range(2)]
         early = held([P, 2, CHUNK], F32, "early", bufs=2)
-        exp_into(early[:], banks[0])
-        exp_into(late[:, :, CHUNK : 2 * CHUNK], banks[1])
+        for t in range(2):
+            nc.scalar.activation(early[:, t, :], drift_factor(t, h_mx)[:], ACT.Exp)
+        for u in range(2):
+            nc.scalar.activation(late[:, u, CHUNK : 2 * CHUNK], drift_factor(2 + u, h_mx)[:], ACT.Exp)
+        y_rows = held([P, PACK, T], BF16, "h_codes1")
         for t in range(2):
             rewrite(t, first, CHUNK, early[:, t, :])
             finish(t)
@@ -320,22 +318,30 @@ def tile_list_gain_drift_rewrite_kernel(
         rewrite(last, first - CHUNK, 2 * CHUNK, late[:, 1, :])
         finish(last)
         y_woven = held([P, PACK * T], BF16, "tab1")
-        y_scales = held([P, T], U8, "y_scales")
+        y_scales = held([P, Y_CHUNK], U8, "y_scales")
         words_out = out_1[0].rearrange("p m t -> p (m t)").bitcast(I32)
-        nc.vector.tensor_copy(y_rows[:, last, 0:Y_SPLIT], pages[last][:, 0:Y_SPLIT])
+        on_vector = ((0, Y_CHUNK), (Y_CHUNK, Y_SPLIT))
+        on_scalar = ((Y_SPLIT, T - Y_CHUNK), (T - Y_CHUNK, T - Y_LAST), (T - Y_LAST, T))
+        for lo, hi in on_vector:
+            nc.vector.tensor_copy(y_rows[:, last, lo:hi], pages[last][:, lo:hi])
         nc.scalar.copy(y_rows[:, last, Y_SPLIT:T], pages[last][:, Y_SPLIT:T])
-        for copy, lo, hi in (
-            (nc.vector.tensor_copy, 0, Y_CHUNK),
-            (nc.vector.tensor_copy, Y_CHUNK, Y_SPLIT),
-            (nc.scalar.copy, Y_SPLIT, T - Y_CHUNK),
-            (nc.scalar.copy, T - Y_CHUNK, T),
-        ):
-            weave(copy, y_woven[:, PACK * lo : PACK * hi], y_rows[:, :, lo:hi])
-        for lo in range(0, T, Y_CHUNK):
-            hi = lo + Y_CHUNK
-            y_codes = held([P, hi - lo], I32, "y_codes%d" % lo)
-            nc.vector.quantize_mx(y_codes[:].bitcast(FP8X4), y_scales[:, lo:hi], y_woven[:, PACK * lo : PACK * hi])
-            nc.sync.dma_start(words_out[:, lo:hi], y_codes[:])
+        for copy, spans in ((nc.vector.tensor_copy, on_vector), (nc.scalar.copy, on_scalar)):
+            for lo, hi in spans:
+                weave(copy, y_woven[:, PACK * lo : PACK * hi], y_rows[:, :, lo:hi])
+        for store_lo, store_hi in ((0, 2 * Y_CHUNK), (2 * Y_CHUNK, T - Y_CHUNK), (T - Y_CHUNK, T - Y_LAST), (T - Y_LAST, T)):
+            y_codes = held([P, store_hi - store_lo], I32, "y_codes%d" % store_lo)
+            for lo in range(store_lo, store_hi, Y_CHUNK):
+                hi = min(lo + Y_CHUNK, store_hi)
+                plane, col = divmod(lo, Y_CHUNK)
+                nc.vector.quantize_mx(
+                    y_codes[:, lo - store_lo : hi - store_lo].bitcast(FP8X4),
+                    y_scales[4 * plane : P, col : col + hi - lo],
+                    y_woven[:, PACK * lo : PACK * hi],
+                )
+            nc.sync.dma_start(words_out[:, store_lo:store_hi], y_codes[:])
         for q in range(4):
             queue = nc.sync if q % 2 == 0 else nc.scalar
-            queue.dma_start(out_2[0, 4 * q : 4 * q + 4, :].bitcast(I32), y_scales[32 * q : 32 * q + 4, :].bitcast(I32))
+            queue.dma_start(
+                out_2[0, 4 * q : 4 * q + 4, :].rearrange("r (i c) -> i r c", c=Y_CHUNK).bitcast(I32),
+                y_scales[32 * q : 32 * q + 16, :].bitcast(I32),
+            )

@@ -28,7 +28,8 @@ DRIFT_BANKS = 2
 Y_SPLIT = 1152
 Y_CHUNK = 512
 Y_LAST = 256
-W3_ROW = 4
+W3_ROW = 8
+MOVED = 112
 
 
 def weave(copy, woven, rows):
@@ -50,10 +51,11 @@ def tile_list_gain_drift_rewrite_kernel(
             return keep.tile(shape, dtype, name=name, align_bytes=64, bufs=bufs)
 
         tab_sc = held([P, T], U8, "tab_sc")
-        w_sc_raw = held([P, K_PASSES * H], U8, "w_sc_raw")
+        w_sc_raw = held([P, H], U8, "w_sc_raw")
+        w_sc_down = held([P, H], U8, "w_sc_down")
         v_planes = held([P, K_PASSES * S], U8, "v_planes")
         nc.gpsimd.memset(w_sc_raw[:].bitcast(I32), 0)
-        for plane in [tab_sc[32:64, :], tab_sc[64:P, :], v_planes[:]]:
+        for plane in [tab_sc[32:64, :], tab_sc[64:P, :], v_planes[:], w_sc_down[:]]:
             nc.vector.memset(plane.bitcast(I32), 0)
         nc.sync.dma_start(tab_sc[0:32, :].bitcast(I32), tab_scales.rearrange("a q c -> q a c").bitcast(I32))
 
@@ -66,43 +68,46 @@ def tile_list_gain_drift_rewrite_kernel(
         w2_raw = [held([P, PACK, GROUP], F32, "w2_raw%d" % g) for g in range(H_GROUPS)]
         w2_dealt = w2.rearrange("(p j) c -> p j c", j=PACK)
         w1_raw = [held([P, 2 * H], U8, "w1_raw%d" % a) for a in range(K_PASSES)]
-        tab = [held([P, T], I32, "tab%d" % a) for a in range(K_PASSES)]
-        w3_raw = held([P, H_GROUPS, N], I32, "w3_raw")
+        tab = []
 
         def load_page(t):
             nc.sync.dma_start(pages[t][:], gT_dealt[t])
 
-        def load_scale_rows(scales, row, quadrants):
-            width = scales.shape[0] * scales.shape[2]
+        def load_w1_scale_rows(quadrants):
             for q in quadrants:
                 nc.sync.dma_start(
-                    w_sc_raw[32 * q + row : 32 * q + row + 4, 0:width].bitcast(I32),
-                    scales[:, 4 * q : 4 * q + 4, :].rearrange("a r c -> r a c").bitcast(I32),
+                    w_sc_raw[32 * q : 32 * q + 8, :].bitcast(I32), w1_scales[:, 4 * q : 4 * q + 4, :].bitcast(I32)
+                )
+
+        def load_w3_scale_rows(quadrants):
+            for q in quadrants:
+                nc.sync.dma_start(
+                    w_sc_raw[32 * q + W3_ROW : 32 * q + W3_ROW + 4, :].bitcast(I32),
+                    w3_scales[:, 4 * q : 4 * q + 4, :].rearrange("a r c -> r a c").bitcast(I32),
                 )
 
         def load_w2(g):
             nc.sync.dma_start(w2_raw[g][:], w2_dealt[:, :, g * GROUP : (g + 1) * GROUP])
 
-        def load_tab(a):
+        def load_tab(a, name):
+            tab.append(held([P, T], I32, name))
             nc.sync.dma_start(tab[a][:], tab_words[a].rearrange("p c i -> p (c i)").bitcast(I32))
 
         load_page(0)
         nc.sync.dma_start(lv_sb[:], lv.rearrange("(p t) -> p t", t=PACK))
         nc.sync.dma_start(b_sb[:], b.rearrange("(g p t) -> p g t", p=P, t=PACK))
         load_page(1)
-        load_scale_rows(w1_scales, 0, range(0, 3))
+        load_w1_scale_rows(range(0, 3))
         load_page(2)
-        load_scale_rows(w1_scales, 0, range(3, 4))
-        load_scale_rows(w3_scales, W3_ROW, range(0, 2))
+        load_w1_scale_rows(range(3, 4))
+        load_w3_scale_rows(range(0, 2))
         load_page(3)
-        load_scale_rows(w3_scales, W3_ROW, range(2, 4))
-        load_tab(0)
+        load_w3_scale_rows(range(2, 4))
+        load_tab(0, "tab0")
         for a in range(K_PASSES):
             nc.sync.dma_start(w1_raw[a][:].bitcast(I32), w1_words[a].bitcast(I32))
         load_w2(0)
         load_w2(1)
-        load_tab(1)
-        nc.sync.dma_start(w3_raw[:], w3_words.rearrange("a p c i -> p a (c i)").bitcast(I32))
 
         def picks(first, count):
             return offsets[:, first // 16 : (first + count) // 16]
@@ -119,7 +124,7 @@ def tile_list_gain_drift_rewrite_kernel(
             return codes, scales
 
         def weave_w2(g):
-            woven = held([P, PACK * GROUP], BF16, "logs%d" % g)
+            woven = held([P, PACK * GROUP], BF16, "logs%d" % (1 + g))
             nc.scalar.copy(
                 woven[:].rearrange("p (t m j) -> p m t j", t=PACK, j=PACK),
                 w2_raw[g][:].rearrange("p j (m t) -> p m t j", t=PACK),
@@ -133,48 +138,64 @@ def tile_list_gain_drift_rewrite_kernel(
 
         gains = [held([P, S], F32, "gains%d" % t) for t in range(PACK)]
         lg_rows = held([P, PACK, S], BF16, "lg_rows")
-        for t in range(PACK):
-            nc.vector.tensor_copy(gains[t][:], pages[t][:].indirect(offsets[:]))
-            logs = held([P, S], F32, "logs%d" % (t % 2))
-            nc.scalar.activation(logs[:], gains[t][:], ACT.Ln)
-            nc.gpsimd.tensor_scalar(lg_rows[:, t, :], logs[:], lv_sb[:, t : t + 1], 0.0, ALU.mult, ALU.add)
-        exp_warm = held([P, 1], F32, "exp_warm")
-        nc.scalar.activation(exp_warm[:], logs[:, 0:1], ACT.Exp, scale=0.0)
-        neg_b = held([P, H_GROUPS, PACK], F32, "neg_b")
-        nc.gpsimd.tensor_scalar(neg_b[:], b_sb[:], -1.0, 0.0, ALU.mult, ALU.add)
-        w_sc = held([P, K_PASSES * H], U8, "w_sc")
+        def log_gains(t, first, count, name):
+            span = slice(first, first + count)
+            nc.vector.tensor_copy(gains[t][:, span], pages[t][:].indirect(picks(first, count)))
+            logs = held([P, count], F32, name)
+            nc.scalar.activation(logs[:], gains[t][:, span], ACT.Ln)
+            nc.gpsimd.tensor_scalar(lg_rows[:, t, span], logs[:], lv_sb[:, t : t + 1], 0.0, ALU.mult, ALU.add)
+            return logs
+
+        def weave_lg_on_gpsimd(first, count, name):
+            woven = held([P, PACK * count], BF16, name)
+            nc.gpsimd.tensor_scalar(
+                woven[:].rearrange("p (c t) -> p c t", t=PACK),
+                lg_rows[:, :, first : first + count].rearrange("p t c -> p c t"),
+                1.0,
+                0.0,
+                ALU.mult,
+                ALU.add,
+            )
+            return woven
+
+        for t in range(PACK - 1):
+            log_gains(t, 0, S, "logs%d" % (t % 2))
+        w_sc = held([P, H], U8, "w_sc")
         nc.vector.tensor_copy(
             w_sc[:].rearrange("p (g t m) -> p g t m", t=PACK, m=P),
             w_sc_raw[:].rearrange("p (g m t) -> p g t m", t=PACK, m=P),
         )
-        v_words = [gather_words(0, 0, 2 * CHUNK, "v0"), []]
-        w1_sb = held([P, K_PASSES, 2 * H], U8, "w1_sb")
+        nc.sync.dma_start(w_sc_down[0:MOVED, :].bitcast(I32), w_sc[4 : 4 + MOVED, :].bitcast(I32))
+        load_tab(1, "w_sc_raw")
+        w3_raw = held([P, H_GROUPS, N], I32, "logs0")
+        nc.sync.dma_start(w3_raw[:], w3_words.rearrange("a p c i -> p a (c i)").bitcast(I32))
+        w1_planes = [w_sc, w_sc_down]
+        neg_b = held([P, H_GROUPS, PACK], F32, "neg_b")
+        log_gains(PACK - 1, 0, 2 * CHUNK, "logs1")
+        second_woven = weave_lg_on_gpsimd(CHUNK, CHUNK, "lg_woven1")
+        logs = log_gains(PACK - 1, 2 * CHUNK, 2 * CHUNK, "logs2")
+        nc.gpsimd.tensor_scalar(neg_b[:], b_sb[:], -1.0, 0.0, ALU.mult, ALU.add)
+        exp_warm = held([P, 1], F32, "exp_warm")
+        nc.scalar.activation(exp_warm[:], logs[:, 0:1], ACT.Exp, scale=0.0)
+        v_words = [gather_words(0, 0, S, "v0"), []]
+        w1_sb = held([P, K_PASSES, 2 * H], U8, "tab0")
         for a in range(K_PASSES):
             nc.vector.tensor_copy(
                 w1_sb[:, a, :].bitcast(U16).rearrange("p (g t m) -> p g t m", t=PACK, m=P),
                 w1_raw[a][:].bitcast(U16).rearrange("p (g m t) -> p g t m", t=PACK, m=P),
             )
-        v_words[0].extend(gather_words(0, 2 * CHUNK, 2 * CHUNK, "w1_raw0"))
 
-        def weave_lg_on_gpsimd(first, count, name):
-            woven = held([P, PACK * count], BF16, name)
-            for lo in range(0, count, P):
-                nc.gpsimd.tensor_scalar(
-                    woven[:, PACK * lo : PACK * (lo + P)].rearrange("p (c t) -> p c t", t=PACK),
-                    lg_rows[:, :, first + lo : first + lo + P].rearrange("p t c -> p c t"),
-                    1.0,
-                    0.0,
-                    ALU.mult,
-                    ALU.add,
-                )
+        def weave_lg(copy, c, name):
+            woven = held([P, PACK * CHUNK], BF16, name)
+            weave(copy, woven[:], lg_rows[:, :, c * CHUNK : (c + 1) * CHUNK])
             return woven
 
-        second_woven = weave_lg_on_gpsimd(CHUNK, CHUNK, "w1_raw1")
+        def quantize_lg(c, woven, name):
+            return quantize(woven, name, "lg_scales%d" % c) + (0,)
+
         w2_mx = [quantize(weave_w2(0), "w2_codes0", "w2_scales0")]
-        lg_second = quantize(second_woven, "tab0", "lg_scales1")
-        first_woven = held([P, PACK * CHUNK], BF16, "w2_raw0")
-        weave(nc.scalar.copy, first_woven[:], lg_rows[:, :, 0:CHUNK])
-        lg_mx = [quantize(first_woven, "lg_codes0", "lg_scales0") + (0,), lg_second + (0,)]
+        lg_second = quantize_lg(1, second_woven, "logs1")
+        lg_mx = [quantize_lg(0, weave_lg(nc.scalar.copy, 0, "w2_raw0"), "lg_codes0"), lg_second]
         late_woven = weave_lg_on_gpsimd(2 * CHUNK, 2 * CHUNK, "w2_raw0")
         v_words[1].extend(gather_words(1, 0, CHUNK, "v1_first"))
         v_words[1].extend(gather_words(1, CHUNK, S - CHUNK, "v1_rest"))
@@ -209,7 +230,7 @@ def tile_list_gain_drift_rewrite_kernel(
                             (
                                 acc[:, n0 : n0 + P],
                                 w1_sb[:, a, 2 * w_col : 2 * (w_col + P)].bitcast(FP4X4),
-                                w_sc[:, a * H + w_col : a * H + w_col + P],
+                                w1_planes[a][:, w_col : w_col + P],
                                 words[:, at + n0 : at + n0 + P].bitcast(FP8X4),
                                 v_planes[:, v_col : v_col + P],
                             )
@@ -238,7 +259,7 @@ def tile_list_gain_drift_rewrite_kernel(
             rows = held([P, PACK, H_GROUPS * CHUNK], BF16, "h_rows%d" % c)
             for g in range(H_GROUPS):
                 relu_rows(c, g, rows[:, :, g * CHUNK : (g + 1) * CHUNK], 0)
-            woven = held([P, PACK * H_GROUPS * CHUNK], BF16, "h_woven%d" % (c % 2))
+            woven = held([P, PACK * H_GROUPS * CHUNK], BF16, "h_first_codes" if c == 1 else "h_woven%d" % (c % 2))
             weave(nc.scalar.copy, woven[:], rows[:])
             codes, scales = quantize(woven, "h_codes%d" % (c % 2), "h_scales%d" % (c % 2))
             return [(codes, scales, g * CHUNK) for g in range(H_GROUPS)]
@@ -317,7 +338,7 @@ def tile_list_gain_drift_rewrite_kernel(
         finish(2)
         rewrite(last, first - CHUNK, 2 * CHUNK, late[:, 1, :])
         finish(last)
-        y_woven = held([P, PACK * T], BF16, "tab1")
+        y_woven = held([P, PACK * T], BF16, "w_sc_raw")
         y_scales = held([P, Y_CHUNK], U8, "y_scales")
         words_out = out_1[0].rearrange("p m t -> p (m t)").bitcast(I32)
         on_vector = ((0, Y_CHUNK), (Y_CHUNK, Y_SPLIT))

@@ -311,21 +311,22 @@ def tile_list_gain_drift_rewrite_kernel(
 
         for c in range(CHUNKS - 1):
             first = c * CHUNK
-            early = held([P, 2, CHUNK], F32, "early", bufs=2)
-            for t in range(2):
+            at_once = 3 if c == 0 else 2
+            early = held([P, last, CHUNK], F32, "early", bufs=2)
+            for t in range(at_once):
                 nc.scalar.activation(early[:, t, :], drift_factor(t, h_mx)[:], ACT.Exp)
                 rewrite(t, first, CHUNK, early[:, t, :])
-            banks = [drift_factor(t, h_mx) for t in range(2, PACK)]
+            banks = {t: drift_factor(t, h_mx) for t in range(at_once, PACK)}
             h_mx = hidden(c + 1)
             late = held([P, 2, 2 * CHUNK], F32, "h_rows%d" % (c + 1))
-            for u in range(2):
-                nc.scalar.activation(late[:, u, 0:CHUNK], banks[u][:], ACT.Exp)
-            rewrite(2, first, CHUNK, late[:, 0, 0:CHUNK])
-            if c < CHUNKS - 2:
-                rewrite(last, first, CHUNK, late[:, 1, 0:CHUNK])
+            for t in banks:
+                nc.scalar.activation(late[:, t - 2, 0:CHUNK], banks[t][:], ACT.Exp)
+            for t in banks:
+                if t < last or c < CHUNKS - 2:
+                    rewrite(t, first, CHUNK, late[:, t - 2, 0:CHUNK])
 
         first = S - CHUNK
-        early = held([P, 2, CHUNK], F32, "early", bufs=2)
+        early = held([P, last, CHUNK], F32, "early", bufs=2)
         for t in range(2):
             nc.scalar.activation(early[:, t, :], drift_factor(t, h_mx)[:], ACT.Exp)
         for u in range(2):
@@ -341,25 +342,30 @@ def tile_list_gain_drift_rewrite_kernel(
         y_woven = held([P, PACK * T], BF16, "w_sc_raw")
         y_scales = held([P, Y_CHUNK], U8, "y_scales")
         words_out = out_1[0].rearrange("p m t -> p (m t)").bitcast(I32)
-        on_vector = ((0, Y_CHUNK), (Y_CHUNK, Y_SPLIT))
-        on_scalar = ((Y_SPLIT, T - Y_CHUNK), (T - Y_CHUNK, T - Y_LAST), (T - Y_LAST, T))
-        for lo, hi in on_vector:
+        y_woven_at = lambda lo, hi: y_woven[:, PACK * lo : PACK * hi]
+
+        def weave_y(copy, lo, hi):
+            weave(copy, y_woven_at(lo, hi), y_rows[:, :, lo:hi])
+
+        def store_planes(lo, hi):
+            y_codes = held([P, hi - lo], I32, "y_codes%d" % lo)
+            plane, col = divmod(lo, Y_CHUNK)
+            scales = y_scales[4 * plane : P, col : col + hi - lo]
+            nc.vector.quantize_mx(y_codes[:].bitcast(FP8X4), scales, y_woven_at(lo, hi))
+            nc.sync.dma_start(words_out[:, lo:hi], y_codes[:])
+
+        for lo, hi in ((0, Y_CHUNK), (Y_CHUNK, Y_SPLIT)):
             nc.vector.tensor_copy(y_rows[:, last, lo:hi], pages[last][:, lo:hi])
         nc.scalar.copy(y_rows[:, last, Y_SPLIT:T], pages[last][:, Y_SPLIT:T])
-        for copy, spans in ((nc.vector.tensor_copy, on_vector), (nc.scalar.copy, on_scalar)):
-            for lo, hi in spans:
-                weave(copy, y_woven[:, PACK * lo : PACK * hi], y_rows[:, :, lo:hi])
-        for store_lo, store_hi in ((0, 2 * Y_CHUNK), (2 * Y_CHUNK, T - Y_CHUNK), (T - Y_CHUNK, T - Y_LAST), (T - Y_LAST, T)):
-            y_codes = held([P, store_hi - store_lo], I32, "y_codes%d" % store_lo)
-            for lo in range(store_lo, store_hi, Y_CHUNK):
-                hi = min(lo + Y_CHUNK, store_hi)
-                plane, col = divmod(lo, Y_CHUNK)
-                nc.vector.quantize_mx(
-                    y_codes[:, lo - store_lo : hi - store_lo].bitcast(FP8X4),
-                    y_scales[4 * plane : P, col : col + hi - lo],
-                    y_woven[:, PACK * lo : PACK * hi],
-                )
-            nc.sync.dma_start(words_out[:, store_lo:store_hi], y_codes[:])
+        for lo, hi in ((Y_SPLIT, T - Y_CHUNK), (T - Y_CHUNK, T - Y_LAST), (T - Y_LAST, T)):
+            weave_y(nc.scalar.copy, lo, hi)
+        middle = 2 * Y_CHUNK
+        weave_y(nc.vector.tensor_copy, 0, Y_CHUNK)
+        weave_y(nc.vector.tensor_copy, Y_CHUNK, middle)
+        store_planes(0, Y_CHUNK)
+        weave_y(nc.vector.tensor_copy, middle, Y_SPLIT)
+        for lo, hi in ((Y_CHUNK, middle), (middle, T - Y_CHUNK), (T - Y_CHUNK, T - Y_LAST), (T - Y_LAST, T)):
+            store_planes(lo, hi)
         for q in range(4):
             queue = nc.sync if q % 2 == 0 else nc.scalar
             queue.dma_start(

@@ -126,8 +126,8 @@ def tile_list_gain_drift_rewrite_kernel(
         def weave_w2(g):
             woven = held([P, PACK * GROUP], BF16, "logs%d" % (1 + g))
             nc.scalar.copy(
-                woven[:].rearrange("p (t m j) -> p m t j", t=PACK, j=PACK),
-                w2_raw[g][:].rearrange("p j (m t) -> p m t j", t=PACK),
+                woven[:].rearrange("p (u e m j) -> p m u j e", u=2, e=2, j=PACK),
+                w2_raw[g][:].rearrange("p j (m u e) -> p m u j e", u=2, e=2),
             )
             return woven
 

@@ -28,8 +28,22 @@ DRIFT_BANKS = 2
 Y_SPLIT = 1152
 Y_CHUNK = 512
 Y_LAST = 256
-W3_ROW = 8
-MOVED = 112
+W3_ROW = 4
+LG = K_PASSES
+W2_SPLIT = 64
+SHARED = {
+    "logs1": 4,
+    "logs2": 8,
+    "w2_raw0": 12,
+    "w2_raw1": 20,
+    "w1_raw0": 28,
+    "w1_raw1": 30,
+    "tab0": 32,
+    "h_first_woven1": 40,
+    "lg_late_woven": 42,
+    "lg_woven": 44,
+    "w3_sb": 46,
+}
 
 
 def weave(copy, woven, rows):
@@ -47,15 +61,22 @@ def tile_list_gain_drift_rewrite_kernel(
         keep = ctx.enter_context(tc.tile_pool(name="keep", bufs=1))
         psum = ctx.enter_context(tc.psum_pool(name="psum", bufs=1))
 
+        shared = ctx.enter_context(tc.tile_pool(name="shared", bufs=1))
+        tenants = {}
+
         def held(shape, dtype, name, bufs=1):
+            if name in SHARED:
+                tenants[name] = tenants.get(name, 0) + 1
+                return shared.tile(
+                    shape, dtype, name="%s_%d" % (name, tenants[name]), align_bytes=64, offset=1024 * SHARED[name]
+                )
             return keep.tile(shape, dtype, name=name, align_bytes=64, bufs=bufs)
 
         tab_sc = held([P, T], U8, "tab_sc")
-        w_sc_raw = held([P, H], U8, "w_sc_raw")
-        w_sc_down = held([P, H], U8, "w_sc_down")
+        w_sc_raw = held([P, K_PASSES * H], U8, "w_sc_raw")
         v_planes = held([P, K_PASSES * S], U8, "v_planes")
         nc.gpsimd.memset(w_sc_raw[:].bitcast(I32), 0)
-        for plane in [tab_sc[32:64, :], tab_sc[64:P, :], v_planes[:], w_sc_down[:]]:
+        for plane in [tab_sc[32:64, :], tab_sc[64:P, :], v_planes[:]]:
             nc.vector.memset(plane.bitcast(I32), 0)
         nc.sync.dma_start(tab_sc[0:32, :].bitcast(I32), tab_scales.rearrange("a q c -> q a c").bitcast(I32))
 
@@ -76,13 +97,14 @@ def tile_list_gain_drift_rewrite_kernel(
         def load_w1_scale_rows(quadrants):
             for q in quadrants:
                 nc.sync.dma_start(
-                    w_sc_raw[32 * q : 32 * q + 8, :].bitcast(I32), w1_scales[:, 4 * q : 4 * q + 4, :].bitcast(I32)
+                    w_sc_raw[32 * q : 32 * q + 4, :].bitcast(I32),
+                    w1_scales[:, 4 * q : 4 * q + 4, :].rearrange("a r c -> r a c").bitcast(I32),
                 )
 
         def load_w3_scale_rows(quadrants):
             for q in quadrants:
                 nc.sync.dma_start(
-                    w_sc_raw[32 * q + W3_ROW : 32 * q + W3_ROW + 4, :].bitcast(I32),
+                    w_sc_raw[32 * q + W3_ROW : 32 * q + W3_ROW + 4, 0 : H_GROUPS * N].bitcast(I32),
                     w3_scales[:, 4 * q : 4 * q + 4, :].rearrange("a r c -> r a c").bitcast(I32),
                 )
 
@@ -93,29 +115,36 @@ def tile_list_gain_drift_rewrite_kernel(
             tab.append(held([P, T], I32, name))
             nc.sync.dma_start(tab[a][:], tab_words[a].rearrange("p c i -> p (c i)").bitcast(I32))
 
+        def picks(first, count):
+            return offsets[:, first // 16 : (first + count) // 16]
+
         load_page(0)
-        nc.sync.dma_start(lv_sb[:], lv.rearrange("(p t) -> p t", t=PACK))
-        nc.sync.dma_start(b_sb[:], b.rearrange("(g p t) -> p g t", p=P, t=PACK))
+        load_w1_scale_rows(range(4))
         load_page(1)
-        load_w1_scale_rows(range(0, 3))
+        nc.sync.dma_start(lv_sb[:], lv.rearrange("(p t) -> p t", t=PACK))
+        load_w3_scale_rows(range(4))
         load_page(2)
-        load_w1_scale_rows(range(3, 4))
-        load_w3_scale_rows(range(0, 2))
         load_page(3)
-        load_w3_scale_rows(range(2, 4))
+        v_sc = held([P, S], U8, "v_sc")
+        nc.vector.tensor_copy(v_sc[:], tab_sc[:].indirect(offsets[:]))
+        for q in range(4):
+            nc.sync.dma_start(v_planes[32 * q : 32 * q + 4, :].bitcast(I32), v_sc[8 * q : 8 * q + 8, :].bitcast(I32))
         load_tab(0, "tab0")
+        nc.sync.dma_start(b_sb[:], b.rearrange("(g p t) -> p g t", p=P, t=PACK))
         for a in range(K_PASSES):
             nc.sync.dma_start(w1_raw[a][:].bitcast(I32), w1_words[a].bitcast(I32))
         load_w2(0)
         load_w2(1)
+        load_tab(1, "tab1")
+        w3_raw = held([P, H_GROUPS, N], I32, "w3_raw")
+        nc.sync.dma_start(w3_raw[:], w3_words.rearrange("a p c i -> p a (c i)").bitcast(I32))
 
-        def picks(first, count):
-            return offsets[:, first // 16 : (first + count) // 16]
-
-        v_sc = held([P, S], U8, "v_sc")
-        nc.vector.tensor_copy(v_sc[:], tab_sc[:].indirect(offsets[:]))
-        for q in range(4):
-            nc.gpsimd.dma_start(v_planes[32 * q : 32 * q + 4, :].bitcast(I32), v_sc[8 * q : 8 * q + 8, :].bitcast(I32))
+        w_sc = held([P, K_PASSES * H], U8, "w_sc")
+        for a in reversed(range(K_PASSES)):
+            nc.gpsimd.tensor_copy(
+                w_sc[:, a * H : (a + 1) * H].rearrange("p (g t m) -> p g t m", t=PACK, m=P),
+                w_sc_raw[:, a * H : (a + 1) * H].rearrange("p (g m t) -> p g t m", t=PACK, m=P),
+            )
 
         def quantize(woven, codes_name, scales_name):
             codes = held([P, woven.shape[1] // PACK], U32, codes_name)
@@ -123,61 +152,40 @@ def tile_list_gain_drift_rewrite_kernel(
             nc.vector.quantize_mx(codes[:].bitcast(FP8X4), scales[:], woven[:])
             return codes, scales
 
-        def weave_w2(g):
-            woven = held([P, PACK * GROUP], BF16, "logs%d" % (1 + g))
-            nc.scalar.copy(
-                woven[:].rearrange("p (u e m j) -> p m u j e", u=2, e=2, j=PACK),
-                w2_raw[g][:].rearrange("p j (m u e) -> p m u j e", u=2, e=2),
-            )
+        def weave_w2(g, name, shares):
+            woven = held([P, PACK * GROUP], BF16, name)
+            dealt = woven[:].rearrange("p (u e m j) -> p m u j e", u=2, e=2, j=PACK)
+            rows = w2_raw[g][:].rearrange("p j (m u e) -> p m u j e", u=2, e=2)
+            for copy, lo, hi in shares:
+                copy(dealt[:, lo:hi], rows[:, lo:hi])
             return woven
 
-        def gather_words(a, first, count, name):
-            words = held([P, count], U32, name)
-            nc.vector.tensor_copy(words[:], tab[a][:].bitcast(U32).indirect(picks(first, count)))
-            return [(words, c * CHUNK) for c in range(count // CHUNK)]
+        def gather_words(a, pieces, name):
+            words = held([P, S], U32, name)
+            for lo, hi in pieces:
+                nc.vector.tensor_copy(words[:, lo:hi], tab[a][:].bitcast(U32).indirect(picks(lo, hi - lo)))
+            return words
 
         gains = [held([P, S], F32, "gains%d" % t) for t in range(PACK)]
-        lg_rows = held([P, PACK, S], BF16, "lg_rows")
+        lg_pairs = held([P, 2, S, 2], BF16, "lg_pairs")
+
         def log_gains(t, first, count, name):
             span = slice(first, first + count)
             nc.vector.tensor_copy(gains[t][:, span], pages[t][:].indirect(picks(first, count)))
             logs = held([P, count], F32, name)
             nc.scalar.activation(logs[:], gains[t][:, span], ACT.Ln)
-            nc.gpsimd.tensor_scalar(lg_rows[:, t, span], logs[:], lv_sb[:, t : t + 1], 0.0, ALU.mult, ALU.add)
+            nc.gpsimd.tensor_scalar(lg_pairs[:, t // 2, span, t % 2], logs[:], lv_sb[:, t : t + 1], 0.0, ALU.mult, ALU.add)
             return logs
 
-        def weave_lg_on_gpsimd(first, count, name):
-            woven = held([P, PACK * count], BF16, name)
-            nc.gpsimd.tensor_scalar(
-                woven[:].rearrange("p (c t) -> p c t", t=PACK),
-                lg_rows[:, :, first : first + count].rearrange("p t c -> p c t"),
-                1.0,
-                0.0,
-                ALU.mult,
-                ALU.add,
-            )
-            return woven
-
         for t in range(PACK - 1):
-            log_gains(t, 0, S, "logs%d" % (t % 2))
-        w_sc = held([P, H], U8, "w_sc")
-        nc.vector.tensor_copy(
-            w_sc[:].rearrange("p (g t m) -> p g t m", t=PACK, m=P),
-            w_sc_raw[:].rearrange("p (g m t) -> p g t m", t=PACK, m=P),
-        )
-        nc.sync.dma_start(w_sc_down[0:MOVED, :].bitcast(I32), w_sc[4 : 4 + MOVED, :].bitcast(I32))
-        load_tab(1, "w_sc_raw")
-        w3_raw = held([P, H_GROUPS, N], I32, "logs0")
-        nc.sync.dma_start(w3_raw[:], w3_words.rearrange("a p c i -> p a (c i)").bitcast(I32))
-        w1_planes = [w_sc, w_sc_down]
+            log_gains(t, 0, S, "page_logs%d" % t)
         neg_b = held([P, H_GROUPS, PACK], F32, "neg_b")
         log_gains(PACK - 1, 0, 2 * CHUNK, "logs1")
-        second_woven = weave_lg_on_gpsimd(CHUNK, CHUNK, "lg_woven1")
         logs = log_gains(PACK - 1, 2 * CHUNK, 2 * CHUNK, "logs2")
         nc.gpsimd.tensor_scalar(neg_b[:], b_sb[:], -1.0, 0.0, ALU.mult, ALU.add)
         exp_warm = held([P, 1], F32, "exp_warm")
         nc.scalar.activation(exp_warm[:], logs[:, 0:1], ACT.Exp, scale=0.0)
-        v_words = [gather_words(0, 0, S, "v0"), []]
+        v_words = [gather_words(0, [(0, S)], "v0")]
         w1_sb = held([P, K_PASSES, 2 * H], U8, "tab0")
         for a in range(K_PASSES):
             nc.vector.tensor_copy(
@@ -185,30 +193,37 @@ def tile_list_gain_drift_rewrite_kernel(
                 w1_raw[a][:].bitcast(U16).rearrange("p (g m t) -> p g t m", t=PACK, m=P),
             )
 
-        def weave_lg(copy, c, name):
-            woven = held([P, PACK * CHUNK], BF16, name)
-            weave(copy, woven[:], lg_rows[:, :, c * CHUNK : (c + 1) * CHUNK])
+        lg_words = lg_pairs[:].rearrange("p u c e -> p u (c e)").bitcast(F32)
+
+        def weave_lg(half, name):
+            woven = held([P, PACK * 2 * CHUNK], BF16, name)
+            nc.gpsimd.tensor_copy(
+                woven[:].bitcast(F32).rearrange("p (c i u) -> p c u i", i=2, u=2),
+                lg_words[:, :, half * 2 * CHUNK : (half + 1) * 2 * CHUNK].rearrange("p u (c i) -> p c u i", i=2),
+            )
             return woven
 
-        def quantize_lg(c, woven, name):
-            return quantize(woven, name, "lg_scales%d" % c) + (0,)
+        lg_early = quantize(weave_lg(0, "lg_woven"), "w1_raw0", "lg_scales0")
+        lg_mx = [lg_early + (0,), lg_early + (CHUNK,)]
+        w2_mx = [quantize(weave_w2(0, "logs1", [(nc.scalar.copy, 0, P)]), "w1_raw1", "w2_scales0")]
+        late_w2 = weave_w2(1, "lg_woven", [(nc.scalar.copy, 0, W2_SPLIT), (nc.vector.tensor_copy, W2_SPLIT, P)])
+        w2_mx.append(quantize(late_w2, "w2_codes1", "w2_scales1"))
+        v_words.append(gather_words(1, [(0, CHUNK), (CHUNK, S)], "w2_raw1"))
+        late_woven = weave_lg(1, "lg_late_woven")
+        w3_sb = held([P, H_GROUPS * N], I32, "w3_sb")
+        nc.gpsimd.tensor_copy(
+            w3_sb[:].rearrange("p (a t m) -> p a t m", t=PACK, m=P),
+            w3_raw[:].rearrange("p a (m t) -> p a t m", t=PACK),
+        )
 
-        w2_mx = [quantize(weave_w2(0), "w2_codes0", "w2_scales0")]
-        lg_second = quantize_lg(1, second_woven, "logs1")
-        lg_mx = [quantize_lg(0, weave_lg(nc.scalar.copy, 0, "w2_raw0"), "lg_codes0"), lg_second]
-        late_woven = weave_lg_on_gpsimd(2 * CHUNK, 2 * CHUNK, "w2_raw0")
-        v_words[1].extend(gather_words(1, 0, CHUNK, "v1_first"))
-        v_words[1].extend(gather_words(1, CHUNK, S - CHUNK, "v1_rest"))
-        w2_mx.append(quantize(weave_w2(1), "w2_codes1", "w2_scales1"))
-
-        def first_sums(c, g, pair, w2_at):
+        def first_sums(c, g, pair, order):
             bank = psum.tile([P, 2 * CHUNK], F32, name="sums", bufs=SUM_BANKS)
             passes = []
-            for step in range(K_PASSES + 1):
+            for a in order:
                 for u in range(2):
                     t = 2 * pair + u
                     acc = bank[:, u * CHUNK : (u + 1) * CHUNK]
-                    if step == w2_at:
+                    if a == LG:
                         codes, scales, at = lg_mx[c]
                         w_cols = slice(t * P, (t + 1) * P)
                         passes.append(
@@ -221,20 +236,17 @@ def tile_list_gain_drift_rewrite_kernel(
                             )
                         )
                         continue
-                    a = step if step < w2_at else step - 1
-                    words, at = v_words[a][c]
                     w_col = g * GROUP + t * P
-                    for n0 in range(0, CHUNK, P):
-                        v_col = a * S + c * CHUNK + n0
-                        passes.append(
-                            (
-                                acc[:, n0 : n0 + P],
-                                w1_sb[:, a, 2 * w_col : 2 * (w_col + P)].bitcast(FP4X4),
-                                w1_planes[a][:, w_col : w_col + P],
-                                words[:, at + n0 : at + n0 + P].bitcast(FP8X4),
-                                v_planes[:, v_col : v_col + P],
-                            )
+                    v_col = a * S + c * CHUNK
+                    passes.append(
+                        (
+                            acc,
+                            w1_sb[:, a, 2 * w_col : 2 * (w_col + P)].bitcast(FP4X4),
+                            w_sc[:, a * H + w_col : a * H + w_col + P],
+                            v_words[a][:, c * CHUNK : (c + 1) * CHUNK].bitcast(FP8X4),
+                            v_planes[:, v_col : v_col + CHUNK],
                         )
+                    )
             for i, (acc, lhsT, lhsT_scale, rhs, rhs_scale) in enumerate(passes):
                 nc.tensor.matmul_mx(
                     acc,
@@ -247,20 +259,27 @@ def tile_list_gain_drift_rewrite_kernel(
                 )
             return bank
 
-        def relu_rows(c, g, rows, w2_at):
+        def relu_rows(c, g, rows, order):
             for pair in range(2):
-                bank = first_sums(c, g, pair, w2_at)
+                bank = first_sums(c, g, pair, order)
                 for u in range(2):
                     t = 2 * pair + u
                     acc = bank[:, u * CHUNK : (u + 1) * CHUNK]
                     nc.scalar.activation(rows[:, t, :], acc, ACT.Relu, bias=neg_b[:, g, t : t + 1])
 
         def hidden(c):
-            rows = held([P, PACK, H_GROUPS * CHUNK], BF16, "h_rows%d" % c)
-            for g in range(H_GROUPS):
-                relu_rows(c, g, rows[:, :, g * CHUNK : (g + 1) * CHUNK], 0)
-            woven = held([P, PACK * H_GROUPS * CHUNK], BF16, "h_first_codes" if c == 1 else "h_woven%d" % (c % 2))
-            weave(nc.scalar.copy, woven[:], rows[:])
+            woven = held([P, PACK * H_GROUPS * CHUNK], BF16, "h_first_codes1" if c == 1 else "h_woven%d" % (c % 2))
+            if c == 1:
+                parts = [held([P, PACK, CHUNK], BF16, name) for name in ("h_rows1", "lg_late_woven")]
+                for g in range(H_GROUPS):
+                    relu_rows(c, g, parts[g][:], (LG, 0, 1))
+                for g in range(H_GROUPS):
+                    weave(nc.scalar.copy, woven[:, g * PACK * CHUNK : (g + 1) * PACK * CHUNK], parts[g][:])
+            else:
+                rows = held([P, PACK, H_GROUPS * CHUNK], BF16, "h_rows%d" % c)
+                for g in range(H_GROUPS):
+                    relu_rows(c, g, rows[:, :, g * CHUNK : (g + 1) * CHUNK], (LG, 0, 1))
+                weave(nc.scalar.copy, woven[:], rows[:])
             codes, scales = quantize(woven, "h_codes%d" % (c % 2), "h_scales%d" % (c % 2))
             return [(codes, scales, g * CHUNK) for g in range(H_GROUPS)]
 
@@ -285,20 +304,14 @@ def tile_list_gain_drift_rewrite_kernel(
                 pages[t][:].indirect(picks(first, count)), gains[t][:, first : first + count], factor, ALU.mult
             )
 
-        woven = held([P, H_GROUPS, PACK * CHUNK], BF16, "h_first_woven")
+        h_mx = []
         for g in range(H_GROUPS):
             rows = held([P, PACK, CHUNK], BF16, "h_first_rows%d" % g)
-            relu_rows(0, g, rows[:], 1 + g)
-            weave(nc.vector.tensor_copy, woven[:, g, :], rows[:])
-            if g == 0:
-                w3_sb = held([P, H_GROUPS * N], I32, "h_first_rows0")
-                nc.vector.tensor_copy(
-                    w3_sb[:].rearrange("p (a t m) -> p a m t", t=PACK, m=P),
-                    w3_raw[:].rearrange("p a (m t) -> p a m t", t=PACK),
-                )
-        codes, scales = quantize(woven[:].rearrange("p g c -> p (g c)"), "h_first_codes", "h_first_scales")
-        h_mx = [(codes, scales, g * CHUNK) for g in range(H_GROUPS)]
-        lg_late = quantize(late_woven, "h_first_woven", "lg_scales2")
+            relu_rows(0, g, rows[:], (0, LG, 1))
+            woven = held([P, PACK * CHUNK], BF16, "h_first_woven%d" % g)
+            weave(nc.vector.tensor_copy, woven[:], rows[:])
+            h_mx.append(quantize(woven, "h_first_codes%d" % g, "h_first_scales%d" % g) + (0,))
+        lg_late = quantize(late_woven, "h_first_woven1", "lg_scales1")
         lg_mx.extend([lg_late + (0,), lg_late + (CHUNK,)])
 
         out_dealt = out_0.rearrange("(p t) c -> t p c", t=PACK)
@@ -339,7 +352,7 @@ def tile_list_gain_drift_rewrite_kernel(
         finish(2)
         rewrite(last, first - CHUNK, 2 * CHUNK, late[:, 1, :])
         finish(last)
-        y_woven = held([P, PACK * T], BF16, "w_sc_raw")
+        y_woven = held([P, PACK * T], BF16, "tab1")
         y_scales = held([P, Y_CHUNK], U8, "y_scales")
         words_out = out_1[0].rearrange("p m t -> p (m t)").bitcast(I32)
         y_woven_at = lambda lo, hi: y_woven[:, PACK * lo : PACK * hi]

@@ -94,19 +94,10 @@ def tile_list_gain_drift_rewrite_kernel(
         def load_page(t):
             nc.sync.dma_start(pages[t][:], gT_dealt[t])
 
-        def load_w1_scale_rows(quadrants):
-            for q in quadrants:
-                nc.sync.dma_start(
-                    w_sc_raw[32 * q : 32 * q + 4, :].bitcast(I32),
-                    w1_scales[:, 4 * q : 4 * q + 4, :].rearrange("a r c -> r a c").bitcast(I32),
-                )
-
-        def load_w3_scale_rows(quadrants):
-            for q in quadrants:
-                nc.sync.dma_start(
-                    w_sc_raw[32 * q + W3_ROW : 32 * q + W3_ROW + 4, 0 : H_GROUPS * N].bitcast(I32),
-                    w3_scales[:, 4 * q : 4 * q + 4, :].rearrange("a r c -> r a c").bitcast(I32),
-                )
+        def load_scale_rows(scales, row, width):
+            by_row = scales.rearrange("a (q r) c -> r q a c", r=4).bitcast(I32)
+            for r in range(4):
+                nc.sync.dma_start(w_sc_raw[row + r : P : 32, 0:width].bitcast(I32), by_row[r])
 
         def load_w2(g):
             nc.sync.dma_start(w2_raw[g][:], w2_dealt[:, :, g * GROUP : (g + 1) * GROUP])
@@ -118,23 +109,35 @@ def tile_list_gain_drift_rewrite_kernel(
         def picks(first, count):
             return offsets[:, first // 16 : (first + count) // 16]
 
-        load_page(0)
-        load_w1_scale_rows(range(4))
-        load_page(1)
-        nc.sync.dma_start(lv_sb[:], lv.rearrange("(p t) -> p t", t=PACK))
-        load_w3_scale_rows(range(4))
-        load_page(2)
-        load_page(3)
         v_sc = held([P, S], U8, "v_sc")
         nc.vector.tensor_copy(v_sc[:], tab_sc[:].indirect(offsets[:]))
-        for q in range(4):
-            nc.sync.dma_start(v_planes[32 * q : 32 * q + 4, :].bitcast(I32), v_sc[8 * q : 8 * q + 8, :].bitcast(I32))
-        load_tab(0, "tab0")
-        nc.sync.dma_start(b_sb[:], b.rearrange("(g p t) -> p g t", p=P, t=PACK))
-        for a in range(K_PASSES):
+
+        def move_planes(r):
+            for a in range(K_PASSES):
+                nc.sync.dma_start(
+                    v_planes[r:P:32, a * S : (a + 1) * S].bitcast(I32), v_sc[2 * r + a : 32 : 8, :].bitcast(I32)
+                )
+
+        def load_w1(a):
             nc.sync.dma_start(w1_raw[a][:].bitcast(I32), w1_words[a].bitcast(I32))
+
+        load_page(0)
+        load_scale_rows(w1_scales, 0, K_PASSES * H)
+        load_page(1)
+        nc.sync.dma_start(lv_sb[:], lv.rearrange("(p t) -> p t", t=PACK))
+        load_scale_rows(w3_scales, W3_ROW, H_GROUPS * N)
+        load_page(2)
+        move_planes(0)
+        load_page(3)
+        move_planes(1)
+        move_planes(2)
+        load_tab(0, "tab0")
+        move_planes(3)
+        load_w1(0)
+        load_w1(1)
         load_w2(0)
         load_w2(1)
+        nc.sync.dma_start(b_sb[:], b.rearrange("(g p t) -> p g t", p=P, t=PACK))
         load_tab(1, "tab1")
         w3_raw = held([P, H_GROUPS, N], I32, "w3_raw")
         nc.sync.dma_start(w3_raw[:], w3_words.rearrange("a p c i -> p a (c i)").bitcast(I32))

@@ -275,7 +275,7 @@ def tile_list_gain_drift_rewrite_kernel(
             if c == 1:
                 parts = [held([P, PACK, CHUNK], BF16, name) for name in ("h_rows1", "lg_late_woven")]
                 for g in range(H_GROUPS):
-                    relu_rows(c, g, parts[g][:], (LG, 0, 1))
+                    relu_rows(c, g, parts[g][:], (0, LG, 1))
                 for g in range(H_GROUPS):
                     weave(nc.scalar.copy, woven[:, g * PACK * CHUNK : (g + 1) * PACK * CHUNK], parts[g][:])
             else:
@@ -283,16 +283,15 @@ def tile_list_gain_drift_rewrite_kernel(
                 for g in range(H_GROUPS):
                     relu_rows(c, g, rows[:, :, g * CHUNK : (g + 1) * CHUNK], (LG, 0, 1))
                 weave(nc.scalar.copy, woven[:], rows[:])
-            codes, scales = quantize(woven, "h_codes%d" % (c % 2), "h_scales%d" % (c % 2))
+            codes, scales = quantize(woven, "h_codes%d" % c, "h_scales%d" % c)
             return [(codes, scales, g * CHUNK) for g in range(H_GROUPS)]
 
-        def drift_factor(t, h_mx):
-            bank = psum.tile([P, CHUNK], F32, name="drift", bufs=DRIFT_BANKS)
+        def drift(acc, t, h_chunk):
             for a in range(H_GROUPS):
-                codes, scales, at = h_mx[a]
+                codes, scales, at = h_chunk[a]
                 c0 = a * N + t * P
                 nc.tensor.matmul_mx(
-                    bank[:],
+                    acc,
                     lhsT=w3_sb[:, c0 : c0 + P].bitcast(FP8X4),
                     lhsT_scale=w_sc[W3_ROW:P, c0 : c0 + P],
                     rhs=codes[:, at : at + CHUNK].bitcast(FP8X4),
@@ -300,61 +299,56 @@ def tile_list_gain_drift_rewrite_kernel(
                     start=(a == 0),
                     stop=(a == H_GROUPS - 1),
                 )
-            return bank
 
         def rewrite(t, first, count, factor):
             nc.vector.tensor_tensor(
                 pages[t][:].indirect(picks(first, count)), gains[t][:, first : first + count], factor, ALU.mult
             )
 
-        h_mx = []
+        h_first = []
         for g in range(H_GROUPS):
             rows = held([P, PACK, CHUNK], BF16, "h_first_rows%d" % g)
             relu_rows(0, g, rows[:], (0, LG, 1))
             woven = held([P, PACK * CHUNK], BF16, "h_first_woven%d" % g)
             weave(nc.vector.tensor_copy, woven[:], rows[:])
-            h_mx.append(quantize(woven, "h_first_codes%d" % g, "h_first_scales%d" % g) + (0,))
+            h_first.append(quantize(woven, "h_first_codes%d" % g, "h_first_scales%d" % g) + (0,))
         lg_late = quantize(late_woven, "h_first_woven1", "lg_scales1")
         lg_mx.extend([lg_late + (0,), lg_late + (CHUNK,)])
 
         out_dealt = out_0.rearrange("(p t) c -> t p c", t=PACK)
         last = PACK - 1
 
+        def drift_bank(t, chunks):
+            bank = psum.tile([P, len(chunks) * CHUNK], F32, name="drift", bufs=DRIFT_BANKS)
+            for i in reversed(range(len(chunks))):
+                drift(bank[:, i * CHUNK : (i + 1) * CHUNK], t, h_mx[chunks[i]])
+            return bank
+
+        def update(t, chunks, bank, name):
+            factor = held([P, len(chunks) * CHUNK], F32, name)
+            nc.scalar.activation(factor[:], bank[:], ACT.Exp)
+            rewrite(t, chunks[0] * CHUNK, len(chunks) * CHUNK, factor[:])
+
+        h_mx = [h_first]
+        waiting = [(last, 0), (2, 1), (last, 1)]
+        for c in range(CHUNKS - 1):
+            for t in range(3 if c == 0 else 2):
+                update(t, [c], drift_bank(t, [c]), "factor%d_%d" % (t, c % 2))
+            t, older = waiting[c]
+            held_back = drift_bank(t, [older])
+            h_mx.append(hidden(c + 1))
+            update(t, [older], held_back, "h_rows%d" % (c + 1))
+
         def finish(t):
             nc.sync.dma_start(out_dealt[t], pages[t][:])
             if t < last:
                 nc.scalar.copy(y_rows[:, t, :], pages[t][:])
 
-        for c in range(CHUNKS - 1):
-            first = c * CHUNK
-            at_once = 3 if c == 0 else 2
-            early = held([P, last, CHUNK], F32, "early", bufs=2)
-            for t in range(at_once):
-                nc.scalar.activation(early[:, t, :], drift_factor(t, h_mx)[:], ACT.Exp)
-                rewrite(t, first, CHUNK, early[:, t, :])
-            banks = {t: drift_factor(t, h_mx) for t in range(at_once, PACK)}
-            h_mx = hidden(c + 1)
-            late = held([P, 2, 2 * CHUNK], F32, "h_rows%d" % (c + 1))
-            for t in banks:
-                nc.scalar.activation(late[:, t - 2, 0:CHUNK], banks[t][:], ACT.Exp)
-            for t in banks:
-                if t < last or c < CHUNKS - 2:
-                    rewrite(t, first, CHUNK, late[:, t - 2, 0:CHUNK])
-
-        first = S - CHUNK
-        early = held([P, last, CHUNK], F32, "early", bufs=2)
-        for t in range(2):
-            nc.scalar.activation(early[:, t, :], drift_factor(t, h_mx)[:], ACT.Exp)
-        for u in range(2):
-            nc.scalar.activation(late[:, u, CHUNK : 2 * CHUNK], drift_factor(2 + u, h_mx)[:], ACT.Exp)
-        y_rows = held([P, PACK, T], BF16, "h_codes1")
-        for t in range(2):
-            rewrite(t, first, CHUNK, early[:, t, :])
+        for t, chunks in ((0, [3]), (1, [3]), (2, [2, 3]), (last, [2, 3])):
+            update(t, chunks, drift_bank(t, chunks), "factor%d_1" % t)
+        y_rows = held([P, PACK, T], BF16, "h_codes3")
+        for t in range(PACK):
             finish(t)
-        rewrite(2, first, CHUNK, late[:, 0, CHUNK : 2 * CHUNK])
-        finish(2)
-        rewrite(last, first - CHUNK, 2 * CHUNK, late[:, 1, :])
-        finish(last)
         y_woven = held([P, PACK * T], BF16, "tab1")
         y_scales = held([P, Y_CHUNK], U8, "y_scales")
         words_out = out_1[0].rearrange("p m t -> p (m t)").bitcast(I32)

@@ -28,7 +28,6 @@ DRIFT_BANKS = 2
 Y_SPLIT = 1152
 Y_CHUNK = 512
 Y_LAST = 256
-W3_ROW = 4
 LG = K_PASSES
 W2_SPLIT = 64
 SHARED = {
@@ -42,7 +41,8 @@ SHARED = {
     "h_first_woven1": 40,
     "lg_late_woven": 42,
     "lg_woven": 44,
-    "w3_sb": 46,
+    "w3_sc": 46,
+    "lg_pairs": 48,
 }
 
 
@@ -73,9 +73,11 @@ def tile_list_gain_drift_rewrite_kernel(
             return keep.tile(shape, dtype, name=name, align_bytes=64, bufs=bufs)
 
         tab_sc = held([P, T], U8, "tab_sc")
-        w_sc_raw = held([P, K_PASSES * H], U8, "w_sc_raw")
+        w1_sc_raw = held([P, K_PASSES * H], U8, "w1_sc_raw")
+        w3_sc_raw = held([P, H_GROUPS * N], U8, "w3_sc_raw")
         v_planes = held([P, K_PASSES * S], U8, "v_planes")
-        nc.gpsimd.memset(w_sc_raw[:].bitcast(I32), 0)
+        for plane in [w1_sc_raw, w3_sc_raw]:
+            nc.gpsimd.memset(plane[:].bitcast(I32), 0)
         for plane in [tab_sc[32:64, :], tab_sc[64:P, :], v_planes[:]]:
             nc.vector.memset(plane.bitcast(I32), 0)
         nc.sync.dma_start(tab_sc[0:32, :].bitcast(I32), tab_scales.rearrange("a q c -> q a c").bitcast(I32))
@@ -94,10 +96,10 @@ def tile_list_gain_drift_rewrite_kernel(
         def load_page(t):
             nc.sync.dma_start(pages[t][:], gT_dealt[t])
 
-        def load_scale_rows(scales, row, width):
+        def load_scale_rows(raw, scales):
             by_row = scales.rearrange("a (q r) c -> r q a c", r=4).bitcast(I32)
             for r in range(4):
-                nc.sync.dma_start(w_sc_raw[row + r : P : 32, 0:width].bitcast(I32), by_row[r])
+                nc.sync.dma_start(raw[r:P:32, :].bitcast(I32), by_row[r])
 
         def load_w2(g):
             nc.sync.dma_start(w2_raw[g][:], w2_dealt[:, :, g * GROUP : (g + 1) * GROUP])
@@ -122,10 +124,9 @@ def tile_list_gain_drift_rewrite_kernel(
             nc.sync.dma_start(w1_raw[a][:].bitcast(I32), w1_words[a].bitcast(I32))
 
         load_page(0)
-        load_scale_rows(w1_scales, 0, K_PASSES * H)
+        load_scale_rows(w1_sc_raw, w1_scales)
         load_page(1)
         nc.sync.dma_start(lv_sb[:], lv.rearrange("(p t) -> p t", t=PACK))
-        load_scale_rows(w3_scales, W3_ROW, H_GROUPS * N)
         load_page(2)
         move_planes(0)
         load_page(3)
@@ -139,15 +140,19 @@ def tile_list_gain_drift_rewrite_kernel(
         load_w2(1)
         nc.sync.dma_start(b_sb[:], b.rearrange("(g p t) -> p g t", p=P, t=PACK))
         load_tab(1, "tab1")
+        load_scale_rows(w3_sc_raw, w3_scales)
         w3_raw = held([P, H_GROUPS, N], I32, "w3_raw")
         nc.sync.dma_start(w3_raw[:], w3_words.rearrange("a p c i -> p a (c i)").bitcast(I32))
 
-        w_sc = held([P, K_PASSES * H], U8, "w_sc")
-        for a in reversed(range(K_PASSES)):
+        def deal_scales(raw, name):
+            dealt = held(raw.shape, U8, name)
             nc.gpsimd.tensor_copy(
-                w_sc[:, a * H : (a + 1) * H].rearrange("p (g t m) -> p g t m", t=PACK, m=P),
-                w_sc_raw[:, a * H : (a + 1) * H].rearrange("p (g m t) -> p g t m", t=PACK, m=P),
+                dealt[:].rearrange("p (g t m) -> p g t m", t=PACK, m=P),
+                raw[:].rearrange("p (g m t) -> p g t m", t=PACK, m=P),
             )
+            return dealt
+
+        w1_sc = deal_scales(w1_sc_raw, "w1_sc")
 
         def quantize(woven, codes_name, scales_name):
             codes = held([P, woven.shape[1] // PACK], U32, codes_name)
@@ -213,10 +218,11 @@ def tile_list_gain_drift_rewrite_kernel(
         w2_mx.append(quantize(late_w2, "w2_codes1", "w2_scales1"))
         v_words.append(gather_words(1, [(0, CHUNK), (CHUNK, S)], "w2_raw1"))
         late_woven = weave_lg(1, "lg_late_woven")
-        w3_sb = held([P, H_GROUPS * N], I32, "w3_sb")
-        nc.gpsimd.tensor_copy(
-            w3_sb[:].rearrange("p (a t m) -> p a t m", t=PACK, m=P),
-            w3_raw[:].rearrange("p a (m t) -> p a t m", t=PACK),
+        w3_sc = deal_scales(w3_sc_raw, "w3_sc")
+        w3_sb = held([P, H_GROUPS * N], I32, "lg_pairs")
+        nc.vector.tensor_copy(
+            w3_sb[:].rearrange("p (a t m) -> p a m t", t=PACK, m=P),
+            w3_raw[:].rearrange("p a (m t) -> p a m t", t=PACK),
         )
 
         def first_sums(c, g, pair, order):
@@ -245,7 +251,7 @@ def tile_list_gain_drift_rewrite_kernel(
                         (
                             acc,
                             w1_sb[:, a, 2 * w_col : 2 * (w_col + P)].bitcast(FP4X4),
-                            w_sc[:, a * H + w_col : a * H + w_col + P],
+                            w1_sc[:, a * H + w_col : a * H + w_col + P],
                             v_words[a][:, c * CHUNK : (c + 1) * CHUNK].bitcast(FP8X4),
                             v_planes[:, v_col : v_col + CHUNK],
                         )
@@ -293,7 +299,7 @@ def tile_list_gain_drift_rewrite_kernel(
                 nc.tensor.matmul_mx(
                     acc,
                     lhsT=w3_sb[:, c0 : c0 + P].bitcast(FP8X4),
-                    lhsT_scale=w_sc[W3_ROW:P, c0 : c0 + P],
+                    lhsT_scale=w3_sc[:, c0 : c0 + P],
                     rhs=codes[:, at : at + CHUNK].bitcast(FP8X4),
                     rhs_scale=scales[:, at : at + CHUNK],
                     start=(a == 0),

@@ -29,20 +29,20 @@ Y_SPLIT = 1152
 Y_CHUNK = 512
 Y_LAST = 256
 LG = K_PASSES
-W2_SPLIT = 64
+W2_SPLIT = 80
 SHARED = {
     "logs1": 4,
     "logs2": 8,
     "w2_raw0": 12,
     "w2_raw1": 20,
-    "w1_raw0": 28,
+    "w1_raw0": 47,
     "w1_raw1": 30,
     "tab0": 32,
     "h_first_woven1": 40,
-    "lg_late_woven": 42,
+    "lg_late_woven": 24,
     "lg_woven": 44,
     "w3_sc": 46,
-    "lg_pairs": 48,
+    "lg_pairs": 49,
 }
 
 
@@ -194,30 +194,35 @@ def tile_list_gain_drift_rewrite_kernel(
         exp_warm = held([P, 1], F32, "exp_warm")
         nc.scalar.activation(exp_warm[:], logs[:, 0:1], ACT.Exp, scale=0.0)
         v_words = [gather_words(0, [(0, S)], "v0")]
-        w1_sb = held([P, K_PASSES, 2 * H], U8, "tab0")
-        for a in range(K_PASSES):
+
+        def deal_w1(a, name):
+            dealt = held([P, 2 * H], U8, name)
             nc.vector.tensor_copy(
-                w1_sb[:, a, :].bitcast(U16).rearrange("p (g t m) -> p g t m", t=PACK, m=P),
+                dealt[:].bitcast(U16).rearrange("p (g t m) -> p g t m", t=PACK, m=P),
                 w1_raw[a][:].bitcast(U16).rearrange("p (g m t) -> p g t m", t=PACK, m=P),
             )
+            return dealt
 
         lg_words = lg_pairs[:].rearrange("p u c e -> p u (c e)").bitcast(F32)
 
-        def weave_lg(half, name):
+        def weave_lg(copy, half, name):
             woven = held([P, PACK * 2 * CHUNK], BF16, name)
-            nc.gpsimd.tensor_copy(
+            copy(
                 woven[:].bitcast(F32).rearrange("p (c i u) -> p c u i", i=2, u=2),
                 lg_words[:, :, half * 2 * CHUNK : (half + 1) * 2 * CHUNK].rearrange("p u (c i) -> p c u i", i=2),
             )
             return woven
 
-        lg_early = quantize(weave_lg(0, "lg_woven"), "w1_raw0", "lg_scales0")
+        w1_sb = [deal_w1(0, "tab0")]
+        early_woven = weave_lg(nc.vector.tensor_copy, 0, "lg_woven")
+        w1_sb.append(deal_w1(1, "logs2"))
+        lg_early = quantize(early_woven, "lg_codes0", "lg_scales0")
         lg_mx = [lg_early + (0,), lg_early + (CHUNK,)]
         w2_mx = [quantize(weave_w2(0, "logs1", [(nc.scalar.copy, 0, P)]), "w1_raw1", "w2_scales0")]
         late_w2 = weave_w2(1, "lg_woven", [(nc.scalar.copy, 0, W2_SPLIT), (nc.vector.tensor_copy, W2_SPLIT, P)])
         w2_mx.append(quantize(late_w2, "w2_codes1", "w2_scales1"))
         v_words.append(gather_words(1, [(0, CHUNK), (CHUNK, S)], "w2_raw1"))
-        late_woven = weave_lg(1, "lg_late_woven")
+        late_woven = weave_lg(nc.scalar.copy, 1, "lg_late_woven")
         w3_sc = deal_scales(w3_sc_raw, "w3_sc")
         w3_sb = held([P, H_GROUPS * N], I32, "lg_pairs")
         nc.vector.tensor_copy(
@@ -250,7 +255,7 @@ def tile_list_gain_drift_rewrite_kernel(
                     passes.append(
                         (
                             acc,
-                            w1_sb[:, a, 2 * w_col : 2 * (w_col + P)].bitcast(FP4X4),
+                            w1_sb[a][:, 2 * w_col : 2 * (w_col + P)].bitcast(FP4X4),
                             w1_sc[:, a * H + w_col : a * H + w_col + P],
                             v_words[a][:, c * CHUNK : (c + 1) * CHUNK].bitcast(FP8X4),
                             v_planes[:, v_col : v_col + CHUNK],

@@ -31,18 +31,20 @@ Y_LAST = 256
 LG = K_PASSES
 W2_SPLIT = 80
 SHARED = {
-    "logs1": 4,
-    "logs2": 8,
-    "w2_raw0": 12,
-    "w2_raw1": 20,
-    "w1_raw0": 47,
-    "w1_raw1": 30,
-    "tab0": 32,
-    "h_first_woven1": 40,
-    "lg_late_woven": 24,
-    "lg_woven": 44,
-    "w3_sc": 46,
-    "lg_pairs": 49,
+    "logs1": 0,
+    "w2_raw1": 4,
+    "lg_late_woven": 8,
+    "tab0": 12,
+    "w1_dealt0": 12,
+    "w1_dealt1": 14,
+    "lg_woven0": 20,
+    "w2_woven1": 20,
+    "w1_raw0": 21,
+    "lg_woven1": 22,
+    "w3_sc": 23,
+    "w1_raw1": 24,
+    "lg_pairs": 26,
+    "h_first_rows1": 34,
 }
 
 
@@ -187,10 +189,8 @@ def tile_list_gain_drift_rewrite_kernel(
 
         for t in range(PACK - 1):
             log_gains(t, 0, S, "page_logs%d" % t)
-        neg_b = held([P, H_GROUPS, PACK], F32, "neg_b")
         log_gains(PACK - 1, 0, 2 * CHUNK, "logs1")
         logs = log_gains(PACK - 1, 2 * CHUNK, 2 * CHUNK, "logs2")
-        nc.gpsimd.tensor_scalar(neg_b[:], b_sb[:], -1.0, 0.0, ALU.mult, ALU.add)
         exp_warm = held([P, 1], F32, "exp_warm")
         nc.scalar.activation(exp_warm[:], logs[:, 0:1], ACT.Exp, scale=0.0)
         v_words = [gather_words(0, [(0, S)], "v0")]
@@ -205,24 +205,24 @@ def tile_list_gain_drift_rewrite_kernel(
 
         lg_words = lg_pairs[:].rearrange("p u c e -> p u (c e)").bitcast(F32)
 
-        def weave_lg(copy, half, name):
-            woven = held([P, PACK * 2 * CHUNK], BF16, name)
+        def weave_lg(copy, first, count, name):
+            woven = held([P, PACK * count], BF16, name)
             copy(
                 woven[:].bitcast(F32).rearrange("p (c i u) -> p c u i", i=2, u=2),
-                lg_words[:, :, half * 2 * CHUNK : (half + 1) * 2 * CHUNK].rearrange("p u (c i) -> p c u i", i=2),
+                lg_words[:, :, first : first + count].rearrange("p u (c i) -> p c u i", i=2),
             )
             return woven
 
-        w1_sb = [deal_w1(0, "tab0")]
-        early_woven = weave_lg(nc.vector.tensor_copy, 0, "lg_woven")
-        w1_sb.append(deal_w1(1, "logs2"))
-        lg_early = quantize(early_woven, "lg_codes0", "lg_scales0")
-        lg_mx = [lg_early + (0,), lg_early + (CHUNK,)]
+        w1_sb = [deal_w1(a, "w1_dealt%d" % a) for a in range(K_PASSES)]
+        early_woven = [weave_lg(nc.vector.tensor_copy, c * CHUNK, CHUNK, "lg_woven%d" % c) for c in range(2)]
+        lg_mx = [quantize(early_woven[c], "lg_codes%d" % c, "lg_scales%d" % c) + (0,) for c in range(2)]
         w2_mx = [quantize(weave_w2(0, "logs1", [(nc.scalar.copy, 0, P)]), "w1_raw1", "w2_scales0")]
-        late_w2 = weave_w2(1, "lg_woven", [(nc.scalar.copy, 0, W2_SPLIT), (nc.vector.tensor_copy, W2_SPLIT, P)])
+        late_w2 = weave_w2(1, "w2_woven1", [(nc.scalar.copy, 0, W2_SPLIT), (nc.vector.tensor_copy, W2_SPLIT, P)])
         w2_mx.append(quantize(late_w2, "w2_codes1", "w2_scales1"))
         v_words.append(gather_words(1, [(0, CHUNK), (CHUNK, S)], "w2_raw1"))
-        late_woven = weave_lg(nc.scalar.copy, 1, "lg_late_woven")
+        late_woven = weave_lg(nc.scalar.copy, 2 * CHUNK, 2 * CHUNK, "lg_late_woven")
+        neg_b = held([P, H_GROUPS, PACK], F32, "w2_raw0")
+        nc.scalar.activation(neg_b[:], b_sb[:], ACT.Copy, scale=-1.0)
         w3_sc = deal_scales(w3_sc_raw, "w3_sc")
         w3_sb = held([P, H_GROUPS * N], I32, "lg_pairs")
         nc.vector.tensor_copy(
@@ -323,7 +323,7 @@ def tile_list_gain_drift_rewrite_kernel(
             woven = held([P, PACK * CHUNK], BF16, "h_first_woven%d" % g)
             weave(nc.vector.tensor_copy, woven[:], rows[:])
             h_first.append(quantize(woven, "h_first_codes%d" % g, "h_first_scales%d" % g) + (0,))
-        lg_late = quantize(late_woven, "h_first_woven1", "lg_scales1")
+        lg_late = quantize(late_woven, "h_first_rows1", "lg_scales2")
         lg_mx.extend([lg_late + (0,), lg_late + (CHUNK,)])
 
         out_dealt = out_0.rearrange("(p t) c -> t p c", t=PACK)

@@ -224,11 +224,6 @@ def tile_list_gain_drift_rewrite_kernel(
         neg_b = held([P, H_GROUPS, PACK], F32, "w2_raw0")
         nc.scalar.activation(neg_b[:], b_sb[:], ACT.Copy, scale=-1.0)
         w3_sc = deal_scales(w3_sc_raw, "w3_sc")
-        w3_sb = held([P, H_GROUPS * N], I32, "lg_pairs")
-        nc.vector.tensor_copy(
-            w3_sb[:].rearrange("p (a t m) -> p a m t", t=PACK, m=P),
-            w3_raw[:].rearrange("p a (m t) -> p a m t", t=PACK),
-        )
 
         def first_sums(c, g, pair, order):
             bank = psum.tile([P, 2 * CHUNK], F32, name="sums", bufs=SUM_BANKS)
@@ -284,7 +279,7 @@ def tile_list_gain_drift_rewrite_kernel(
         def hidden(c):
             woven = held([P, PACK * H_GROUPS * CHUNK], BF16, "h_first_codes1" if c == 1 else "h_woven%d" % (c % 2))
             if c == 1:
-                parts = [held([P, PACK, CHUNK], BF16, name) for name in ("h_rows1", "lg_late_woven")]
+                parts = [held([P, PACK, CHUNK], BF16, name) for name in ("w3_raw", "lg_late_woven")]
                 for g in range(H_GROUPS):
                     relu_rows(c, g, parts[g][:], (0, LG, 1))
                 for g in range(H_GROUPS):
@@ -323,6 +318,11 @@ def tile_list_gain_drift_rewrite_kernel(
             woven = held([P, PACK * CHUNK], BF16, "h_first_woven%d" % g)
             weave(nc.vector.tensor_copy, woven[:], rows[:])
             h_first.append(quantize(woven, "h_first_codes%d" % g, "h_first_scales%d" % g) + (0,))
+        w3_sb = held([P, H_GROUPS * N], U32, "h_first_rows0")
+        nc.scalar.copy(
+            w3_sb[:].rearrange("p (a t m) -> p a m t", t=PACK, m=P),
+            w3_raw[:].bitcast(U32).rearrange("p a (m t) -> p a m t", t=PACK),
+        )
         lg_late = quantize(late_woven, "h_first_rows1", "lg_scales2")
         lg_mx.extend([lg_late + (0,), lg_late + (CHUNK,)])
 
@@ -348,7 +348,7 @@ def tile_list_gain_drift_rewrite_kernel(
             t, older = waiting[c]
             held_back = drift_bank(t, [older])
             h_mx.append(hidden(c + 1))
-            update(t, [older], held_back, "h_rows%d" % (c + 1))
+            update(t, [older], held_back, "w3_raw" if c == 0 else "h_rows%d" % (c + 1))
 
         def finish(t):
             nc.sync.dma_start(out_dealt[t], pages[t][:])

@@ -23,28 +23,32 @@ K_PASSES = K // GROUP
 H_GROUPS = H // GROUP
 CHUNK = 256
 CHUNKS = S // CHUNK
+HALF = P // 2
 SUM_BANKS = 6
 DRIFT_BANKS = 2
 Y_SPLIT = 1152
 Y_CHUNK = 512
 Y_LAST = 256
 LG = K_PASSES
-W2_SPLIT = 80
+W2_SPLIT = 40
 SHARED = {
+    "w1_raw0": 0,
     "logs1": 0,
-    "w2_raw1": 4,
-    "lg_late_woven": 8,
-    "tab0": 12,
-    "w1_dealt0": 12,
-    "w1_dealt1": 14,
-    "lg_woven0": 20,
-    "w2_woven1": 20,
-    "w1_raw0": 21,
-    "lg_woven1": 22,
-    "w3_sc": 23,
-    "w1_raw1": 24,
-    "lg_pairs": 26,
-    "h_first_rows1": 34,
+    "w1_raw1": 4,
+    "logs2": 4,
+    "tab0": 8,
+    "lg_woven0": 8,
+    "lg_woven1": 12,
+    "h_first_rows1": 16,
+    "v1_last": 16,
+    "h_rows1": 20,
+    "held1": 20,
+    "h_rows2": 24,
+    "held2": 24,
+    "h_rows3": 28,
+    "held3": 28,
+    "h_codes3": 32,
+    "y_rows": 32,
 }
 
 
@@ -62,17 +66,12 @@ def tile_list_gain_drift_rewrite_kernel(
     with ExitStack() as ctx:
         keep = ctx.enter_context(tc.tile_pool(name="keep", bufs=1))
         psum = ctx.enter_context(tc.psum_pool(name="psum", bufs=1))
-
         shared = ctx.enter_context(tc.tile_pool(name="shared", bufs=1))
-        tenants = {}
 
-        def held(shape, dtype, name, bufs=1):
+        def held(shape, dtype, name):
             if name in SHARED:
-                tenants[name] = tenants.get(name, 0) + 1
-                return shared.tile(
-                    shape, dtype, name="%s_%d" % (name, tenants[name]), align_bytes=64, offset=1024 * SHARED[name]
-                )
-            return keep.tile(shape, dtype, name=name, align_bytes=64, bufs=bufs)
+                return shared.tile(shape, dtype, name=name, align_bytes=64, offset=1024 * SHARED[name])
+            return keep.tile(shape, dtype, name=name, align_bytes=64)
 
         tab_sc = held([P, T], U8, "tab_sc")
         w1_sc_raw = held([P, K_PASSES * H], U8, "w1_sc_raw")
@@ -90,10 +89,11 @@ def tile_list_gain_drift_rewrite_kernel(
         gT_dealt = gT.rearrange("(p t) c -> t p c", t=PACK)
         lv_sb = held([P, PACK], F32, "lv_sb")
         b_sb = held([P, H_GROUPS, PACK], F32, "b_sb")
-        w2_raw = [held([P, PACK, GROUP], F32, "w2_raw%d" % g) for g in range(H_GROUPS)]
+        w2_raw = [[held([P, PACK, GROUP // 2], F32, "w2_raw%d_%d" % (g, k)) for k in range(2)] for g in range(H_GROUPS)]
         w2_dealt = w2.rearrange("(p j) c -> p j c", j=PACK)
         w1_raw = [held([P, 2 * H], U8, "w1_raw%d" % a) for a in range(K_PASSES)]
-        tab = []
+        w3_raw = [held([P, N], I32, "w3_raw%d" % a) for a in range(H_GROUPS)]
+        tab = [held([P, T], I32, "tab%d" % a) for a in range(K_PASSES)]
 
         def load_page(t):
             nc.sync.dma_start(pages[t][:], gT_dealt[t])
@@ -103,11 +103,11 @@ def tile_list_gain_drift_rewrite_kernel(
             for r in range(4):
                 nc.sync.dma_start(raw[r:P:32, :].bitcast(I32), by_row[r])
 
-        def load_w2(g):
-            nc.sync.dma_start(w2_raw[g][:], w2_dealt[:, :, g * GROUP : (g + 1) * GROUP])
+        def load_w2(g, k):
+            first = g * GROUP + k * GROUP // 2
+            nc.sync.dma_start(w2_raw[g][k][:], w2_dealt[:, :, first : first + GROUP // 2])
 
-        def load_tab(a, name):
-            tab.append(held([P, T], I32, name))
+        def load_tab(a):
             nc.sync.dma_start(tab[a][:], tab_words[a].rearrange("p c i -> p (c i)").bitcast(I32))
 
         def picks(first, count):
@@ -116,8 +116,8 @@ def tile_list_gain_drift_rewrite_kernel(
         v_sc = held([P, S], U8, "v_sc")
         nc.vector.tensor_copy(v_sc[:], tab_sc[:].indirect(offsets[:]))
 
-        def move_planes(r):
-            for a in range(K_PASSES):
+        def move_planes(a, rows):
+            for r in rows:
                 nc.sync.dma_start(
                     v_planes[r:P:32, a * S : (a + 1) * S].bitcast(I32), v_sc[2 * r + a : 32 : 8, :].bitcast(I32)
                 )
@@ -129,22 +129,23 @@ def tile_list_gain_drift_rewrite_kernel(
         load_scale_rows(w1_sc_raw, w1_scales)
         load_page(1)
         nc.sync.dma_start(lv_sb[:], lv.rearrange("(p t) -> p t", t=PACK))
-        load_page(2)
-        move_planes(0)
-        load_page(3)
-        move_planes(1)
-        move_planes(2)
-        load_tab(0, "tab0")
-        move_planes(3)
         load_w1(0)
-        load_w1(1)
-        load_w2(0)
-        load_w2(1)
-        nc.sync.dma_start(b_sb[:], b.rearrange("(g p t) -> p g t", p=P, t=PACK))
-        load_tab(1, "tab1")
+        load_page(2)
         load_scale_rows(w3_sc_raw, w3_scales)
-        w3_raw = held([P, H_GROUPS, N], I32, "w3_raw")
-        nc.sync.dma_start(w3_raw[:], w3_words.rearrange("a p c i -> p a (c i)").bitcast(I32))
+        load_w1(1)
+        load_page(3)
+        load_tab(0)
+        move_planes(0, range(4))
+        load_w2(0, 0)
+        load_w2(0, 1)
+        load_w2(1, 0)
+        move_planes(1, (0, 1))
+        load_w2(1, 1)
+        move_planes(1, (2, 3))
+        load_tab(1)
+        nc.sync.dma_start(b_sb[:], b.rearrange("(g p t) -> p g t", p=P, t=PACK))
+        for a in range(H_GROUPS):
+            nc.sync.dma_start(w3_raw[a][:], w3_words[a].rearrange("p c i -> p (c i)").bitcast(I32))
 
         def deal_scales(raw, name):
             dealt = held(raw.shape, U8, name)
@@ -154,26 +155,23 @@ def tile_list_gain_drift_rewrite_kernel(
             )
             return dealt
 
-        w1_sc = deal_scales(w1_sc_raw, "w1_sc")
+        def deal_w1(a):
+            dealt = held([P, 2 * H], U8, "w1_dealt%d" % a)
+            nc.scalar.copy(
+                dealt[:].bitcast(U16).rearrange("p (g t m) -> p g m t", t=PACK, m=P),
+                w1_raw[a][:].bitcast(U16).rearrange("p (g m t) -> p g m t", t=PACK, m=P),
+            )
+            return dealt
 
-        def quantize(woven, codes_name, scales_name):
-            codes = held([P, woven.shape[1] // PACK], U32, codes_name)
-            scales = held([P, woven.shape[1] // PACK], U8, scales_name)
+        def quantize(woven, name):
+            codes = held([P, woven.shape[1] // PACK], U32, name.replace("?", "codes"))
+            scales = held([P, woven.shape[1] // PACK], U8, name.replace("?", "scales"))
             nc.vector.quantize_mx(codes[:].bitcast(FP8X4), scales[:], woven[:])
             return codes, scales
 
-        def weave_w2(g, name, shares):
-            woven = held([P, PACK * GROUP], BF16, name)
-            dealt = woven[:].rearrange("p (u e m j) -> p m u j e", u=2, e=2, j=PACK)
-            rows = w2_raw[g][:].rearrange("p j (m u e) -> p m u j e", u=2, e=2)
-            for copy, lo, hi in shares:
-                copy(dealt[:, lo:hi], rows[:, lo:hi])
-            return woven
-
-        def gather_words(a, pieces, name):
-            words = held([P, S], U32, name)
-            for lo, hi in pieces:
-                nc.vector.tensor_copy(words[:, lo:hi], tab[a][:].bitcast(U32).indirect(picks(lo, hi - lo)))
+        def gather_words(a, first, count, name):
+            words = held([P, count], U32, name)
+            nc.vector.tensor_copy(words[:], tab[a][:].bitcast(U32).indirect(picks(first, count)))
             return words
 
         gains = [held([P, S], F32, "gains%d" % t) for t in range(PACK)]
@@ -185,74 +183,90 @@ def tile_list_gain_drift_rewrite_kernel(
             logs = held([P, count], F32, name)
             nc.scalar.activation(logs[:], gains[t][:, span], ACT.Ln)
             nc.gpsimd.tensor_scalar(lg_pairs[:, t // 2, span, t % 2], logs[:], lv_sb[:, t : t + 1], 0.0, ALU.mult, ALU.add)
-            return logs
 
-        for t in range(PACK - 1):
-            log_gains(t, 0, S, "page_logs%d" % t)
-        log_gains(PACK - 1, 0, 2 * CHUNK, "logs1")
-        logs = log_gains(PACK - 1, 2 * CHUNK, 2 * CHUNK, "logs2")
-        exp_warm = held([P, 1], F32, "exp_warm")
-        nc.scalar.activation(exp_warm[:], logs[:, 0:1], ACT.Exp, scale=0.0)
-        v_words = [gather_words(0, [(0, S)], "v0")]
-
-        def deal_w1(a, name):
-            dealt = held([P, 2 * H], U8, name)
-            nc.vector.tensor_copy(
-                dealt[:].bitcast(U16).rearrange("p (g t m) -> p g t m", t=PACK, m=P),
-                w1_raw[a][:].bitcast(U16).rearrange("p (g m t) -> p g t m", t=PACK, m=P),
-            )
-            return dealt
+        w1_sc = deal_scales(w1_sc_raw, "w1_sc")
+        log_gains(0, 0, S, "logs0")
+        w1_sb = [deal_w1(0)]
+        w3_sc = deal_scales(w3_sc_raw, "w3_sc")
+        log_gains(1, 0, S, "logs1")
+        w1_sb.append(deal_w1(1))
+        log_gains(2, 0, S, "logs2")
+        for k in range(2):
+            log_gains(PACK - 1, k * S // 2, S // 2, "logs3_%d" % k)
+        v0_words = gather_words(0, 0, S, "v0")
 
         lg_words = lg_pairs[:].rearrange("p u c e -> p u (c e)").bitcast(F32)
 
-        def weave_lg(copy, first, count, name):
-            woven = held([P, PACK * count], BF16, name)
-            copy(
+        def weave_lg(k):
+            woven = held([P, PACK * S // 2], BF16, "lg_woven%d" % k)
+            nc.vector.tensor_copy(
                 woven[:].bitcast(F32).rearrange("p (c i u) -> p c u i", i=2, u=2),
-                lg_words[:, :, first : first + count].rearrange("p u (c i) -> p c u i", i=2),
+                lg_words[:, :, k * S // 2 : (k + 1) * S // 2].rearrange("p u (c i) -> p c u i", i=2),
             )
             return woven
 
-        w1_sb = [deal_w1(a, "w1_dealt%d" % a) for a in range(K_PASSES)]
-        early_woven = [weave_lg(nc.vector.tensor_copy, c * CHUNK, CHUNK, "lg_woven%d" % c) for c in range(2)]
-        lg_mx = [quantize(early_woven[c], "lg_codes%d" % c, "lg_scales%d" % c) + (0,) for c in range(2)]
-        w2_mx = [quantize(weave_w2(0, "logs1", [(nc.scalar.copy, 0, P)]), "w1_raw1", "w2_scales0")]
-        late_w2 = weave_w2(1, "w2_woven1", [(nc.scalar.copy, 0, W2_SPLIT), (nc.vector.tensor_copy, W2_SPLIT, P)])
-        w2_mx.append(quantize(late_w2, "w2_codes1", "w2_scales1"))
-        v_words.append(gather_words(1, [(0, CHUNK), (CHUNK, S)], "w2_raw1"))
-        late_woven = weave_lg(nc.scalar.copy, 2 * CHUNK, 2 * CHUNK, "lg_late_woven")
-        neg_b = held([P, H_GROUPS, PACK], F32, "w2_raw0")
-        nc.scalar.activation(neg_b[:], b_sb[:], ACT.Copy, scale=-1.0)
-        w3_sc = deal_scales(w3_sc_raw, "w3_sc")
+        lg_woven = [weave_lg(k) for k in range(2)]
+        lg_mx = [quantize(lg_woven[k], "lg_?%d" % k) for k in range(2)]
 
-        def first_sums(c, g, pair, order):
+        def cast_w2(copy, woven, g, k, lo, hi):
+            dealt = woven[:].rearrange("p (u e m j) -> p m u j e", u=2, e=2, j=PACK)
+            rows = w2_raw[g][k][:].rearrange("p j (m u e) -> p m u j e", u=2, e=2)
+            copy(dealt[:, k * HALF + lo : k * HALF + hi], rows[:, lo:hi])
+
+        w2_woven = [held([P, PACK * GROUP], BF16, "w2_woven%d" % g) for g in range(H_GROUPS)]
+        for k in range(2):
+            cast_w2(nc.scalar.copy, w2_woven[0], 0, k, 0, HALF)
+        w2_mx = [quantize(w2_woven[0], "w2_?0")]
+        cast_w2(nc.scalar.copy, w2_woven[1], 1, 0, 0, HALF)
+        cast_w2(nc.scalar.copy, w2_woven[1], 1, 1, 0, W2_SPLIT)
+        cast_w2(nc.vector.tensor_copy, w2_woven[1], 1, 1, W2_SPLIT, HALF)
+        w2_mx.append(quantize(w2_woven[1], "w2_?1"))
+        exp_warm = held([P, 1], F32, "exp_warm")
+        nc.scalar.activation(exp_warm[:], w2_woven[1][:, HALF * PACK : HALF * PACK + 1], ACT.Exp, scale=0.0)
+
+        v1_words = [(gather_words(1, 0, CHUNK, "v1_first"), 0)]
+        v1_middle = gather_words(1, CHUNK, 2 * CHUNK, "v1_middle")
+        v1_words.extend([(v1_middle, 0), (v1_middle, CHUNK)])
+        neg_b = held([P, H_GROUPS, PACK], F32, "neg_b")
+        nc.gpsimd.tensor_scalar(neg_b[:], b_sb[:], -1.0, 0.0, ALU.mult, ALU.add)
+        w3_sb = []
+        for a in range(H_GROUPS):
+            w3_sb.append(held([P, N], U32, "w3_dealt%d" % a))
+            nc.gpsimd.tensor_copy(
+                w3_sb[a][:].rearrange("p (t c i) -> p c t i", t=PACK, i=4),
+                w3_raw[a][:].bitcast(U32).rearrange("p (c i t) -> p c t i", t=PACK, i=4),
+            )
+
+        def first_sums(c, g, pair):
             bank = psum.tile([P, 2 * CHUNK], F32, name="sums", bufs=SUM_BANKS)
             passes = []
-            for a in order:
+            for a in (0, LG, 1):
                 for u in range(2):
                     t = 2 * pair + u
                     acc = bank[:, u * CHUNK : (u + 1) * CHUNK]
                     if a == LG:
-                        codes, scales, at = lg_mx[c]
+                        codes, scales = lg_mx[c // 2]
+                        cols = slice(c % 2 * CHUNK, (c % 2 + 1) * CHUNK)
                         w_cols = slice(t * P, (t + 1) * P)
                         passes.append(
                             (
                                 acc,
                                 w2_mx[g][0][:, w_cols].bitcast(FP8X4),
                                 w2_mx[g][1][:, w_cols],
-                                codes[:, at : at + CHUNK].bitcast(FP8X4),
-                                scales[:, at : at + CHUNK],
+                                codes[:, cols].bitcast(FP8X4),
+                                scales[:, cols],
                             )
                         )
                         continue
                     w_col = g * GROUP + t * P
                     v_col = a * S + c * CHUNK
+                    words, at = (v0_words, c * CHUNK) if a == 0 else v1_words[c]
                     passes.append(
                         (
                             acc,
                             w1_sb[a][:, 2 * w_col : 2 * (w_col + P)].bitcast(FP4X4),
                             w1_sc[:, a * H + w_col : a * H + w_col + P],
-                            v_words[a][:, c * CHUNK : (c + 1) * CHUNK].bitcast(FP8X4),
+                            words[:, at : at + CHUNK].bitcast(FP8X4),
                             v_planes[:, v_col : v_col + CHUNK],
                         )
                     )
@@ -268,40 +282,34 @@ def tile_list_gain_drift_rewrite_kernel(
                 )
             return bank
 
-        def relu_rows(c, g, rows, order):
+        def relu_rows(c, g, rows, on_vector=()):
             for pair in range(2):
-                bank = first_sums(c, g, pair, order)
+                bank = first_sums(c, g, pair)
                 for u in range(2):
                     t = 2 * pair + u
                     acc = bank[:, u * CHUNK : (u + 1) * CHUNK]
-                    nc.scalar.activation(rows[:, t, :], acc, ACT.Relu, bias=neg_b[:, g, t : t + 1])
+                    if pair in on_vector:
+                        nc.vector.tensor_scalar(rows[:, t, :], acc, b_sb[:, g, t : t + 1], 0.0, ALU.subtract, ALU.max)
+                    else:
+                        nc.scalar.activation(rows[:, t, :], acc, ACT.Relu, bias=neg_b[:, g, t : t + 1])
 
         def hidden(c):
-            woven = held([P, PACK * H_GROUPS * CHUNK], BF16, "h_first_codes1" if c == 1 else "h_woven%d" % (c % 2))
-            if c == 1:
-                parts = [held([P, PACK, CHUNK], BF16, name) for name in ("w3_raw", "lg_late_woven")]
-                for g in range(H_GROUPS):
-                    relu_rows(c, g, parts[g][:], (0, LG, 1))
-                for g in range(H_GROUPS):
-                    weave(nc.scalar.copy, woven[:, g * PACK * CHUNK : (g + 1) * PACK * CHUNK], parts[g][:])
-            else:
-                rows = held([P, PACK, H_GROUPS * CHUNK], BF16, "h_rows%d" % c)
-                for g in range(H_GROUPS):
-                    relu_rows(c, g, rows[:, :, g * CHUNK : (g + 1) * CHUNK], (LG, 0, 1))
-                weave(nc.scalar.copy, woven[:], rows[:])
-            codes, scales = quantize(woven, "h_codes%d" % c, "h_scales%d" % c)
-            return [(codes, scales, g * CHUNK) for g in range(H_GROUPS)]
+            woven = held([P, PACK * H_GROUPS * CHUNK], BF16, "h_woven%d" % (c % 2))
+            rows = held([P, PACK, H_GROUPS * CHUNK], BF16, "h_rows%d" % c)
+            for g in range(H_GROUPS):
+                relu_rows(c, g, rows[:, :, g * CHUNK : (g + 1) * CHUNK])
+            weave(nc.scalar.copy, woven[:], rows[:])
+            return quantize(woven, "h_?%d" % c)
 
         def drift(acc, t, h_chunk):
+            codes, scales = h_chunk
             for a in range(H_GROUPS):
-                codes, scales, at = h_chunk[a]
-                c0 = a * N + t * P
                 nc.tensor.matmul_mx(
                     acc,
-                    lhsT=w3_sb[:, c0 : c0 + P].bitcast(FP8X4),
-                    lhsT_scale=w3_sc[:, c0 : c0 + P],
-                    rhs=codes[:, at : at + CHUNK].bitcast(FP8X4),
-                    rhs_scale=scales[:, at : at + CHUNK],
+                    lhsT=w3_sb[a][:, t * P : (t + 1) * P].bitcast(FP8X4),
+                    lhsT_scale=w3_sc[:, a * N + t * P : a * N + (t + 1) * P],
+                    rhs=codes[:, a * CHUNK : (a + 1) * CHUNK].bitcast(FP8X4),
+                    rhs_scale=scales[:, a * CHUNK : (a + 1) * CHUNK],
                     start=(a == 0),
                     stop=(a == H_GROUPS - 1),
                 )
@@ -311,20 +319,13 @@ def tile_list_gain_drift_rewrite_kernel(
                 pages[t][:].indirect(picks(first, count)), gains[t][:, first : first + count], factor, ALU.mult
             )
 
-        h_first = []
+        first_woven = held([P, PACK * H_GROUPS * CHUNK], BF16, "h_woven0")
         for g in range(H_GROUPS):
             rows = held([P, PACK, CHUNK], BF16, "h_first_rows%d" % g)
-            relu_rows(0, g, rows[:], (0, LG, 1))
-            woven = held([P, PACK * CHUNK], BF16, "h_first_woven%d" % g)
-            weave(nc.vector.tensor_copy, woven[:], rows[:])
-            h_first.append(quantize(woven, "h_first_codes%d" % g, "h_first_scales%d" % g) + (0,))
-        w3_sb = held([P, H_GROUPS * N], U32, "h_first_rows0")
-        nc.scalar.copy(
-            w3_sb[:].rearrange("p (a t m) -> p a m t", t=PACK, m=P),
-            w3_raw[:].bitcast(U32).rearrange("p a (m t) -> p a m t", t=PACK),
-        )
-        lg_late = quantize(late_woven, "h_first_rows1", "lg_scales2")
-        lg_mx.extend([lg_late + (0,), lg_late + (CHUNK,)])
+            relu_rows(0, g, rows[:], on_vector=(1,) if g == 0 else ())
+            weave(nc.vector.tensor_copy, first_woven[:, g * PACK * CHUNK : (g + 1) * PACK * CHUNK], rows[:])
+        h_mx = [quantize(first_woven, "h_?0")]
+        v1_words.append((gather_words(1, 3 * CHUNK, CHUNK, "v1_last"), 0))
 
         out_dealt = out_0.rearrange("(p t) c -> t p c", t=PACK)
         last = PACK - 1
@@ -340,7 +341,6 @@ def tile_list_gain_drift_rewrite_kernel(
             nc.scalar.activation(factor[:], bank[:], ACT.Exp)
             rewrite(t, chunks[0] * CHUNK, len(chunks) * CHUNK, factor[:])
 
-        h_mx = [h_first]
         waiting = [(last, 0), (2, 1), (last, 1)]
         for c in range(CHUNKS - 1):
             for t in range(3 if c == 0 else 2):
@@ -348,7 +348,7 @@ def tile_list_gain_drift_rewrite_kernel(
             t, older = waiting[c]
             held_back = drift_bank(t, [older])
             h_mx.append(hidden(c + 1))
-            update(t, [older], held_back, "w3_raw" if c == 0 else "h_rows%d" % (c + 1))
+            update(t, [older], held_back, "held%d" % (c + 1))
 
         def finish(t):
             nc.sync.dma_start(out_dealt[t], pages[t][:])
@@ -357,10 +357,10 @@ def tile_list_gain_drift_rewrite_kernel(
 
         for t, chunks in ((0, [3]), (1, [3]), (2, [2, 3]), (last, [2, 3])):
             update(t, chunks, drift_bank(t, chunks), "factor%d_1" % t)
-        y_rows = held([P, PACK, T], BF16, "h_codes3")
+        y_rows = held([P, PACK, T], BF16, "y_rows")
         for t in range(PACK):
             finish(t)
-        y_woven = held([P, PACK * T], BF16, "tab1")
+        y_woven = held([P, PACK * T], BF16, "y_woven")
         y_scales = held([P, Y_CHUNK], U8, "y_scales")
         words_out = out_1[0].rearrange("p m t -> p (m t)").bitcast(I32)
         y_woven_at = lambda lo, hi: y_woven[:, PACK * lo : PACK * hi]

@@ -41,6 +41,8 @@ SHARED = {
     "lg_woven1": 12,
     "h_first_rows1": 16,
     "v1_last": 16,
+    "lg_codes1": 17,
+    "y_woven": 0,
     "h_rows1": 20,
     "held1": 20,
     "h_rows2": 24,
@@ -139,10 +141,9 @@ def tile_list_gain_drift_rewrite_kernel(
         load_w2(0, 0)
         load_w2(0, 1)
         load_w2(1, 0)
-        move_planes(1, (0, 1))
         load_w2(1, 1)
-        move_planes(1, (2, 3))
         load_tab(1)
+        move_planes(1, range(4))
         nc.sync.dma_start(b_sb[:], b.rearrange("(g p t) -> p g t", p=P, t=PACK))
         for a in range(H_GROUPS):
             nc.sync.dma_start(w3_raw[a][:], w3_words[a].rearrange("p c i -> p (c i)").bitcast(I32))
@@ -206,7 +207,7 @@ def tile_list_gain_drift_rewrite_kernel(
             return woven
 
         lg_woven = [weave_lg(k) for k in range(2)]
-        lg_mx = [quantize(lg_woven[k], "lg_?%d" % k) for k in range(2)]
+        lg_mx = [quantize(lg_woven[0], "lg_?0")]
 
         def cast_w2(copy, woven, g, k, lo, hi):
             dealt = woven[:].rearrange("p (u e m j) -> p m u j e", u=2, e=2, j=PACK)
@@ -299,17 +300,18 @@ def tile_list_gain_drift_rewrite_kernel(
             for g in range(H_GROUPS):
                 relu_rows(c, g, rows[:, :, g * CHUNK : (g + 1) * CHUNK])
             weave(nc.scalar.copy, woven[:], rows[:])
-            return quantize(woven, "h_?%d" % c)
+            codes, scales = quantize(woven, "h_?%d" % c)
+            return [(codes, scales, g * CHUNK) for g in range(H_GROUPS)]
 
         def drift(acc, t, h_chunk):
-            codes, scales = h_chunk
             for a in range(H_GROUPS):
+                codes, scales, at = h_chunk[a]
                 nc.tensor.matmul_mx(
                     acc,
                     lhsT=w3_sb[a][:, t * P : (t + 1) * P].bitcast(FP8X4),
                     lhsT_scale=w3_sc[:, a * N + t * P : a * N + (t + 1) * P],
-                    rhs=codes[:, a * CHUNK : (a + 1) * CHUNK].bitcast(FP8X4),
-                    rhs_scale=scales[:, a * CHUNK : (a + 1) * CHUNK],
+                    rhs=codes[:, at : at + CHUNK].bitcast(FP8X4),
+                    rhs_scale=scales[:, at : at + CHUNK],
                     start=(a == 0),
                     stop=(a == H_GROUPS - 1),
                 )
@@ -319,13 +321,16 @@ def tile_list_gain_drift_rewrite_kernel(
                 pages[t][:].indirect(picks(first, count)), gains[t][:, first : first + count], factor, ALU.mult
             )
 
-        first_woven = held([P, PACK * H_GROUPS * CHUNK], BF16, "h_woven0")
+        h_first = []
         for g in range(H_GROUPS):
             rows = held([P, PACK, CHUNK], BF16, "h_first_rows%d" % g)
             relu_rows(0, g, rows[:], on_vector=(1,) if g == 0 else ())
-            weave(nc.vector.tensor_copy, first_woven[:, g * PACK * CHUNK : (g + 1) * PACK * CHUNK], rows[:])
-        h_mx = [quantize(first_woven, "h_?0")]
+            woven = held([P, PACK * CHUNK], BF16, "h_first_woven%d" % g)
+            weave(nc.vector.tensor_copy, woven[:], rows[:])
+            h_first.append(quantize(woven, "h_first_?%d" % g) + (0,))
+        h_mx = [h_first]
         v1_words.append((gather_words(1, 3 * CHUNK, CHUNK, "v1_last"), 0))
+        lg_mx.append(quantize(lg_woven[1], "lg_?1"))
 
         out_dealt = out_0.rearrange("(p t) c -> t p c", t=PACK)
         last = PACK - 1

@@ -39,9 +39,8 @@ SHARED = {
     "tab0": 8,
     "lg_woven0": 8,
     "lg_woven1": 12,
-    "h_first_rows1": 16,
+    "h_first_woven1": 16,
     "v1_last": 16,
-    "lg_codes1": 17,
     "y_woven": 0,
     "h_rows1": 20,
     "held1": 20,
@@ -167,7 +166,7 @@ def tile_list_gain_drift_rewrite_kernel(
         def quantize(woven, name):
             codes = held([P, woven.shape[1] // PACK], U32, name.replace("?", "codes"))
             scales = held([P, woven.shape[1] // PACK], U8, name.replace("?", "scales"))
-            nc.vector.quantize_mx(codes[:].bitcast(FP8X4), scales[:], woven[:])
+            nc.vector.quantize_mx(codes[:].bitcast(FP8X4), scales[:], woven)
             return codes, scales
 
         def gather_words(a, first, count, name):
@@ -207,7 +206,9 @@ def tile_list_gain_drift_rewrite_kernel(
             return woven
 
         lg_woven = [weave_lg(k) for k in range(2)]
-        lg_mx = [quantize(lg_woven[0], "lg_?0")]
+        lg_early = quantize(lg_woven[0][:], "lg_?0")
+        lg_late = quantize(lg_woven[1][:], "lg_?1")
+        lg_mx = [half + (at,) for half in (lg_early, lg_late) for at in (0, CHUNK)]
 
         def cast_w2(copy, woven, g, k, lo, hi):
             dealt = woven[:].rearrange("p (u e m j) -> p m u j e", u=2, e=2, j=PACK)
@@ -217,17 +218,15 @@ def tile_list_gain_drift_rewrite_kernel(
         w2_woven = [held([P, PACK * GROUP], BF16, "w2_woven%d" % g) for g in range(H_GROUPS)]
         for k in range(2):
             cast_w2(nc.scalar.copy, w2_woven[0], 0, k, 0, HALF)
-        w2_mx = [quantize(w2_woven[0], "w2_?0")]
+        w2_mx = [quantize(w2_woven[0][:], "w2_?0")]
         cast_w2(nc.scalar.copy, w2_woven[1], 1, 0, 0, HALF)
         cast_w2(nc.scalar.copy, w2_woven[1], 1, 1, 0, W2_SPLIT)
         cast_w2(nc.vector.tensor_copy, w2_woven[1], 1, 1, W2_SPLIT, HALF)
-        w2_mx.append(quantize(w2_woven[1], "w2_?1"))
+        w2_mx.append(quantize(w2_woven[1][:], "w2_?1"))
         exp_warm = held([P, 1], F32, "exp_warm")
         nc.scalar.activation(exp_warm[:], w2_woven[1][:, HALF * PACK : HALF * PACK + 1], ACT.Exp, scale=0.0)
 
-        v1_words = [(gather_words(1, 0, CHUNK, "v1_first"), 0)]
-        v1_middle = gather_words(1, CHUNK, 2 * CHUNK, "v1_middle")
-        v1_words.extend([(v1_middle, 0), (v1_middle, CHUNK)])
+        v1_words = [(gather_words(1, c * CHUNK, CHUNK, "v1_%d" % c), 0) for c in range(2)]
         neg_b = held([P, H_GROUPS, PACK], F32, "neg_b")
         nc.gpsimd.tensor_scalar(neg_b[:], b_sb[:], -1.0, 0.0, ALU.mult, ALU.add)
         w3_sb = []
@@ -241,13 +240,13 @@ def tile_list_gain_drift_rewrite_kernel(
         def first_sums(c, g, pair):
             bank = psum.tile([P, 2 * CHUNK], F32, name="sums", bufs=SUM_BANKS)
             passes = []
-            for a in (0, LG, 1):
+            for a in (0, LG, 1) if c < 2 else (1, 0, LG):
                 for u in range(2):
                     t = 2 * pair + u
                     acc = bank[:, u * CHUNK : (u + 1) * CHUNK]
                     if a == LG:
-                        codes, scales = lg_mx[c // 2]
-                        cols = slice(c % 2 * CHUNK, (c % 2 + 1) * CHUNK)
+                        codes, scales, at = lg_mx[c]
+                        cols = slice(at, at + CHUNK)
                         w_cols = slice(t * P, (t + 1) * P)
                         passes.append(
                             (
@@ -300,7 +299,7 @@ def tile_list_gain_drift_rewrite_kernel(
             for g in range(H_GROUPS):
                 relu_rows(c, g, rows[:, :, g * CHUNK : (g + 1) * CHUNK])
             weave(nc.scalar.copy, woven[:], rows[:])
-            codes, scales = quantize(woven, "h_?%d" % c)
+            codes, scales = quantize(woven[:], "h_?%d" % c)
             return [(codes, scales, g * CHUNK) for g in range(H_GROUPS)]
 
         def drift(acc, t, h_chunk):
@@ -327,10 +326,10 @@ def tile_list_gain_drift_rewrite_kernel(
             relu_rows(0, g, rows[:], on_vector=(1,) if g == 0 else ())
             woven = held([P, PACK * CHUNK], BF16, "h_first_woven%d" % g)
             weave(nc.vector.tensor_copy, woven[:], rows[:])
-            h_first.append(quantize(woven, "h_first_?%d" % g) + (0,))
+            h_first.append(quantize(woven[:], "h_first_?%d" % g) + (0,))
         h_mx = [h_first]
-        v1_words.append((gather_words(1, 3 * CHUNK, CHUNK, "v1_last"), 0))
-        lg_mx.append(quantize(lg_woven[1], "lg_?1"))
+        v1_last = gather_words(1, 2 * CHUNK, 2 * CHUNK, "v1_last")
+        v1_words.extend([(v1_last, 0), (v1_last, CHUNK)])
 
         out_dealt = out_0.rearrange("(p t) c -> t p c", t=PACK)
         last = PACK - 1

@@ -30,11 +30,12 @@ Y_SPLIT = 1152
 Y_CHUNK = 512
 Y_LAST = 256
 LG = K_PASSES
-W2_SPLIT = 40
 SHARED = {
-    "w1_raw0": 0,
+    "w1_raw0_0": 16,
     "logs1": 0,
-    "w1_raw1": 4,
+    "w1_raw1_0": 18,
+    "w1_raw1_1": 19,
+    "exp_warm": 18,
     "logs2": 4,
     "tab0": 8,
     "lg_woven0": 8,
@@ -92,7 +93,7 @@ def tile_list_gain_drift_rewrite_kernel(
         b_sb = held([P, H_GROUPS, PACK], F32, "b_sb")
         w2_raw = [[held([P, PACK, GROUP // 2], F32, "w2_raw%d_%d" % (g, k)) for k in range(2)] for g in range(H_GROUPS)]
         w2_dealt = w2.rearrange("(p j) c -> p j c", j=PACK)
-        w1_raw = [held([P, 2 * H], U8, "w1_raw%d" % a) for a in range(K_PASSES)]
+        w1_raw = {}
         w3_raw = [held([P, N], I32, "w3_raw%d" % a) for a in range(H_GROUPS)]
         tab = [held([P, T], I32, "tab%d" % a) for a in range(K_PASSES)]
 
@@ -123,26 +124,29 @@ def tile_list_gain_drift_rewrite_kernel(
                     v_planes[r:P:32, a * S : (a + 1) * S].bitcast(I32), v_sc[2 * r + a : 32 : 8, :].bitcast(I32)
                 )
 
-        def load_w1(a):
-            nc.sync.dma_start(w1_raw[a][:].bitcast(I32), w1_words[a].bitcast(I32))
+        def load_w1(a, g, groups):
+            w1_raw[a, g] = held([P, 2 * GROUP * groups], U8, "w1_raw%d_%d" % (a, g))
+            span = slice(2 * GROUP * g, 2 * GROUP * (g + groups))
+            nc.sync.dma_start(w1_raw[a, g][:].bitcast(I32), w1_words[a][:, span].bitcast(I32))
 
         load_page(0)
         load_scale_rows(w1_sc_raw, w1_scales)
         load_page(1)
         nc.sync.dma_start(lv_sb[:], lv.rearrange("(p t) -> p t", t=PACK))
-        load_w1(0)
         load_page(2)
         load_scale_rows(w3_sc_raw, w3_scales)
-        load_w1(1)
         load_page(3)
         load_tab(0)
+        load_w1(0, 0, H_GROUPS)
         move_planes(0, range(4))
         load_w2(0, 0)
         load_w2(0, 1)
         load_w2(1, 0)
         load_w2(1, 1)
-        load_tab(1)
+        load_w1(1, 0, 1)
         move_planes(1, range(4))
+        load_tab(1)
+        load_w1(1, 1, 1)
         nc.sync.dma_start(b_sb[:], b.rearrange("(g p t) -> p g t", p=P, t=PACK))
         for a in range(H_GROUPS):
             nc.sync.dma_start(w3_raw[a][:], w3_words[a].rearrange("p c i -> p (c i)").bitcast(I32))
@@ -155,13 +159,15 @@ def tile_list_gain_drift_rewrite_kernel(
             )
             return dealt
 
-        def deal_w1(a):
-            dealt = held([P, 2 * H], U8, "w1_dealt%d" % a)
+        w1_sb = [held([P, 2 * H], U8, "w1_dealt%d" % a) for a in range(K_PASSES)]
+
+        def deal_w1(a, g):
+            raw = w1_raw[a, g]
+            dealt = w1_sb[a][:, 2 * GROUP * g : 2 * GROUP * g + raw.shape[1]]
             nc.scalar.copy(
-                dealt[:].bitcast(U16).rearrange("p (g t m) -> p g m t", t=PACK, m=P),
-                w1_raw[a][:].bitcast(U16).rearrange("p (g m t) -> p g m t", t=PACK, m=P),
+                dealt.bitcast(U16).rearrange("p (g t m) -> p g m t", t=PACK, m=P),
+                raw[:].bitcast(U16).rearrange("p (g m t) -> p g m t", t=PACK, m=P),
             )
-            return dealt
 
         def quantize(woven, name):
             codes = held([P, woven.shape[1] // PACK], U32, name.replace("?", "codes"))
@@ -186,14 +192,13 @@ def tile_list_gain_drift_rewrite_kernel(
 
         w1_sc = deal_scales(w1_sc_raw, "w1_sc")
         log_gains(0, 0, S, "logs0")
-        w1_sb = [deal_w1(0)]
         w3_sc = deal_scales(w3_sc_raw, "w3_sc")
         log_gains(1, 0, S, "logs1")
-        w1_sb.append(deal_w1(1))
         log_gains(2, 0, S, "logs2")
         for k in range(2):
             log_gains(PACK - 1, k * S // 2, S // 2, "logs3_%d" % k)
         v0_words = gather_words(0, 0, S, "v0")
+        deal_w1(0, 0)
 
         lg_words = lg_pairs[:].rearrange("p u c e -> p u (c e)").bitcast(F32)
 
@@ -220,11 +225,12 @@ def tile_list_gain_drift_rewrite_kernel(
             cast_w2(nc.scalar.copy, w2_woven[0], 0, k, 0, HALF)
         w2_mx = [quantize(w2_woven[0][:], "w2_?0")]
         cast_w2(nc.scalar.copy, w2_woven[1], 1, 0, 0, HALF)
-        cast_w2(nc.scalar.copy, w2_woven[1], 1, 1, 0, W2_SPLIT)
-        cast_w2(nc.vector.tensor_copy, w2_woven[1], 1, 1, W2_SPLIT, HALF)
+        cast_w2(nc.vector.tensor_copy, w2_woven[1], 1, 1, 0, HALF)
         w2_mx.append(quantize(w2_woven[1][:], "w2_?1"))
+        deal_w1(1, 0)
         exp_warm = held([P, 1], F32, "exp_warm")
-        nc.scalar.activation(exp_warm[:], w2_woven[1][:, HALF * PACK : HALF * PACK + 1], ACT.Exp, scale=0.0)
+        nc.scalar.activation(exp_warm[:], lv_sb[:, 0:1], ACT.Exp, scale=0.0)
+        deal_w1(1, 1)
 
         v1_words = [(gather_words(1, c * CHUNK, CHUNK, "v1_%d" % c), 0) for c in range(2)]
         neg_b = held([P, H_GROUPS, PACK], F32, "neg_b")

@@ -30,13 +30,15 @@ Y_SPLIT = 1152
 Y_CHUNK = 512
 Y_LAST = 256
 LG = K_PASSES
+LV_SPLIT = 384
 SHARED = {
     "w1_raw0_0": 16,
     "logs1": 0,
     "w1_raw1_0": 18,
     "w1_raw1_1": 19,
     "exp_warm": 18,
-    "logs2": 4,
+    "logs2_0": 4,
+    "logs2_1": 6,
     "tab0": 8,
     "lg_woven0": 8,
     "lg_woven1": 12,
@@ -77,7 +79,7 @@ def tile_list_gain_drift_rewrite_kernel(
 
         tab_sc = held([P, T], U8, "tab_sc")
         w1_sc_raw = held([P, K_PASSES * H], U8, "w1_sc_raw")
-        w3_sc_raw = held([P, H_GROUPS * N], U8, "w3_sc_raw")
+        w3_sc_raw = held([P, N], U8, "w3_sc_raw")
         v_planes = held([P, K_PASSES * S], U8, "v_planes")
         for plane in [w1_sc_raw, w3_sc_raw]:
             nc.gpsimd.memset(plane[:].bitcast(I32), 0)
@@ -104,6 +106,10 @@ def tile_list_gain_drift_rewrite_kernel(
             by_row = scales.rearrange("a (q r) c -> r q a c", r=4).bitcast(I32)
             for r in range(4):
                 nc.sync.dma_start(raw[r:P:32, :].bitcast(I32), by_row[r])
+
+        def load_stacked_scale_rows(raw, scales):
+            for q in range(4):
+                nc.sync.dma_start(raw[32 * q : 32 * q + 8, :].bitcast(I32), scales[:, 4 * q : 4 * q + 4, :].bitcast(I32))
 
         def load_w2(g, k):
             first = g * GROUP + k * GROUP // 2
@@ -133,8 +139,8 @@ def tile_list_gain_drift_rewrite_kernel(
         load_scale_rows(w1_sc_raw, w1_scales)
         load_page(1)
         nc.sync.dma_start(lv_sb[:], lv.rearrange("(p t) -> p t", t=PACK))
+        load_stacked_scale_rows(w3_sc_raw, w3_scales)
         load_page(2)
-        load_scale_rows(w3_sc_raw, w3_scales)
         load_page(3)
         load_tab(0)
         load_w1(0, 0, H_GROUPS)
@@ -183,20 +189,25 @@ def tile_list_gain_drift_rewrite_kernel(
         gains = [held([P, S], F32, "gains%d" % t) for t in range(PACK)]
         lg_pairs = held([P, 2, S, 2], BF16, "lg_pairs")
 
-        def log_gains(t, first, count, name):
+        def log_gains(t, first, count, name, on_scalar=0):
             span = slice(first, first + count)
             nc.vector.tensor_copy(gains[t][:, span], pages[t][:].indirect(picks(first, count)))
             logs = held([P, count], F32, name)
             nc.scalar.activation(logs[:], gains[t][:, span], ACT.Ln)
-            nc.gpsimd.tensor_scalar(lg_pairs[:, t // 2, span, t % 2], logs[:], lv_sb[:, t : t + 1], 0.0, ALU.mult, ALU.add)
+            lane = lg_pairs[:, t // 2, span, t % 2]
+            if on_scalar:
+                nc.scalar.activation(lane[:, 0:on_scalar], logs[:, 0:on_scalar], ACT.Copy, scale=lv_sb[:, t : t + 1])
+            nc.gpsimd.tensor_scalar(
+                lane[:, on_scalar:count], logs[:, on_scalar:count], lv_sb[:, t : t + 1], 0.0, ALU.mult, ALU.add
+            )
 
         w1_sc = deal_scales(w1_sc_raw, "w1_sc")
-        log_gains(0, 0, S, "logs0")
+        log_gains(0, 0, S, "logs0", LV_SPLIT)
         w3_sc = deal_scales(w3_sc_raw, "w3_sc")
-        log_gains(1, 0, S, "logs1")
-        log_gains(2, 0, S, "logs2")
-        for k in range(2):
-            log_gains(PACK - 1, k * S // 2, S // 2, "logs3_%d" % k)
+        log_gains(1, 0, S, "logs1", LV_SPLIT)
+        for t in (2, 3):
+            for k in range(2):
+                log_gains(t, k * S // 2, S // 2, "logs%d_%d" % (t, k))
         v0_words = gather_words(0, 0, S, "v0")
         deal_w1(0, 0)
 
@@ -314,7 +325,7 @@ def tile_list_gain_drift_rewrite_kernel(
                 nc.tensor.matmul_mx(
                     acc,
                     lhsT=w3_sb[a][:, t * P : (t + 1) * P].bitcast(FP8X4),
-                    lhsT_scale=w3_sc[:, a * N + t * P : a * N + (t + 1) * P],
+                    lhsT_scale=w3_sc[4 * a : P, t * P : (t + 1) * P],
                     rhs=codes[:, at : at + CHUNK].bitcast(FP8X4),
                     rhs_scale=scales[:, at : at + CHUNK],
                     start=(a == 0),

@@ -171,8 +171,8 @@ def tile_list_gain_drift_rewrite_kernel(
             raw = w1_raw[a, g]
             dealt = w1_sb[a][:, 2 * GROUP * g : 2 * GROUP * g + raw.shape[1]]
             nc.scalar.copy(
-                dealt.bitcast(U16).rearrange("p (g t m) -> p g m t", t=PACK, m=P),
-                raw[:].bitcast(U16).rearrange("p (g m t) -> p g m t", t=PACK, m=P),
+                dealt.bitcast(U16).rearrange("p (g u e m) -> p g u m e", u=2, e=2, m=P),
+                raw[:].bitcast(U16).rearrange("p (g m u e) -> p g u m e", u=2, e=2, m=P),
             )
 
         def quantize(woven, name):
@@ -227,9 +227,9 @@ def tile_list_gain_drift_rewrite_kernel(
         lg_mx = [half + (at,) for half in (lg_early, lg_late) for at in (0, CHUNK)]
 
         def cast_w2(copy, woven, g, k, lo, hi):
-            dealt = woven[:].rearrange("p (u e m j) -> p m u j e", u=2, e=2, j=PACK)
-            rows = w2_raw[g][k][:].rearrange("p j (m u e) -> p m u j e", u=2, e=2)
-            copy(dealt[:, k * HALF + lo : k * HALF + hi], rows[:, lo:hi])
+            dealt = woven[:].rearrange("p (u e m j) -> p u m j e", u=2, e=2, j=PACK)
+            rows = w2_raw[g][k][:].rearrange("p j (m u e) -> p u m j e", u=2, e=2)
+            copy(dealt[:, :, k * HALF + lo : k * HALF + hi], rows[:, :, lo:hi])
 
         w2_woven = [held([P, PACK * GROUP], BF16, "w2_woven%d" % g) for g in range(H_GROUPS)]
         for k in range(2):

@@ -24,7 +24,8 @@ H_GROUPS = H // GROUP
 CHUNK = 256
 CHUNKS = S // CHUNK
 HALF = P // 2
-SUM_BANKS = 6
+BANK = 2048
+SUM_BANKS = ((0, 1, 2, 3), (4, 5, 6, 7), (2, 3, 4, 5), (6, 7, 2, 3))
 DRIFT_BANKS = 2
 Y_SPLIT = 1152
 Y_CHUNK = 512
@@ -58,8 +59,8 @@ SHARED = {
 
 def weave(copy, woven, rows):
     copy(
-        woven.rearrange("p (c i t) -> p c t i", i=4, t=PACK),
-        rows.rearrange("p t (c i) -> p c t i", i=4),
+        woven.rearrange("p (c i t) -> p c t i", i=8, t=PACK),
+        rows.rearrange("p t (c i) -> p c t i", i=8),
     )
 
 
@@ -255,9 +256,10 @@ def tile_list_gain_drift_rewrite_kernel(
             )
 
         def first_sums(c, g, pair):
-            bank = psum.tile([P, 2 * CHUNK], F32, name="sums", bufs=SUM_BANKS)
+            place = SUM_BANKS[c][2 * g + pair]
+            bank = psum.tile([P, 2 * CHUNK], F32, name="sums%d_%d_%d" % (c, g, pair), offset=BANK * place)
             passes = []
-            for a in (0, LG, 1) if c < 2 else (1, 0, LG):
+            for a in (1, 0, LG) if c >= 2 else (0, 1, LG) if (c, g) == (1, 1) else (0, LG, 1):
                 for u in range(2):
                     t = 2 * pair + u
                     acc = bank[:, u * CHUNK : (u + 1) * CHUNK]
@@ -351,8 +353,12 @@ def tile_list_gain_drift_rewrite_kernel(
         out_dealt = out_0.rearrange("(p t) c -> t p c", t=PACK)
         last = PACK - 1
 
+        drifts = []
+
         def drift_bank(t, chunks):
-            bank = psum.tile([P, len(chunks) * CHUNK], F32, name="drift", bufs=DRIFT_BANKS)
+            place = len(drifts) % DRIFT_BANKS
+            bank = psum.tile([P, len(chunks) * CHUNK], F32, name="drift%d" % len(drifts), offset=BANK * place)
+            drifts.append(bank)
             for i in reversed(range(len(chunks))):
                 drift(bank[:, i * CHUNK : (i + 1) * CHUNK], t, h_mx[chunks[i]])
             return bank

from contextlib import ExitStack

import concourse.mybir as mybir

K, T, S, H, N = 1024, 2048, 1024, 1024, 512
FLOPS = 2 * S * (K * H + N * H + H * N)

F32 = mybir.dt.float32
BF16 = mybir.dt.bfloat16
I32 = mybir.dt.int32
U32 = mybir.dt.uint32
U16 = mybir.dt.uint16
U8 = mybir.dt.uint8
FP8X4 = mybir.dt.float8_e4m3fn_x4
FP4X4 = mybir.dt.float4_e2m1fn_x4
ACT = mybir.ActivationFunctionType
ALU = mybir.AluOpType

P = 128
PACK = 4
GROUP = P * PACK
K_PASSES = K // GROUP
H_GROUPS = H // GROUP
CHUNK = 256
CHUNKS = S // CHUNK
HALF = P // 2
BANK = 2048
SUM_BANKS = ((0, 1, 2, 3), (4, 5, 6, 7), (2, 3, 4, 5), (6, 7, 2, 3))
DRIFT_BANKS = 2
Y_SPLIT = 1152
Y_CHUNK = 512
Y_LAST = 256
LG = K_PASSES
LV_SPLIT = 384
SHARED = {
    "w1_raw0_0": 16,
    "logs1": 0,
    "w1_raw1_0": 18,
    "w1_raw1_1": 19,
    "exp_warm": 18,
    "logs2_0": 4,
    "logs2_1": 6,
    "tab0": 8,
    "lg_woven0": 8,
    "lg_woven1": 12,
    "h_first_woven1": 16,
    "v1_last": 16,
    "y_woven": 0,
    "h_rows1": 20,
    "held1": 20,
    "h_rows2": 24,
    "held2": 24,
    "h_rows3": 28,
    "held3": 28,
    "h_codes3": 32,
    "y_rows": 32,
}


def weave(copy, woven, rows):
    copy(
        woven.rearrange("p (c i t) -> p c t i", i=8, t=PACK),
        rows.rearrange("p t (c i) -> p c t i", i=8),
    )


def tile_list_gain_drift_rewrite_kernel(
    tc, tab_words, tab_scales, offs, gT, lv, w1_words, w1_scales, w2, b, w3_words, w3_scales, out_0, out_1, out_2
):
    nc = tc.nc
    with ExitStack() as ctx:
        keep = ctx.enter_context(tc.tile_pool(name="keep", bufs=1))
        psum = ctx.enter_context(tc.psum_pool(name="psum", bufs=1))
        shared = ctx.enter_context(tc.tile_pool(name="shared", bufs=1))

        def held(shape, dtype, name):
            if name in SHARED:
                return shared.tile(shape, dtype, name=name, align_bytes=64, offset=1024 * SHARED[name])
            return keep.tile(shape, dtype, name=name, align_bytes=64)

        tab_sc = held([P, T], U8, "tab_sc")
        w1_sc_raw = held([P, K_PASSES * H], U8, "w1_sc_raw")
        w3_sc_raw = held([P, N], U8, "w3_sc_raw")
        v_planes = held([P, K_PASSES * S], U8, "v_planes")
        for plane in [w1_sc_raw, w3_sc_raw]:
            nc.gpsimd.memset(plane[:].bitcast(I32), 0)
        for plane in [tab_sc[32:64, :], tab_sc[64:P, :], v_planes[:]]:
            nc.vector.memset(plane.bitcast(I32), 0)
        nc.sync.dma_start(tab_sc[0:32, :].bitcast(I32), tab_scales.rearrange("a q c -> q a c").bitcast(I32))

        offsets = keep.tile([P, S // 16], U16, name="offsets")
        nc.sync.dma_start(offsets[:], offs)
        pages = [held([P, T], F32, "page%d" % t) for t in range(PACK)]
        gT_dealt = gT.rearrange("(p t) c -> t p c", t=PACK)
        lv_sb = held([P, PACK], F32, "lv_sb")
        b_sb = held([P, H_GROUPS, PACK], F32, "b_sb")
        w2_raw = [[held([P, PACK, GROUP // 2], F32, "w2_raw%d_%d" % (g, k)) for k in range(2)] for g in range(H_GROUPS)]
        w2_dealt = w2.rearrange("(p j) c -> p j c", j=PACK)
        w1_raw = {}
        w3_raw = [held([P, N], I32, "w3_raw%d" % a) for a in range(H_GROUPS)]
        tab = [held([P, T], I32, "tab%d" % a) for a in range(K_PASSES)]

        def load_page(t):
            nc.sync.dma_start(pages[t][:], gT_dealt[t])

        def load_scale_rows(raw, scales):
            by_row = scales.rearrange("a (q r) c -> r q a c", r=4).bitcast(I32)
            for r in range(4):
                nc.sync.dma_start(raw[r:P:32, :].bitcast(I32), by_row[r])

        def load_stacked_scale_rows(raw, scales):
            for q in range(4):
                nc.sync.dma_start(raw[32 * q : 32 * q + 8, :].bitcast(I32), scales[:, 4 * q : 4 * q + 4, :].bitcast(I32))

        def load_w2(g, k):
            first = g * GROUP + k * GROUP // 2
            nc.sync.dma_start(w2_raw[g][k][:], w2_dealt[:, :, first : first + GROUP // 2])

        def load_tab(a):
            nc.sync.dma_start(tab[a][:], tab_words[a].rearrange("p c i -> p (c i)").bitcast(I32))

        def picks(first, count):
            return offsets[:, first // 16 : (first + count) // 16]

        v_sc = held([P, S], U8, "v_sc")
        nc.vector.tensor_copy(v_sc[:], tab_sc[:].indirect(offsets[:]))

        def move_planes(a, rows):
            for r in rows:
                nc.sync.dma_start(
                    v_planes[r:P:32, a * S : (a + 1) * S].bitcast(I32), v_sc[2 * r + a : 32 : 8, :].bitcast(I32)
                )

        def load_w1(a, g, groups):
            w1_raw[a, g] = held([P, 2 * GROUP * groups], U8, "w1_raw%d_%d" % (a, g))
            span = slice(2 * GROUP * g, 2 * GROUP * (g + groups))
            nc.sync.dma_start(w1_raw[a, g][:].bitcast(I32), w1_words[a][:, span].bitcast(I32))

        load_page(0)
        load_scale_rows(w1_sc_raw, w1_scales)
        load_page(1)
        nc.sync.dma_start(lv_sb[:], lv.rearrange("(p t) -> p t", t=PACK))
        load_stacked_scale_rows(w3_sc_raw, w3_scales)
        load_page(2)
        load_page(3)
        load_tab(0)
        load_w1(0, 0, H_GROUPS)
        move_planes(0, range(4))
        load_w2(0, 0)
        load_w2(0, 1)
        load_w2(1, 0)
        load_w2(1, 1)
        load_w1(1, 0, 1)
        move_planes(1, range(4))
        load_tab(1)
        load_w1(1, 1, 1)
        nc.sync.dma_start(b_sb[:], b.rearrange("(g p t) -> p g t", p=P, t=PACK))
        for a in range(H_GROUPS):
            nc.sync.dma_start(w3_raw[a][:], w3_words[a].rearrange("p c i -> p (c i)").bitcast(I32))

        def deal_scales(raw, name):
            dealt = held(raw.shape, U8, name)
            nc.gpsimd.tensor_copy(
                dealt[:].rearrange("p (g t m) -> p g t m", t=PACK, m=P),
                raw[:].rearrange("p (g m t) -> p g t m", t=PACK, m=P),
            )
            return dealt

        w1_sb = [held([P, 2 * H], U8, "w1_dealt%d" % a) for a in range(K_PASSES)]

        def deal_w1(a, g):
            raw = w1_raw[a, g]
            dealt = w1_sb[a][:, 2 * GROUP * g : 2 * GROUP * g + raw.shape[1]]
            nc.scalar.copy(
                dealt.bitcast(U16).rearrange("p (g u e m) -> p g u m e", u=2, e=2, m=P),
                raw[:].bitcast(U16).rearrange("p (g m u e) -> p g u m e", u=2, e=2, m=P),
            )

        def quantize(woven, name):
            codes = held([P, woven.shape[1] // PACK], U32, name.replace("?", "codes"))
            scales = held([P, woven.shape[1] // PACK], U8, name.replace("?", "scales"))
            nc.vector.quantize_mx(codes[:].bitcast(FP8X4), scales[:], woven)
            return codes, scales

        def gather_words(a, first, count, name):
            words = held([P, count], U32, name)
            nc.vector.tensor_copy(words[:], tab[a][:].bitcast(U32).indirect(picks(first, count)))
            return words

        gains = [held([P, S], F32, "gains%d" % t) for t in range(PACK)]
        lg_pairs = held([P, 2, S, 2], BF16, "lg_pairs")

        def log_gains(t, first, count, name, on_scalar=0):
            span = slice(first, first + count)
            nc.vector.tensor_copy(gains[t][:, span], pages[t][:].indirect(picks(first, count)))
            logs = held([P, count], F32, name)
            nc.scalar.activation(logs[:], gains[t][:, span], ACT.Ln)
            lane = lg_pairs[:, t // 2, span, t % 2]
            if on_scalar:
                nc.scalar.activation(lane[:, 0:on_scalar], logs[:, 0:on_scalar], ACT.Copy, scale=lv_sb[:, t : t + 1])
            nc.gpsimd.tensor_scalar(
                lane[:, on_scalar:count], logs[:, on_scalar:count], lv_sb[:, t : t + 1], 0.0, ALU.mult, ALU.add
            )

        w1_sc = deal_scales(w1_sc_raw, "w1_sc")
        log_gains(0, 0, S, "logs0", LV_SPLIT)
        w3_sc = deal_scales(w3_sc_raw, "w3_sc")
        log_gains(1, 0, S, "logs1", LV_SPLIT)
        for t in (2, 3):
            for k in range(2):
                log_gains(t, k * S // 2, S // 2, "logs%d_%d" % (t, k))
        v0_words = gather_words(0, 0, S, "v0")
        deal_w1(0, 0)

        lg_words = lg_pairs[:].rearrange("p u c e -> p u (c e)").bitcast(F32)

        def weave_lg(k):
            woven = held([P, PACK * S // 2], BF16, "lg_woven%d" % k)
            nc.vector.tensor_copy(
                woven[:].bitcast(F32).rearrange("p (c i u) -> p c u i", i=2, u=2),
                lg_words[:, :, k * S // 2 : (k + 1) * S // 2].rearrange("p u (c i) -> p c u i", i=2),
            )
            return woven

        lg_woven = [weave_lg(k) for k in range(2)]
        lg_early = quantize(lg_woven[0][:], "lg_?0")
        lg_late = quantize(lg_woven[1][:], "lg_?1")
        lg_mx = [half + (at,) for half in (lg_early, lg_late) for at in (0, CHUNK)]

        def cast_w2(copy, woven, g, k, lo, hi):
            dealt = woven[:].rearrange("p (u e m j) -> p u m j e", u=2, e=2, j=PACK)
            rows = w2_raw[g][k][:].rearrange("p j (m u e) -> p u m j e", u=2, e=2)
            copy(dealt[:, :, k * HALF + lo : k * HALF + hi], rows[:, :, lo:hi])

        w2_woven = [held([P, PACK * GROUP], BF16, "w2_woven%d" % g) for g in range(H_GROUPS)]
        for k in range(2):
            cast_w2(nc.scalar.copy, w2_woven[0], 0, k, 0, HALF)
        w2_mx = [quantize(w2_woven[0][:], "w2_?0")]
        cast_w2(nc.scalar.copy, w2_woven[1], 1, 0, 0, HALF)
        cast_w2(nc.vector.tensor_copy, w2_woven[1], 1, 1, 0, HALF)
        w2_mx.append(quantize(w2_woven[1][:], "w2_?1"))
        deal_w1(1, 0)
        exp_warm = held([P, 1], F32, "exp_warm")
        nc.scalar.activation(exp_warm[:], lv_sb[:, 0:1], ACT.Exp, scale=0.0)
        deal_w1(1, 1)

        v1_words = [(gather_words(1, c * CHUNK, CHUNK, "v1_%d" % c), 0) for c in range(2)]
        neg_b = held([P, H_GROUPS, PACK], F32, "neg_b")
        nc.gpsimd.tensor_scalar(neg_b[:], b_sb[:], -1.0, 0.0, ALU.mult, ALU.add)
        w3_sb = []
        for a in range(H_GROUPS):
            w3_sb.append(held([P, N], U32, "w3_dealt%d" % a))
            nc.gpsimd.tensor_copy(
                w3_sb[a][:].rearrange("p (t c i) -> p c t i", t=PACK, i=4),
                w3_raw[a][:].bitcast(U32).rearrange("p (c i t) -> p c t i", t=PACK, i=4),
            )

        def first_sums(c, g, pair):
            place = SUM_BANKS[c][2 * g + pair]
            bank = psum.tile([P, 2 * CHUNK], F32, name="sums%d_%d_%d" % (c, g, pair), offset=BANK * place)
            passes = []
            for a in (1, 0, LG) if c >= 2 else (0, 1, LG) if (c, g) == (1, 1) else (0, LG, 1):
                for u in range(2):
                    t = 2 * pair + u
                    acc = bank[:, u * CHUNK : (u + 1) * CHUNK]
                    if a == LG:
                        codes, scales, at = lg_mx[c]
                        cols = slice(at, at + CHUNK)
                        w_cols = slice(t * P, (t + 1) * P)
                        passes.append(
                            (
                                acc,
                                w2_mx[g][0][:, w_cols].bitcast(FP8X4),
                                w2_mx[g][1][:, w_cols],
                                codes[:, cols].bitcast(FP8X4),
                                scales[:, cols],
                            )
                        )
                        continue
                    w_col = g * GROUP + t * P
                    v_col = a * S + c * CHUNK
                    words, at = (v0_words, c * CHUNK) if a == 0 else v1_words[c]
                    passes.append(
                        (
                            acc,
                            w1_sb[a][:, 2 * w_col : 2 * (w_col + P)].bitcast(FP4X4),
                            w1_sc[:, a * H + w_col : a * H + w_col + P],
                            words[:, at : at + CHUNK].bitcast(FP8X4),
                            v_planes[:, v_col : v_col + CHUNK],
                        )
                    )
            for i, (acc, lhsT, lhsT_scale, rhs, rhs_scale) in enumerate(passes):
                nc.tensor.matmul_mx(
                    acc,
                    lhsT=lhsT,
                    lhsT_scale=lhsT_scale,
                    rhs=rhs,
                    rhs_scale=rhs_scale,
                    start=(i == 0),
                    stop=(i == len(passes) - 1),
                )
            return bank

        def relu_rows(c, g, rows, on_vector=()):
            for pair in range(2):
                bank = first_sums(c, g, pair)
                for u in range(2):
                    t = 2 * pair + u
                    acc = bank[:, u * CHUNK : (u + 1) * CHUNK]
                    if pair in on_vector:
                        nc.vector.tensor_scalar(rows[:, t, :], acc, b_sb[:, g, t : t + 1], 0.0, ALU.subtract, ALU.max)
                    else:
                        nc.scalar.activation(rows[:, t, :], acc, ACT.Relu, bias=neg_b[:, g, t : t + 1])

        def hidden(c):
            woven = held([P, PACK * H_GROUPS * CHUNK], BF16, "h_woven%d" % (c % 2))
            rows = held([P, PACK, H_GROUPS * CHUNK], BF16, "h_rows%d" % c)
            for g in range(H_GROUPS):
                relu_rows(c, g, rows[:, :, g * CHUNK : (g + 1) * CHUNK])
            weave(nc.scalar.copy, woven[:], rows[:])
            codes, scales = quantize(woven[:], "h_?%d" % c)
            return [(codes, scales, g * CHUNK) for g in range(H_GROUPS)]

        def drift(acc, t, h_chunk):
            for a in range(H_GROUPS):
                codes, scales, at = h_chunk[a]
                nc.tensor.matmul_mx(
                    acc,
                    lhsT=w3_sb[a][:, t * P : (t + 1) * P].bitcast(FP8X4),
                    lhsT_scale=w3_sc[4 * a : P, t * P : (t + 1) * P],
                    rhs=codes[:, at : at + CHUNK].bitcast(FP8X4),
                    rhs_scale=scales[:, at : at + CHUNK],
                    start=(a == 0),
                    stop=(a == H_GROUPS - 1),
                )

        def rewrite(t, first, count, factor):
            nc.vector.tensor_tensor(
                pages[t][:].indirect(picks(first, count)), gains[t][:, first : first + count], factor, ALU.mult
            )

        h_first = []
        for g in range(H_GROUPS):
            rows = held([P, PACK, CHUNK], BF16, "h_first_rows%d" % g)
            relu_rows(0, g, rows[:], on_vector=(1,) if g == 0 else ())
            woven = held([P, PACK * CHUNK], BF16, "h_first_woven%d" % g)
            weave(nc.vector.tensor_copy, woven[:], rows[:])
            h_first.append(quantize(woven[:], "h_first_?%d" % g) + (0,))
        h_mx = [h_first]
        v1_last = gather_words(1, 2 * CHUNK, 2 * CHUNK, "v1_last")
        v1_words.extend([(v1_last, 0), (v1_last, CHUNK)])

        out_dealt = out_0.rearrange("(p t) c -> t p c", t=PACK)
        last = PACK - 1

        drifts = []

        def drift_bank(t, chunks):
            place = len(drifts) % DRIFT_BANKS
            bank = psum.tile([P, len(chunks) * CHUNK], F32, name="drift%d" % len(drifts), offset=BANK * place)
            drifts.append(bank)
            for i in reversed(range(len(chunks))):
                drift(bank[:, i * CHUNK : (i + 1) * CHUNK], t, h_mx[chunks[i]])
            return bank

        def update(t, chunks, bank, name):
            factor = held([P, len(chunks) * CHUNK], F32, name)
            nc.scalar.activation(factor[:], bank[:], ACT.Exp)
            rewrite(t, chunks[0] * CHUNK, len(chunks) * CHUNK, factor[:])

        waiting = [(last, 0), (2, 1), (last, 1)]
        for c in range(CHUNKS - 1):
            for t in range(3 if c == 0 else 2):
                update(t, [c], drift_bank(t, [c]), "factor%d_%d" % (t, c % 2))
            t, older = waiting[c]
            held_back = drift_bank(t, [older])
            h_mx.append(hidden(c + 1))
            update(t, [older], held_back, "held%d" % (c + 1))

        def finish(t):
            nc.sync.dma_start(out_dealt[t], pages[t][:])
            if t < last:
                nc.scalar.copy(y_rows[:, t, :], pages[t][:])

        for t, chunks in ((0, [3]), (1, [3]), (2, [2, 3]), (last, [2, 3])):
            update(t, chunks, drift_bank(t, chunks), "factor%d_1" % t)
        y_rows = held([P, PACK, T], BF16, "y_rows")
        for t in range(PACK):
            finish(t)
        y_woven = held([P, PACK * T], BF16, "y_woven")
        y_scales = held([P, Y_CHUNK], U8, "y_scales")
        words_out = out_1[0].rearrange("p m t -> p (m t)").bitcast(I32)
        y_woven_at = lambda lo, hi: y_woven[:, PACK * lo : PACK * hi]

        def weave_y(copy, lo, hi):
            weave(copy, y_woven_at(lo, hi), y_rows[:, :, lo:hi])

        def store_planes(lo, hi):
            y_codes = held([P, hi - lo], I32, "y_codes%d" % lo)
            plane, col = divmod(lo, Y_CHUNK)
            scales = y_scales[4 * plane : P, col : col + hi - lo]
            nc.vector.quantize_mx(y_codes[:].bitcast(FP8X4), scales, y_woven_at(lo, hi))
            nc.sync.dma_start(words_out[:, lo:hi], y_codes[:])

        for lo, hi in ((0, Y_CHUNK), (Y_CHUNK, Y_SPLIT)):
            nc.vector.tensor_copy(y_rows[:, last, lo:hi], pages[last][:, lo:hi])
        nc.scalar.copy(y_rows[:, last, Y_SPLIT:T], pages[last][:, Y_SPLIT:T])
        for lo, hi in ((Y_SPLIT, T - Y_CHUNK), (T - Y_CHUNK, T - Y_LAST), (T - Y_LAST, T)):
            weave_y(nc.scalar.copy, lo, hi)
        middle = 2 * Y_CHUNK
        weave_y(nc.vector.tensor_copy, 0, Y_CHUNK)
        weave_y(nc.vector.tensor_copy, Y_CHUNK, middle)
        store_planes(0, Y_CHUNK)
        weave_y(nc.vector.tensor_copy, middle, Y_SPLIT)
        for lo, hi in ((Y_CHUNK, middle), (middle, T - Y_CHUNK), (T - Y_CHUNK, T - Y_LAST), (T - Y_LAST, T)):
            store_planes(lo, hi)
        for q in range(4):
            queue = nc.sync if q % 2 == 0 else nc.scalar
            queue.dma_start(
                out_2[0, 4 * q : 4 * q + 4, :].rearrange("r (i c) -> i r c", c=Y_CHUNK).bitcast(I32),
                y_scales[32 * q : 32 * q + 16, :].bitcast(I32),
            )
